import numpy as np
import ml_dtypes


def mxq(x, axis, fmt="e4m3"):
    dtype, down = {"e4m3": (ml_dtypes.float8_e4m3fn, 7), "e5m2": (ml_dtypes.float8_e5m2, 14)}[fmt]
    v = np.moveaxis(np.asarray(x, np.float32).astype(ml_dtypes.bfloat16).astype(np.float64), axis, -1)
    blocks = v.reshape(v.shape[:-1] + (-1, 32))
    amax = np.abs(blocks).max(-1, keepdims=True)
    byte = np.maximum(np.where(amax > 0, np.frexp(amax)[1] - 1 + 127, 0) - down, 1)
    scale = np.exp2(byte - 127.0)
    codes = (blocks / scale).astype(np.float32).astype(dtype).astype(np.float64)
    return np.moveaxis((codes * scale).reshape(v.shape), -1, axis)


WIDE = False


def mx_kscale(k):
    if not WIDE:
        return np.ones(k)
    levels = np.array([30, -30])
    if k % 512:
        return np.exp2(np.random.permutation(np.resize(levels, k // 32))).repeat(32)
    a = np.empty((k // 512, 16))
    for p in range(k // 512):
        a[p, :8] = np.random.permutation(np.resize(levels, 8))
        for g in range(8):
            far = levels[np.abs(levels - a[p, g]) >= 10]
            a[p, g + 8] = far[np.random.randint(len(far))]
    return np.exp2(a.ravel()).repeat(32)


def f64(x):
    return np.asarray(x).astype(np.float64)


E2M1 = np.array([0.0, 0.5, 1.0, 1.5, 2.0, 3.0, 4.0, 6.0, -0.0, -0.5, -1.0, -1.5, -2.0, -3.0, -4.0, -6.0])


def pack_weight(w, fmt):
    k, n = w.shape
    w = f64(np.asarray(w, np.float32).astype(ml_dtypes.bfloat16)).reshape(k // 32, 32, n)
    amax = np.abs(w).max(1)
    if fmt == "e4m3":
        byte = np.frexp(amax)[1] - 1 + 127 - 7
    else:
        mant, ex = np.frexp(amax / 6.0)
        byte = np.where(mant > 0.5, ex, ex - 1) + 127
    byte = np.clip(np.where(amax > 0, byte, 1), 1, 254)
    scaled = (w * np.exp2(127.0 - byte)[:, None, :]).reshape(k, n).astype(np.float32)
    by_word = np.ascontiguousarray(scaled.reshape(k // 512, 128, 4, n).transpose(0, 1, 3, 2))
    if fmt == "e4m3":
        words = by_word.astype(ml_dtypes.float8_e4m3fn).view(np.uint8)
    else:
        c = by_word.astype(ml_dtypes.float4_e2m1fn).view(np.uint8) & 0xF
        words = (c[..., 0::2] | (c[..., 1::2] << 4)).reshape(k // 512, 128, 2 * n)
    return np.ascontiguousarray(words), np.ascontiguousarray(byte.astype(np.uint8).reshape(k // 512, 16, n))


def unpack_weight(words, scales, fmt):
    g, _, n = scales.shape
    words = np.ascontiguousarray(words).reshape(g, 128, n, -1)
    if fmt == "e4m3":
        vals = words.view(ml_dtypes.float8_e4m3fn).astype(np.float64)
    else:
        nib = np.empty((g, 128, n, 4), np.uint8)
        nib[..., 0::2] = words & 0xF
        nib[..., 1::2] = words >> 4
        vals = E2M1[nib]
    vals = vals * np.repeat(np.exp2(scales.astype(np.float64) - 127.0), 8, axis=1)[..., None]
    return vals.transpose(0, 1, 3, 2).reshape(g * 512, n)


def gelu(f):
    return 0.5 * f * (1.0 + np.tanh(np.sqrt(2.0 / np.pi) * (f + 0.044715 * f**3)))


K, N, T = 1024, 512, 1024


def setup_inputs():
    n = np.random.standard_normal
    s = mx_kscale(K)[:, None]
    w = n((K, N)) / np.sqrt(K) / s
    p_w8 = pack_weight(w[:512], "e4m3")
    p_w4 = pack_weight(w[512:], "e2m1")
    return {
        "x": (n((K, T)) * s).astype(np.float32),
        "w8_words": p_w8[0],
        "w8_scales": p_w8[1],
        "w4_words": p_w4[0],
        "w4_scales": p_w4[1],
        "b": (0.3 * n(N)).astype(np.float32),
    }


def reference(x, w8_words, w8_scales, w4_words, w4_scales, b):
    x_q_ = mxq(f64(x), 0, "e4m3")
    x_r_ = mxq(f64(x) - x_q_, 0, "e5m2")
    w8_ = unpack_weight(w8_words, w8_scales, "e4m3")
    w4_ = unpack_weight(w4_words, w4_scales, "e2m1")
    y = w8_.T @ x_q_[:512] + w4_.T @ x_q_[512:] + w8_.T @ x_r_[:512] + w4_.T @ x_r_[512:]
    return gelu(y + f64(b)[:, None])

@@ -1,0 +1,233 @@
+from contextlib import ExitStack
+
+import concourse.mybir as mybir
+from concourse.masks import make_identity
+
+K, N, T = 1024, 512, 1024
+FLOPS = 2 * 2 * K * N * T
+
+F32 = mybir.dt.float32
+BF16 = mybir.dt.bfloat16
+I32 = mybir.dt.int32
+U32 = mybir.dt.uint32
+U8 = mybir.dt.uint8
+E4M3 = mybir.dt.float8_e4m3fn_x4
+E5M2 = mybir.dt.float8_e5m2_x4
+E2M1 = mybir.dt.float4_e2m1fn_x4
+GELU = mybir.ActivationFunctionType.Gelu_apprx_tanh
+
+P = 128
+PACK = 4
+K_PASS = P * PACK
+BANK = 512
+CHUNK = 128
+PER_UNIT = BANK // CHUNK
+N_CHUNKS = (K // K_PASS) * (T // CHUNK)
+N_TILES = N // P
+LINE = 4
+
+
+def tile_mix_tierx_mix_gelu_kernel(tc, x, w8_words, w8_scales, w4_words, w4_scales, b, out):
+    nc = tc.nc
+    with ExitStack() as ctx:
+        keep = ctx.enter_context(tc.tile_pool(name="keep", bufs=1))
+        psum = ctx.enter_context(tc.psum_pool(name="psum", bufs=1))
+        ctx.enter_context(tc.manual_schedule())
+
+        def sb(name, shape, dtype):
+            return keep.tile(shape, dtype, name=name, align_bytes=64)
+
+        w_planes = [sb("w8_plane", [P, N], U8), sb("w4_plane", [P, N], U8)]
+        eye_in = sb("eye_in", [P, PACK * (K_PASS + 1)], BF16)
+        eye = sb("eye", [P, P], BF16)
+        eye_codes = sb("eye_codes", [P, K_PASS], U32)
+        eye_plane = sb("eye_plane", [P, K_PASS], U8)
+        make_identity(nc, eye[:])
+        for plane in w_planes:
+            nc.gpsimd.memset(plane[:].bitcast(I32), 0)
+        nc.vector.memset(eye_in[:].bitcast(I32), 0)
+        nc.vector.tensor_copy(
+            out=eye_in[:].rearrange("p (j s) -> p j s", j=PACK)[:, :, 0 : K_PASS : PACK],
+            in_=eye[:].unsqueeze(1).to_broadcast([P, PACK, P]),
+        )
+        nc.vector.quantize_mx(out=eye_codes[:].bitcast(E4M3), scales=eye_plane[:], in_=eye_in[:, 0 : PACK * K_PASS])
+
+        raw = {}
+
+        def load_x(chunks):
+            unit, c = divmod(chunks[0], PER_UNIT)
+            half, g = divmod(unit, 2)
+            width = CHUNK * len(chunks)
+            t0 = half * BANK + c * CHUNK
+            slab = sb("x%d" % chunks[0], [P, PACK, width], F32)
+            nc.sync.dma_start(
+                out=slab[:],
+                in_=x[g * K_PASS : (g + 1) * K_PASS, t0 : t0 + width].rearrange("(p j) w -> p j w", j=PACK),
+            )
+            for pos, i in enumerate(chunks):
+                raw[i] = (slab, pos * CHUNK)
+
+        def load_plane(plane, scales):
+            for r in range(4):
+                nc.sync.dma_start(out=plane[r:P:32, :].bitcast(I32), in_=scales[0, r:16:4, :].bitcast(I32))
+
+        w8 = sb("w8", [P, 4 * N], U8)
+        w4 = sb("w4", [P, 2 * N], U8)
+        bias = sb("bias", [P, N_TILES], F32)
+        load_x([0])
+        load_x([1])
+        load_x([2, 3])
+        load_x([4, 5])
+        nc.sync.dma_start(out=w8[:].bitcast(I32), in_=w8_words[0].rearrange("p n i -> p (n i)").bitcast(I32))
+        load_plane(w_planes[0], w8_scales)
+        load_x([6, 7])
+        nc.sync.dma_start(out=w4[:].bitcast(I32), in_=w4_words[0].bitcast(I32))
+        load_plane(w_planes[1], w4_scales)
+        load_x([8, 9])
+        load_x([10, 11])
+        with nc.allow_non_contiguous_dma(reason="one bias value to a partition"):
+            nc.sync.dma_start(out=bias[:], in_=b.rearrange("(c p) -> p c", p=P))
+        load_x([12, 13])
+        load_x([14, 15])
+
+        n_units = N_CHUNKS // PER_UNIT
+        q_codes = [sb("q_codes%d" % u, [P, BANK], U32) for u in range(n_units)]
+        q_plane = [sb("q_plane%d" % u, [P, BANK], U8) for u in range(n_units)]
+        r_codes = [sb("r_codes%d" % u, [P, BANK], U32) for u in range(n_units)]
+        r_plane = [sb("r_plane%d" % u, [P, BANK], U8) for u in range(n_units)]
+
+        def rows_walk(ap):
+            return ap.rearrange("p j (c i) -> p c j i", i=LINE)
+
+        def words_walk(ap):
+            return ap.rearrange("p (c i j) -> p c j i", i=LINE, j=PACK)
+
+        def x_rows(chunks):
+            slab, pos = raw[chunks[0]]
+            return slab[:, :, pos : pos + CHUNK * len(chunks)]
+
+        def unit_cols(chunks):
+            unit, c = divmod(chunks[0], PER_UNIT)
+            return unit, slice(c * CHUNK, (c + len(chunks)) * CHUNK)
+
+        x_bf = {}
+        r_bf = {}
+        values = {}
+        acc = {}
+
+        def cast(chunks, copy):
+            staged = sb("x_bf%d" % chunks[0], [P, PACK * CHUNK * len(chunks)], BF16)
+            copy(out=words_walk(staged[:]), in_=rows_walk(x_rows(chunks)))
+            x_bf[chunks[0]] = staged
+
+        def quantise_x(chunks):
+            unit, cols = unit_cols(chunks)
+            nc.vector.quantize_mx(
+                out=q_codes[unit][:, cols].bitcast(E4M3), scales=q_plane[unit][:, cols], in_=x_bf[chunks[0]][:]
+            )
+
+        def dequantise(i):
+            unit, cols = unit_cols([i])
+            bank = psum.tile([P, PACK, CHUNK], F32, tag="values", bufs=2, name="values")
+            for j in range(PACK):
+                nc.tensor.matmul_mx(
+                    out=bank[:, j, :],
+                    lhsT=eye_codes[:, j * P : (j + 1) * P].bitcast(E4M3),
+                    lhsT_scale=eye_plane[:, j * P : (j + 1) * P],
+                    rhs=q_codes[unit][:, cols].bitcast(E4M3),
+                    rhs_scale=q_plane[unit][:, cols],
+                    start=True,
+                    stop=True,
+                )
+            values[i] = bank
+
+        def subtract(i):
+            if i % 2 == 0:
+                r_bf[i // 2] = sb("r_bf%d" % i, [P, 2 * PACK * CHUNK], BF16)
+            lo = (i % 2) * PACK * CHUNK
+            nc.vector.tensor_tensor(
+                out=words_walk(r_bf[i // 2][:, lo : lo + PACK * CHUNK]),
+                in0=rows_walk(x_rows([i])),
+                in1=rows_walk(values[i][:]),
+                op=mybir.AluOpType.subtract,
+            )
+
+        def quantise_rest(chunks):
+            unit, cols = unit_cols(chunks)
+            lo = (chunks[0] % 2) * PACK * CHUNK
+            nc.vector.quantize_mx(
+                out=r_codes[unit][:, cols].bitcast(E5M2),
+                scales=r_plane[unit][:, cols],
+                in_=r_bf[chunks[0] // 2][:, lo : lo + PACK * CHUNK * len(chunks)],
+            )
+
+        def multiply(stage, tiles):
+            unit, tier = divmod(stage, 2)
+            half, g = divmod(unit, 2)
+            codes, plane, fmt = (r_codes, r_plane, E5M2) if tier else (q_codes, q_plane, E4M3)
+            for n in tiles:
+                first = g == 0 and tier == 0
+                if first:
+                    acc[half, n] = psum.tile([P, BANK], F32, tag="acc", bufs=6, name="acc")
+                if g == 0:
+                    weights = w8[:, 4 * P * n : 4 * P * (n + 1)].bitcast(E4M3)
+                else:
+                    weights = w4[:, 2 * P * n : 2 * P * (n + 1)].bitcast(E2M1)
+                nc.tensor.matmul_mx(
+                    out=acc[half, n][:],
+                    lhsT=weights,
+                    lhsT_scale=w_planes[g][:, P * n : P * (n + 1)],
+                    rhs=codes[unit][:].bitcast(fmt),
+                    rhs_scale=plane[unit][:],
+                    start=first,
+                    stop=(g == 1 and tier == 1),
+                )
+
+        def finish(half, n):
+            result = sb("result%d_%d" % (half, n), [P, BANK], F32)
+            nc.scalar.activation(out=result[:], in_=acc[half, n][:], func=GELU, bias=bias[:, n : n + 1], scale=1.0)
+            nc.sync.dma_start(out=out[n * P : (n + 1) * P, half * BANK : (half + 1) * BANK], in_=result[:])
+
+        for i in (0, 1, 2, 3):
+            cast([i], nc.scalar.copy)
+        quantise_x([0])
+        dequantise(0)
+        quantise_x([1])
+        dequantise(1)
+        subtract(0)
+        quantise_x([2])
+        dequantise(2)
+        subtract(1)
+        quantise_x([3])
+        dequantise(3)
+
+        last = N_CHUNKS // 2 - 1
+        for p in range(1, last + 1):
+            nxt = [2 * p + 2, 2 * p + 3]
+            if p < last:
+                cast(nxt, nc.scalar.copy)
+            if p == last - 1:
+                for n in range(1, N_TILES):
+                    finish(0, n)
+            subtract(2 * p)
+            if p < last:
+                quantise_x(nxt)
+                dequantise(nxt[0])
+            quantise_rest([2 * p - 2, 2 * p - 1])
+            if p == last - 1:
+                multiply(p - 2, [3])
+            multiply(p - 1, [0, 1])
+            subtract(2 * p + 1)
+            if p < last:
+                dequantise(nxt[1])
+            if p == last - 2:
+                finish(0, 0)
+                multiply(p - 1, [2])
+            else:
+                multiply(p - 1, [2, 3])
+
+        quantise_rest([2 * last])
+        quantise_rest([2 * last + 1])
+        multiply(last, range(N_TILES))
+        for n in range(N_TILES):
+            finish(1, n)

@@ -24,7 +24,7 @@ CHUNK = 128
 PER_UNIT = BANK // CHUNK
 N_CHUNKS = (K // K_PASS) * (T // CHUNK)
 N_TILES = N // P
-LINE = 4
+LINE = 2
 
 
 def tile_mix_tierx_mix_gelu_kernel(tc, x, w8_words, w8_scales, w4_words, w4_scales, b, out):

@@ -25,6 +25,7 @@ PER_UNIT = BANK // CHUNK
 N_CHUNKS = (K // K_PASS) * (T // CHUNK)
 N_TILES = N // P
 LINE = 2
+SINGLY = 2
 
 
 def tile_mix_tierx_mix_gelu_kernel(tc, x, w8_words, w8_scales, w4_words, w4_scales, b, out):
@@ -44,7 +45,7 @@ def tile_mix_tierx_mix_gelu_kernel(tc, x, w8_words, w8_scales, w4_words, w4_scal
         eye_plane = sb("eye_plane", [P, K_PASS], U8)
         make_identity(nc, eye[:])
         for plane in w_planes:
-            nc.gpsimd.memset(plane[:].bitcast(I32), 0)
+            nc.vector.memset(plane[:].bitcast(I32), 0)
         nc.vector.memset(eye_in[:].bitcast(I32), 0)
         nc.vector.tensor_copy(
             out=eye_in[:].rearrange("p (j s) -> p j s", j=PACK)[:, :, 0 : K_PASS : PACK],
@@ -74,19 +75,18 @@ def tile_mix_tierx_mix_gelu_kernel(tc, x, w8_words, w8_scales, w4_words, w4_scal
         w8 = sb("w8", [P, 4 * N], U8)
         w4 = sb("w4", [P, 2 * N], U8)
         bias = sb("bias", [P, N_TILES], F32)
-        load_x([0])
-        load_x([1])
+        load_x([0, 1])
         load_x([2, 3])
+        load_plane(w_planes[0], w8_scales)
         load_x([4, 5])
         nc.sync.dma_start(out=w8[:].bitcast(I32), in_=w8_words[0].rearrange("p n i -> p (n i)").bitcast(I32))
-        load_plane(w_planes[0], w8_scales)
         load_x([6, 7])
+        load_x([8, 9])
         nc.sync.dma_start(out=w4[:].bitcast(I32), in_=w4_words[0].bitcast(I32))
         load_plane(w_planes[1], w4_scales)
-        load_x([8, 9])
-        load_x([10, 11])
         with nc.allow_non_contiguous_dma(reason="one bias value to a partition"):
             nc.sync.dma_start(out=bias[:], in_=b.rearrange("(c p) -> p c", p=P))
+        load_x([10, 11])
         load_x([12, 13])
         load_x([14, 15])
 
@@ -183,51 +183,49 @@ def tile_mix_tierx_mix_gelu_kernel(tc, x, w8_words, w8_scales, w4_words, w4_scal
                     stop=(g == 1 and tier == 1),
                 )
 
-        def finish(half, n):
-            result = sb("result%d_%d" % (half, n), [P, BANK], F32)
-            nc.scalar.activation(out=result[:], in_=acc[half, n][:], func=GELU, bias=bias[:, n : n + 1], scale=1.0)
-            nc.sync.dma_start(out=out[n * P : (n + 1) * P, half * BANK : (half + 1) * BANK], in_=result[:])
+        def finish(half, n, pieces=1):
+            width = BANK // pieces
+            for lo in range(0, BANK, width):
+                result = sb("result%d_%d_%d" % (half, n, lo), [P, width], F32)
+                nc.scalar.activation(
+                    out=result[:], in_=acc[half, n][:, lo : lo + width], func=GELU, bias=bias[:, n : n + 1], scale=1.0
+                )
+                t0 = half * BANK + lo
+                nc.sync.dma_start(out=out[n * P : (n + 1) * P, t0 : t0 + width], in_=result[:])
 
-        for i in (0, 1, 2, 3):
-            cast([i], nc.scalar.copy)
-        quantise_x([0])
-        dequantise(0)
-        quantise_x([1])
-        dequantise(1)
-        subtract(0)
-        quantise_x([2])
-        dequantise(2)
-        subtract(1)
-        quantise_x([3])
-        dequantise(3)
+        def stage_x(chunks, copy):
+            cast(chunks, copy)
+            quantise_x(chunks)
+            dequantise(chunks[0])
 
+        stage_x([0], nc.vector.tensor_copy)
+        stage_x([1], nc.scalar.copy)
         last = N_CHUNKS // 2 - 1
-        for p in range(1, last + 1):
-            nxt = [2 * p + 2, 2 * p + 3]
-            if p < last:
-                cast(nxt, nc.scalar.copy)
-            if p == last - 1:
-                for n in range(1, N_TILES):
-                    finish(0, n)
+        for p in range(last + 1):
+            ahead = [2 * p + 2, 2 * p + 3]
+            singly = p < SINGLY
             subtract(2 * p)
             if p < last:
-                quantise_x(nxt)
-                dequantise(nxt[0])
-            quantise_rest([2 * p - 2, 2 * p - 1])
-            if p == last - 1:
-                multiply(p - 2, [3])
-            multiply(p - 1, [0, 1])
-            subtract(2 * p + 1)
-            if p < last:
-                dequantise(nxt[1])
+                stage_x(ahead[:1] if singly else ahead, nc.scalar.copy)
             if p == last - 2:
                 finish(0, 0)
-                multiply(p - 1, [2])
-            else:
+                finish(0, 1)
+            if p == last - 1:
+                finish(0, 2)
+                finish(0, 3)
+            if p > 0:
+                quantise_rest([2 * p - 2, 2 * p - 1])
+                multiply(p - 1, [0, 1])
+            subtract(2 * p + 1)
+            if singly:
+                stage_x(ahead[1:], nc.scalar.copy)
+            elif p < last:
+                dequantise(ahead[1])
+            if p > 0:
                 multiply(p - 1, [2, 3])
 
         quantise_rest([2 * last])
         quantise_rest([2 * last + 1])
         multiply(last, range(N_TILES))
         for n in range(N_TILES):
-            finish(1, n)
+            finish(1, n, 2 if n == N_TILES - 1 else 1)

@@ -43,21 +43,24 @@ def tile_mix_tierx_mix_gelu_kernel(tc, x, w8_words, w8_scales, w4_words, w4_scal
         eye = sb("eye", [P, P], BF16)
         eye_codes = sb("eye_codes", [P, K_PASS], U32)
         eye_plane = sb("eye_plane", [P, K_PASS], U8)
+        bias_rows = sb("bias_rows", [P, P], F32)
+        bias = sb("bias", [P, P], F32)
         make_identity(nc, eye[:])
-        for plane in w_planes:
-            nc.vector.memset(plane[:].bitcast(I32), 0)
         nc.vector.memset(eye_in[:].bitcast(I32), 0)
+        nc.vector.memset(bias_rows[:], 0.0)
         nc.vector.tensor_copy(
             out=eye_in[:].rearrange("p (j s) -> p j s", j=PACK)[:, :, 0 : K_PASS : PACK],
             in_=eye[:].unsqueeze(1).to_broadcast([P, PACK, P]),
         )
+        for plane in w_planes:
+            nc.vector.memset(plane[:].bitcast(I32), 0)
         nc.vector.quantize_mx(out=eye_codes[:].bitcast(E4M3), scales=eye_plane[:], in_=eye_in[:, 0 : PACK * K_PASS])
 
         raw = {}
 
         def load_x(chunks):
             unit, c = divmod(chunks[0], PER_UNIT)
-            half, g = divmod(unit, 2)
+            half, g = unit // 2, 1 - unit % 2
             width = CHUNK * len(chunks)
             t0 = half * BANK + c * CHUNK
             slab = sb("x%d" % chunks[0], [P, PACK, width], F32)
@@ -74,18 +77,29 @@ def tile_mix_tierx_mix_gelu_kernel(tc, x, w8_words, w8_scales, w4_words, w4_scal
 
         w8 = sb("w8", [P, 4 * N], U8)
         w4 = sb("w4", [P, 2 * N], U8)
-        bias = sb("bias", [P, N_TILES], F32)
+
+        def load_w8():
+            nc.sync.dma_start(out=w8[:].bitcast(I32), in_=w8_words[0].rearrange("p n i -> p (n i)").bitcast(I32))
+
+        def load_w4():
+            nc.sync.dma_start(out=w4[:].bitcast(I32), in_=w4_words[0].bitcast(I32))
+
+        def load_bias():
+            nc.sync.dma_start(
+                out=bias_rows[0:P:32, :].rearrange("q (n i) -> q n i", n=N_TILES),
+                in_=b.rearrange("(n q i) -> q n i", n=N_TILES, q=4),
+            )
+
         load_x([0, 1])
         load_x([2, 3])
-        load_plane(w_planes[0], w8_scales)
-        load_x([4, 5])
-        nc.sync.dma_start(out=w8[:].bitcast(I32), in_=w8_words[0].rearrange("p n i -> p (n i)").bitcast(I32))
-        load_x([6, 7])
-        load_x([8, 9])
-        nc.sync.dma_start(out=w4[:].bitcast(I32), in_=w4_words[0].bitcast(I32))
         load_plane(w_planes[1], w4_scales)
-        with nc.allow_non_contiguous_dma(reason="one bias value to a partition"):
-            nc.sync.dma_start(out=bias[:], in_=b.rearrange("(c p) -> p c", p=P))
+        load_x([4, 5])
+        load_w4()
+        load_x([6, 7])
+        load_plane(w_planes[0], w8_scales)
+        load_x([8, 9])
+        load_w8()
+        load_bias()
         load_x([10, 11])
         load_x([12, 13])
         load_x([14, 15])
@@ -163,10 +177,10 @@ def tile_mix_tierx_mix_gelu_kernel(tc, x, w8_words, w8_scales, w4_words, w4_scal
 
         def multiply(stage, tiles):
             unit, tier = divmod(stage, 2)
-            half, g = divmod(unit, 2)
+            half, g = unit // 2, 1 - unit % 2
             codes, plane, fmt = (r_codes, r_plane, E5M2) if tier else (q_codes, q_plane, E4M3)
             for n in tiles:
-                first = g == 0 and tier == 0
+                first = unit % 2 == 0 and tier == 0
                 if first:
                     acc[half, n] = psum.tile([P, BANK], F32, tag="acc", bufs=6, name="acc")
                 if g == 0:
@@ -180,7 +194,7 @@ def tile_mix_tierx_mix_gelu_kernel(tc, x, w8_words, w8_scales, w4_words, w4_scal
                     rhs=codes[unit][:].bitcast(fmt),
                     rhs_scale=plane[unit][:],
                     start=first,
-                    stop=(g == 1 and tier == 1),
+                    stop=(unit % 2 == 1 and tier == 1),
                 )
 
         def finish(half, n, pieces=1):
@@ -188,44 +202,51 @@ def tile_mix_tierx_mix_gelu_kernel(tc, x, w8_words, w8_scales, w4_words, w4_scal
             for lo in range(0, BANK, width):
                 result = sb("result%d_%d_%d" % (half, n, lo), [P, width], F32)
                 nc.scalar.activation(
-                    out=result[:], in_=acc[half, n][:, lo : lo + width], func=GELU, bias=bias[:, n : n + 1], scale=1.0
+                    out=result[:], in_=acc[half, n][:, lo : lo + width], func=GELU, bias=bias[:, 32 * n : 32 * n + 1], scale=1.0
                 )
                 t0 = half * BANK + lo
                 nc.sync.dma_start(out=out[n * P : (n + 1) * P, t0 : t0 + width], in_=result[:])
 
-        def stage_x(chunks, copy):
-            cast(chunks, copy)
-            quantise_x(chunks)
-            dequantise(chunks[0])
+        def stage_x(i, copy):
+            cast([i], copy)
+            quantise_x([i])
+            dequantise(i)
 
-        stage_x([0], nc.vector.tensor_copy)
-        stage_x([1], nc.scalar.copy)
-        last = N_CHUNKS // 2 - 1
-        for p in range(last + 1):
-            ahead = [2 * p + 2, 2 * p + 3]
-            singly = p < SINGLY
-            subtract(2 * p)
-            if p < last:
-                stage_x(ahead[:1] if singly else ahead, nc.scalar.copy)
-            if p == last - 2:
-                finish(0, 0)
-                finish(0, 1)
-            if p == last - 1:
-                finish(0, 2)
-                finish(0, 3)
-            if p > 0:
-                quantise_rest([2 * p - 2, 2 * p - 1])
-                multiply(p - 1, [0, 1])
-            subtract(2 * p + 1)
-            if singly:
-                stage_x(ahead[1:], nc.scalar.copy)
-            elif p < last:
-                dequantise(ahead[1])
-            if p > 0:
-                multiply(p - 1, [2, 3])
-
-        quantise_rest([2 * last])
-        quantise_rest([2 * last + 1])
-        multiply(last, range(N_TILES))
-        for n in range(N_TILES):
-            finish(1, n, 2 if n == N_TILES - 1 else 1)
+        ahead = 2
+        spare = 2
+        finish_at = [10, 12, 14, 14]
+        passes = []
+        for stage in range(2 * n_units):
+            unit, tier = divmod(stage, 2)
+            codes_at = PER_UNIT * unit + (PER_UNIT if tier else PER_UNIT - 1 - ahead)
+            for n in range(N_TILES):
+                bank_at = finish_at[n - spare] + 1 if unit >= 2 and n >= spare else 0
+                passes.append((max(codes_at, bank_at), stage, n))
+        passes.sort()
+        stage_x(0, nc.vector.tensor_copy)
+        for i in range(1, ahead):
+            stage_x(i, nc.scalar.copy)
+        for i in range(N_CHUNKS):
+            subtract(i)
+            if i + ahead < N_CHUNKS:
+                stage_x(i + ahead, nc.scalar.copy)
+            if i >= 2 and i % 2 == 0:
+                quantise_rest([i - 2, i - 1])
+            if i == 9:
+                nc.vector.transpose(out=bias[:], in_=bias_rows[:])
+            for n in range(N_TILES):
+                if finish_at[n] == i:
+                    finish(0, n)
+            for turn in range(2 if i < 15 else 1):
+                ready = [entry for entry in passes if entry[0] <= i]
+                if ready:
+                    entry = min(ready, key=lambda e: (e[1] // 4, e[2], e[1]))
+                    passes.remove(entry)
+                    multiply(entry[1], [entry[2]])
+        quantise_rest([N_CHUNKS - 2])
+        quantise_rest([N_CHUNKS - 1])
+        passes.sort(key=lambda entry: (entry[2], entry[1]))
+        for at, stage, n in passes:
+            multiply(stage, [n])
+            if stage == 2 * n_units - 1:
+                finish(1, n, 2 if n == N_TILES - 1 else 1)

@@ -90,16 +90,17 @@ def tile_mix_tierx_mix_gelu_kernel(tc, x, w8_words, w8_scales, w4_words, w4_scal
                 in_=b.rearrange("(n q i) -> q n i", n=N_TILES, q=4),
             )
 
-        load_x([0, 1])
-        load_x([2, 3])
-        load_plane(w_planes[1], w4_scales)
+        load_x([0])
+        load_x([1, 2])
+        load_x([3])
         load_x([4, 5])
+        load_plane(w_planes[1], w4_scales)
         load_w4()
         load_x([6, 7])
-        load_plane(w_planes[0], w8_scales)
         load_x([8, 9])
-        load_w8()
         load_bias()
+        load_plane(w_planes[0], w8_scales)
+        load_w8()
         load_x([10, 11])
         load_x([12, 13])
         load_x([14, 15])
@@ -223,16 +224,16 @@ def tile_mix_tierx_mix_gelu_kernel(tc, x, w8_words, w8_scales, w4_words, w4_scal
                 bank_at = finish_at[n - spare] + 1 if unit >= 2 and n >= spare else 0
                 passes.append((max(codes_at, bank_at), stage, n))
         passes.sort()
-        stage_x(0, nc.vector.tensor_copy)
+        stage_x(0, nc.scalar.copy)
         for i in range(1, ahead):
-            stage_x(i, nc.scalar.copy)
+            stage_x(i, nc.vector.tensor_copy)
         for i in range(N_CHUNKS):
             subtract(i)
             if i + ahead < N_CHUNKS:
                 stage_x(i + ahead, nc.scalar.copy)
             if i >= 2 and i % 2 == 0:
                 quantise_rest([i - 2, i - 1])
-            if i == 9:
+            if i == 7:
                 nc.vector.transpose(out=bias[:], in_=bias_rows[:])
             for n in range(N_TILES):
                 if finish_at[n] == i:

@@ -1,7 +1,6 @@
 from contextlib import ExitStack
 
 import concourse.mybir as mybir
-from concourse.masks import make_identity
 
 K, N, T = 1024, 512, 1024
 FLOPS = 2 * 2 * K * N * T
@@ -39,22 +38,39 @@ def tile_mix_tierx_mix_gelu_kernel(tc, x, w8_words, w8_scales, w4_words, w4_scal
             return keep.tile(shape, dtype, name=name, align_bytes=64)
 
         w_planes = [sb("w8_plane", [P, N], U8), sb("w4_plane", [P, N], U8)]
-        eye_in = sb("eye_in", [P, PACK * (K_PASS + 1)], BF16)
-        eye = sb("eye", [P, P], BF16)
+        diag = sb("diag", [P, K_PASS + PACK], BF16)
+        shifted = sb("shifted", [P, (PACK - 1) * K_PASS], BF16)
         eye_codes = sb("eye_codes", [P, K_PASS], U32)
         eye_plane = sb("eye_plane", [P, K_PASS], U8)
         bias_rows = sb("bias_rows", [P, P], F32)
         bias = sb("bias", [P, P], F32)
-        make_identity(nc, eye[:])
-        nc.vector.memset(eye_in[:].bitcast(I32), 0)
-        nc.vector.memset(bias_rows[:], 0.0)
-        nc.vector.tensor_copy(
-            out=eye_in[:].rearrange("p (j s) -> p j s", j=PACK)[:, :, 0 : K_PASS : PACK],
-            in_=eye[:].unsqueeze(1).to_broadcast([P, PACK, P]),
+        nc.gpsimd.memset(diag[:].bitcast(I32), 0)
+        nc.gpsimd.affine_select(
+            out=diag[:].bitcast(F32),
+            in_=diag[:].bitcast(F32),
+            compare_op=mybir.AluOpType.not_equal,
+            fill=1.0,
+            base=1,
+            pattern=[[-1, (K_PASS + PACK) // 2]],
+            channel_multiplier=2,
         )
-        for plane in w_planes:
-            nc.vector.memset(plane[:].bitcast(I32), 0)
-        nc.vector.quantize_mx(out=eye_codes[:].bitcast(E4M3), scales=eye_plane[:], in_=eye_in[:, 0 : PACK * K_PASS])
+        nc.vector.memset(bias_rows[:], 0.0)
+        table_warm = sb("table_warm", [P, 1], F32)
+        nc.scalar.activation(out=table_warm[:], in_=bias_rows[:, 0:1], func=GELU, bias=bias_rows[:, 1:2], scale=1.0)
+        nc.vector.memset(w_planes[1][:].bitcast(I32), 0)
+        nc.vector.memset(w_planes[0][:].bitcast(I32), 0)
+
+        def quantise_eye(lo, hi, rows):
+            nc.vector.quantize_mx(
+                out=eye_codes[:, lo * P : hi * P].bitcast(E4M3), scales=eye_plane[:, lo * P : hi * P], in_=rows
+            )
+
+        quantise_eye(3, 4, diag[:, 0:K_PASS])
+        for j in range(PACK - 1):
+            shift = PACK - 1 - j
+            nc.vector.tensor_copy(out=shifted[:, j * K_PASS : (j + 1) * K_PASS], in_=diag[:, shift : shift + K_PASS])
+        quantise_eye(0, 2, shifted[:, 0 : 2 * K_PASS])
+        quantise_eye(2, 3, shifted[:, 2 * K_PASS :])
 
         raw = {}
 
@@ -91,17 +107,18 @@ def tile_mix_tierx_mix_gelu_kernel(tc, x, w8_words, w8_scales, w4_words, w4_scal
             )
 
         load_x([0])
-        load_x([1, 2])
+        load_x([1])
+        load_x([2])
         load_x([3])
         load_x([4, 5])
+        load_x([6, 7])
         load_plane(w_planes[1], w4_scales)
         load_w4()
-        load_x([6, 7])
         load_x([8, 9])
-        load_bias()
-        load_plane(w_planes[0], w8_scales)
         load_w8()
+        load_plane(w_planes[0], w8_scales)
         load_x([10, 11])
+        load_bias()
         load_x([12, 13])
         load_x([14, 15])
 
@@ -222,18 +239,29 @@ def tile_mix_tierx_mix_gelu_kernel(tc, x, w8_words, w8_scales, w4_words, w4_scal
             codes_at = PER_UNIT * unit + (PER_UNIT if tier else PER_UNIT - 1 - ahead)
             for n in range(N_TILES):
                 bank_at = finish_at[n - spare] + 1 if unit >= 2 and n >= spare else 0
-                passes.append((max(codes_at, bank_at), stage, n))
+                passes.append((max(codes_at, bank_at, 2), stage, n))
         passes.sort()
-        stage_x(0, nc.scalar.copy)
+        warm = psum.tile([P, BANK], F32, tag="acc", bufs=6, name="acc")
+        for cols in [slice(3 * P, 4 * P)] * 4 + [slice(0, BANK)] * 2:
+            nc.tensor.matmul_mx(
+                out=warm[:, cols],
+                lhsT=eye_codes[:, 3 * P :].bitcast(E4M3),
+                lhsT_scale=eye_plane[:, 3 * P :],
+                rhs=eye_codes[:, cols].bitcast(E4M3),
+                rhs_scale=eye_plane[:, cols],
+                start=True,
+                stop=True,
+            )
+        stage_x(0, nc.vector.tensor_copy)
         for i in range(1, ahead):
-            stage_x(i, nc.vector.tensor_copy)
+            stage_x(i, nc.scalar.copy)
         for i in range(N_CHUNKS):
             subtract(i)
             if i + ahead < N_CHUNKS:
                 stage_x(i + ahead, nc.scalar.copy)
             if i >= 2 and i % 2 == 0:
                 quantise_rest([i - 2, i - 1])
-            if i == 7:
+            if i == 8:
                 nc.vector.transpose(out=bias[:], in_=bias_rows[:])
             for n in range(N_TILES):
                 if finish_at[n] == i:
@@ -250,4 +278,4 @@ def tile_mix_tierx_mix_gelu_kernel(tc, x, w8_words, w8_scales, w4_words, w4_scal
         for at, stage, n in passes:
             multiply(stage, [n])
             if stage == 2 * n_units - 1:
-                finish(1, n, 2 if n == N_TILES - 1 else 1)
+                finish(1, n, 2 if n in (0, N_TILES - 1) else 1)

@@ -24,7 +24,11 @@ PER_UNIT = BANK // CHUNK
 N_CHUNKS = (K // K_PASS) * (T // CHUNK)
 N_TILES = N // P
 LINE = 2
-SINGLY = 2
+AHEAD = 2
+SUM_BANKS = 6
+SPLIT = 1
+READ_AT = [10, 12, 12, 13]
+EYE_ORDER = [3, 1, 0, 2]
 
 
 def tile_mix_tierx_mix_gelu_kernel(tc, x, w8_words, w8_scales, w4_words, w4_scales, b, out):
@@ -37,7 +41,7 @@ def tile_mix_tierx_mix_gelu_kernel(tc, x, w8_words, w8_scales, w4_words, w4_scal
         def sb(name, shape, dtype):
             return keep.tile(shape, dtype, name=name, align_bytes=64)
 
-        w_planes = [sb("w8_plane", [P, N], U8), sb("w4_plane", [P, N], U8)]
+        w_planes = sb("w_planes", [P, 2 * N], U8)
         diag = sb("diag", [P, K_PASS + PACK], BF16)
         shifted = sb("shifted", [P, (PACK - 1) * K_PASS], BF16)
         eye_codes = sb("eye_codes", [P, K_PASS], U32)
@@ -45,88 +49,92 @@ def tile_mix_tierx_mix_gelu_kernel(tc, x, w8_words, w8_scales, w4_words, w4_scal
         bias_rows = sb("bias_rows", [P, P], F32)
         bias = sb("bias", [P, P], F32)
         nc.gpsimd.memset(diag[:].bitcast(I32), 0)
+        nc.vector.memset(bias_rows[:], 0.0)
+        nc.vector.memset(w_planes[:].bitcast(I32), 0)
+        table_warm = sb("table_warm", [P, 1], F32)
+        nc.scalar.activation(
+            out=table_warm[:], in_=diag[:].bitcast(F32)[:, 0:1], func=GELU, bias=diag[:].bitcast(F32)[:, 0:1], scale=1.0
+        )
         nc.gpsimd.affine_select(
-            out=diag[:].bitcast(F32),
-            in_=diag[:].bitcast(F32),
+            out=diag[:].bitcast(F32)[:, 1:],
+            in_=diag[:].bitcast(F32)[:, 1:],
             compare_op=mybir.AluOpType.not_equal,
             fill=1.0,
-            base=1,
-            pattern=[[-1, (K_PASS + PACK) // 2]],
+            base=0,
+            pattern=[[-1, (K_PASS + PACK) // 2 - 1]],
             channel_multiplier=2,
         )
-        nc.vector.memset(bias_rows[:], 0.0)
-        table_warm = sb("table_warm", [P, 1], F32)
-        nc.scalar.activation(out=table_warm[:], in_=bias_rows[:, 0:1], func=GELU, bias=bias_rows[:, 1:2], scale=1.0)
-        nc.vector.memset(w_planes[1][:].bitcast(I32), 0)
-        nc.vector.memset(w_planes[0][:].bitcast(I32), 0)
 
-        def quantise_eye(lo, hi, rows):
-            nc.vector.quantize_mx(
-                out=eye_codes[:, lo * P : hi * P].bitcast(E4M3), scales=eye_plane[:, lo * P : hi * P], in_=rows
+        def eye_cols(slot, count=1):
+            return slice(slot * P, (slot + count) * P)
+
+        def quantise_eye(slot, count, rows):
+            cols = eye_cols(slot, count)
+            nc.vector.quantize_mx(out=eye_codes[:, cols].bitcast(E4M3), scales=eye_plane[:, cols], in_=rows)
+
+        def shift_diag(slot):
+            shift = PACK - 1 - EYE_ORDER[slot]
+            nc.vector.tensor_copy(
+                out=shifted[:, (slot - 1) * K_PASS : slot * K_PASS], in_=diag[:, shift : shift + K_PASS]
             )
 
-        quantise_eye(3, 4, diag[:, 0:K_PASS])
-        for j in range(PACK - 1):
-            shift = PACK - 1 - j
-            nc.vector.tensor_copy(out=shifted[:, j * K_PASS : (j + 1) * K_PASS], in_=diag[:, shift : shift + K_PASS])
-        quantise_eye(0, 2, shifted[:, 0 : 2 * K_PASS])
-        quantise_eye(2, 3, shifted[:, 2 * K_PASS :])
+        quantise_eye(0, 1, diag[:, 0:K_PASS])
+        shift_diag(1)
+        shift_diag(2)
+        quantise_eye(1, 1, shifted[:, 0:K_PASS])
+        shift_diag(3)
+        quantise_eye(2, 2, shifted[:, K_PASS:])
 
         raw = {}
 
-        def load_x(chunks):
-            unit, c = divmod(chunks[0], PER_UNIT)
-            half, g = unit // 2, 1 - unit % 2
-            width = CHUNK * len(chunks)
-            t0 = half * BANK + c * CHUNK
-            slab = sb("x%d" % chunks[0], [P, PACK, width], F32)
+        def place(i):
+            unit, c = divmod(i, PER_UNIT)
+            return 1 - unit % 2, (unit // 2) * BANK + c * CHUNK
+
+        def load_x(first, count):
+            g, t0 = place(first)
+            width = CHUNK * count
+            slab = sb("x%d" % first, [P, PACK, width], F32)
             nc.sync.dma_start(
                 out=slab[:],
                 in_=x[g * K_PASS : (g + 1) * K_PASS, t0 : t0 + width].rearrange("(p j) w -> p j w", j=PACK),
             )
-            for pos, i in enumerate(chunks):
-                raw[i] = (slab, pos * CHUNK)
+            for pos in range(count):
+                raw[first + pos] = slab[:, :, pos * CHUNK : (pos + 1) * CHUNK]
 
-        def load_plane(plane, scales):
+        def load_plane(g, scales):
             for r in range(4):
-                nc.sync.dma_start(out=plane[r:P:32, :].bitcast(I32), in_=scales[0, r:16:4, :].bitcast(I32))
+                nc.sync.dma_start(
+                    out=w_planes[r:P:32, g * N : (g + 1) * N].bitcast(I32), in_=scales[0, r:16:4, :].bitcast(I32)
+                )
 
         w8 = sb("w8", [P, 4 * N], U8)
         w4 = sb("w4", [P, 2 * N], U8)
+        load_x(0, 1)
+        load_x(1, 1)
+        nc.sync.dma_start(
+            out=bias_rows[0:P:32, :].rearrange("q (n i) -> q n i", n=N_TILES),
+            in_=b.rearrange("(n q i) -> q n i", n=N_TILES, q=4),
+        )
+        load_x(2, 1)
+        load_x(3, 1)
+        load_x(4, 2)
+        nc.sync.dma_start(out=w4[:].bitcast(I32), in_=w4_words[0].bitcast(I32))
+        load_plane(1, w4_scales)
+        load_x(6, 2)
+        load_x(8, 2)
+        nc.sync.dma_start(out=w8[:].bitcast(I32), in_=w8_words[0].rearrange("p n i -> p (n i)").bitcast(I32))
+        load_plane(0, w8_scales)
+        load_x(10, 2)
+        load_x(12, 2)
+        load_x(14, 2)
 
-        def load_w8():
-            nc.sync.dma_start(out=w8[:].bitcast(I32), in_=w8_words[0].rearrange("p n i -> p (n i)").bitcast(I32))
-
-        def load_w4():
-            nc.sync.dma_start(out=w4[:].bitcast(I32), in_=w4_words[0].bitcast(I32))
-
-        def load_bias():
-            nc.sync.dma_start(
-                out=bias_rows[0:P:32, :].rearrange("q (n i) -> q n i", n=N_TILES),
-                in_=b.rearrange("(n q i) -> q n i", n=N_TILES, q=4),
-            )
-
-        load_x([0])
-        load_x([1])
-        load_x([2])
-        load_x([3])
-        load_x([4, 5])
-        load_x([6, 7])
-        load_plane(w_planes[1], w4_scales)
-        load_w4()
-        load_x([8, 9])
-        load_w8()
-        load_plane(w_planes[0], w8_scales)
-        load_x([10, 11])
-        load_bias()
-        load_x([12, 13])
-        load_x([14, 15])
-
-        n_units = N_CHUNKS // PER_UNIT
-        q_codes = [sb("q_codes%d" % u, [P, BANK], U32) for u in range(n_units)]
-        q_plane = [sb("q_plane%d" % u, [P, BANK], U8) for u in range(n_units)]
-        r_codes = [sb("r_codes%d" % u, [P, BANK], U32) for u in range(n_units)]
-        r_plane = [sb("r_plane%d" % u, [P, BANK], U8) for u in range(n_units)]
+        q_codes = [sb("q_codes%d" % g, [P, T], U32) for g in range(2)]
+        q_plane = [sb("q_plane%d" % g, [P, T], U8) for g in range(2)]
+        r_codes = [sb("r_codes%d" % g, [P, T], U32) for g in range(2)]
+        r_plane = [sb("r_plane%d" % g, [P, T], U8) for g in range(2)]
+        x_bf = sb("x_bf", [P, N_CHUNKS * K_PASS], BF16)
+        r_bf = sb("r_bf", [P, N_CHUNKS * K_PASS], BF16)
 
         def rows_walk(ap):
             return ap.rearrange("p j (c i) -> p c j i", i=LINE)
@@ -134,148 +142,163 @@ def tile_mix_tierx_mix_gelu_kernel(tc, x, w8_words, w8_scales, w4_words, w4_scal
         def words_walk(ap):
             return ap.rearrange("p (c i j) -> p c j i", i=LINE, j=PACK)
 
-        def x_rows(chunks):
-            slab, pos = raw[chunks[0]]
-            return slab[:, :, pos : pos + CHUNK * len(chunks)]
-
-        def unit_cols(chunks):
-            unit, c = divmod(chunks[0], PER_UNIT)
-            return unit, slice(c * CHUNK, (c + len(chunks)) * CHUNK)
-
-        x_bf = {}
-        r_bf = {}
         values = {}
         acc = {}
 
-        def cast(chunks, copy):
-            staged = sb("x_bf%d" % chunks[0], [P, PACK * CHUNK * len(chunks)], BF16)
-            copy(out=words_walk(staged[:]), in_=rows_walk(x_rows(chunks)))
-            x_bf[chunks[0]] = staged
-
-        def quantise_x(chunks):
-            unit, cols = unit_cols(chunks)
-            nc.vector.quantize_mx(
-                out=q_codes[unit][:, cols].bitcast(E4M3), scales=q_plane[unit][:, cols], in_=x_bf[chunks[0]][:]
+        def cast(i, copy, lo=0, hi=CHUNK):
+            copy(
+                out=words_walk(x_bf[:, i * K_PASS + lo * PACK : i * K_PASS + hi * PACK]),
+                in_=rows_walk(raw[i][:, :, lo:hi]),
             )
 
+        def quantise(codes, plane, fmt, staged, first, count):
+            g, t0 = place(first)
+            cols = slice(t0, t0 + count * CHUNK)
+            nc.vector.quantize_mx(
+                out=codes[g][:, cols].bitcast(fmt),
+                scales=plane[g][:, cols],
+                in_=staged[:, first * K_PASS : (first + count) * K_PASS],
+            )
+
+        def quantise_x(first, count=1):
+            quantise(q_codes, q_plane, E4M3, x_bf, first, count)
+
+        def quantise_rest(first, count):
+            quantise(r_codes, r_plane, E5M2, r_bf, first, count)
+
         def dequantise(i):
-            unit, cols = unit_cols([i])
+            g, t0 = place(i)
+            cols = slice(t0, t0 + CHUNK)
             bank = psum.tile([P, PACK, CHUNK], F32, tag="values", bufs=2, name="values")
-            for j in range(PACK):
+            for slot, j in enumerate(EYE_ORDER):
                 nc.tensor.matmul_mx(
                     out=bank[:, j, :],
-                    lhsT=eye_codes[:, j * P : (j + 1) * P].bitcast(E4M3),
-                    lhsT_scale=eye_plane[:, j * P : (j + 1) * P],
-                    rhs=q_codes[unit][:, cols].bitcast(E4M3),
-                    rhs_scale=q_plane[unit][:, cols],
+                    lhsT=eye_codes[:, eye_cols(slot)].bitcast(E4M3),
+                    lhsT_scale=eye_plane[:, eye_cols(slot)],
+                    rhs=q_codes[g][:, cols].bitcast(E4M3),
+                    rhs_scale=q_plane[g][:, cols],
                     start=True,
                     stop=True,
                 )
             values[i] = bank
 
         def subtract(i):
-            if i % 2 == 0:
-                r_bf[i // 2] = sb("r_bf%d" % i, [P, 2 * PACK * CHUNK], BF16)
-            lo = (i % 2) * PACK * CHUNK
             nc.vector.tensor_tensor(
-                out=words_walk(r_bf[i // 2][:, lo : lo + PACK * CHUNK]),
-                in0=rows_walk(x_rows([i])),
+                out=words_walk(r_bf[:, i * K_PASS : (i + 1) * K_PASS]),
+                in0=rows_walk(raw[i]),
                 in1=rows_walk(values[i][:]),
                 op=mybir.AluOpType.subtract,
             )
 
-        def quantise_rest(chunks):
-            unit, cols = unit_cols(chunks)
-            lo = (chunks[0] % 2) * PACK * CHUNK
-            nc.vector.quantize_mx(
-                out=r_codes[unit][:, cols].bitcast(E5M2),
-                scales=r_plane[unit][:, cols],
-                in_=r_bf[chunks[0] // 2][:, lo : lo + PACK * CHUNK * len(chunks)],
-            )
-
-        def multiply(stage, tiles):
-            unit, tier = divmod(stage, 2)
-            half, g = unit // 2, 1 - unit % 2
+        def multiply(sum_id, g, tier):
+            n, window, lo, hi = sum_id
             codes, plane, fmt = (r_codes, r_plane, E5M2) if tier else (q_codes, q_plane, E4M3)
-            for n in tiles:
-                first = unit % 2 == 0 and tier == 0
-                if first:
-                    acc[half, n] = psum.tile([P, BANK], F32, tag="acc", bufs=6, name="acc")
-                if g == 0:
-                    weights = w8[:, 4 * P * n : 4 * P * (n + 1)].bitcast(E4M3)
-                else:
-                    weights = w4[:, 2 * P * n : 2 * P * (n + 1)].bitcast(E2M1)
+            first = sum_id not in acc
+            if first:
+                acc[sum_id] = psum.tile([P, BANK], F32, tag="acc", bufs=SUM_BANKS, name="acc")
+            if g == 0:
+                weights = w8[:, 4 * P * n : 4 * P * (n + 1)].bitcast(E4M3)
+            else:
+                weights = w4[:, 2 * P * n : 2 * P * (n + 1)].bitcast(E2M1)
+            if tier or hi - lo == BANK:
+                spans = [(window, window + BANK)]
+            else:
+                width = CHUNK if g else hi - lo
+                spans = [(t0, t0 + width) for t0 in range(lo, hi, width)]
+            for t0, t1 in spans:
                 nc.tensor.matmul_mx(
-                    out=acc[half, n][:],
+                    out=acc[sum_id][:, t0 - window : t1 - window],
                     lhsT=weights,
-                    lhsT_scale=w_planes[g][:, P * n : P * (n + 1)],
-                    rhs=codes[unit][:].bitcast(fmt),
-                    rhs_scale=plane[unit][:],
+                    lhsT_scale=w_planes[:, g * N + P * n : g * N + P * (n + 1)],
+                    rhs=codes[g][:, t0:t1].bitcast(fmt),
+                    rhs_scale=plane[g][:, t0:t1],
                     start=first,
-                    stop=(unit % 2 == 1 and tier == 1),
+                    stop=(g == 0 and tier == 1),
                 )
 
-        def finish(half, n, pieces=1):
-            width = BANK // pieces
-            for lo in range(0, BANK, width):
-                result = sb("result%d_%d_%d" % (half, n, lo), [P, width], F32)
+        def finish(sum_id, pieces=1):
+            n, window, lo, hi = sum_id
+            width = (hi - lo) // pieces
+            for t0 in range(lo, hi, width):
+                result = sb("result%d_%d" % (n, t0), [P, width], F32)
                 nc.scalar.activation(
-                    out=result[:], in_=acc[half, n][:, lo : lo + width], func=GELU, bias=bias[:, 32 * n : 32 * n + 1], scale=1.0
+                    out=result[:],
+                    in_=acc[sum_id][:, t0 - window : t0 - window + width],
+                    func=GELU,
+                    bias=bias[:, 32 * n : 32 * n + 1],
+                    scale=1.0,
                 )
-                t0 = half * BANK + lo
                 nc.sync.dma_start(out=out[n * P : (n + 1) * P, t0 : t0 + width], in_=result[:])
 
-        def stage_x(i, copy):
-            cast([i], copy)
-            quantise_x([i])
-            dequantise(i)
-
-        ahead = 2
-        spare = 2
-        finish_at = [10, 12, 14, 14]
-        passes = []
-        for stage in range(2 * n_units):
-            unit, tier = divmod(stage, 2)
-            codes_at = PER_UNIT * unit + (PER_UNIT if tier else PER_UNIT - 1 - ahead)
-            for n in range(N_TILES):
-                bank_at = finish_at[n - spare] + 1 if unit >= 2 and n >= spare else 0
-                passes.append((max(codes_at, bank_at, 2), stage, n))
-        passes.sort()
-        warm = psum.tile([P, BANK], F32, tag="acc", bufs=6, name="acc")
-        for cols in [slice(3 * P, 4 * P)] * 4 + [slice(0, BANK)] * 2:
+        warm = psum.tile([P, BANK], F32, tag="acc", bufs=SUM_BANKS, name="acc")
+        for count in [1] * 4 + [2] * 4:
             nc.tensor.matmul_mx(
-                out=warm[:, cols],
-                lhsT=eye_codes[:, 3 * P :].bitcast(E4M3),
-                lhsT_scale=eye_plane[:, 3 * P :],
-                rhs=eye_codes[:, cols].bitcast(E4M3),
-                rhs_scale=eye_plane[:, cols],
+                out=warm[:, eye_cols(0, count)],
+                lhsT=eye_codes[:, eye_cols(0)].bitcast(E4M3),
+                lhsT_scale=eye_plane[:, eye_cols(0)],
+                rhs=eye_codes[:, eye_cols(0, count)].bitcast(E4M3),
+                rhs_scale=eye_plane[:, eye_cols(0, count)],
                 start=True,
                 stop=True,
             )
-        stage_x(0, nc.vector.tensor_copy)
-        for i in range(1, ahead):
-            stage_x(i, nc.scalar.copy)
+
+        last_cast = N_CHUNKS - 1 - AHEAD
+        cut = BANK + BANK // 2
+        whole = N_TILES - SPLIT
+        first_half = [(n, 0, 0, BANK) for n in range(N_TILES)]
+        early = [(n, cut - BANK, BANK, cut) for n in range(whole, N_TILES)]
+        late = [(n, BANK, BANK if n < whole else cut, T) for n in range(N_TILES)]
+        sums = first_half + late[: SUM_BANKS - N_TILES - SPLIT] + early + late[SUM_BANKS - N_TILES - SPLIT :]
+        read_at = dict(zip(first_half, READ_AT))
+        waiting = []
+        for sum_id in sums:
+            order = [(1, 0), (1, 1), (0, 0), (0, 1)] if sum_id[3] - sum_id[2] == BANK else [(1, 1), (1, 0), (0, 0), (0, 1)]
+            waiting.extend((sum_id, g, tier) for g, tier in order)
+
+        def ready_at(sum_id, g, tier):
+            last_block = sum_id[3] // CHUNK - 1
+            last_chunk = 2 * PER_UNIT * (last_block // PER_UNIT) + PER_UNIT * (1 - g) + last_block % PER_UNIT
+            codes_at = last_chunk + 1 if tier else last_chunk - AHEAD
+            reused = sums.index(sum_id) - SUM_BANKS
+            return max(codes_at, read_at[sums[reused]] + 1 if reused >= 0 else 0)
+
+        def take_passes(i, count):
+            for turn in range(count):
+                seen = set()
+                for entry in waiting:
+                    opened = entry[0] in acc
+                    if ready_at(*entry) <= i and (entry[0] not in seen or (opened and entry[1:] != (0, 1))):
+                        waiting.remove(entry)
+                        multiply(*entry)
+                        if entry[0] in early and entry[1:] == (0, 1):
+                            finish(entry[0])
+                        break
+                    seen.add(entry[0])
+
+        cast(0, nc.vector.tensor_copy)
+        nc.vector.transpose(out=bias[:], in_=bias_rows[:])
+        quantise_x(0)
+        dequantise(0)
+        cast(1, nc.scalar.copy)
+        quantise_x(1)
+        dequantise(1)
+        cast(2, nc.scalar.copy)
         for i in range(N_CHUNKS):
             subtract(i)
-            if i + ahead < N_CHUNKS:
-                stage_x(i + ahead, nc.scalar.copy)
-            if i >= 2 and i % 2 == 0:
-                quantise_rest([i - 2, i - 1])
-            if i == 8:
-                nc.vector.transpose(out=bias[:], in_=bias_rows[:])
-            for n in range(N_TILES):
-                if finish_at[n] == i:
-                    finish(0, n)
-            for turn in range(2 if i < 15 else 1):
-                ready = [entry for entry in passes if entry[0] <= i]
-                if ready:
-                    entry = min(ready, key=lambda e: (e[1] // 4, e[2], e[1]))
-                    passes.remove(entry)
-                    multiply(entry[1], [entry[2]])
-        quantise_rest([N_CHUNKS - 2])
-        quantise_rest([N_CHUNKS - 1])
-        passes.sort(key=lambda entry: (entry[2], entry[1]))
-        for at, stage, n in passes:
-            multiply(stage, [n])
-            if stage == 2 * n_units - 1:
-                finish(1, n, 2 if n in (0, N_TILES - 1) else 1)
+            if i + AHEAD + 1 < N_CHUNKS:
+                cast(i + AHEAD + 1, nc.scalar.copy)
+            if i <= last_cast:
+                quantise_x(i + AHEAD)
+                dequantise(i + AHEAD)
+            if 2 <= i and i % 2 == 0:
+                quantise_rest(i - 2, 2)
+            for sum_id in first_half:
+                if read_at[sum_id] == i:
+                    finish(sum_id)
+            take_passes(i, 2)
+        quantise_rest(N_CHUNKS - 2, 1)
+        quantise_rest(N_CHUNKS - 1, 1)
+        for sum_id, g, tier in waiting:
+            multiply(sum_id, g, tier)
+            if (g, tier) == (0, 1):
+                finish(sum_id, 2 if sum_id == late[0] else 1)

@@ -27,6 +27,8 @@ LINE = 2
 AHEAD = 2
 SUM_BANKS = 6
 SPLIT = 1
+PIECE = 256
+VECTOR_SHARE = 80
 READ_AT = [10, 12, 12, 13]
 EYE_ORDER = [3, 1, 0, 2]
 
@@ -46,10 +48,8 @@ def tile_mix_tierx_mix_gelu_kernel(tc, x, w8_words, w8_scales, w4_words, w4_scal
         shifted = sb("shifted", [P, (PACK - 1) * K_PASS], BF16)
         eye_codes = sb("eye_codes", [P, K_PASS], U32)
         eye_plane = sb("eye_plane", [P, K_PASS], U8)
-        bias_rows = sb("bias_rows", [P, P], F32)
-        bias = sb("bias", [P, P], F32)
-        nc.gpsimd.memset(diag[:].bitcast(I32), 0)
-        nc.vector.memset(bias_rows[:], 0.0)
+        bias = sb("bias", [P, N_TILES], F32)
+        nc.vector.memset(diag[:].bitcast(I32), 0)
         nc.vector.memset(w_planes[:].bitcast(I32), 0)
         table_warm = sb("table_warm", [P, 1], F32)
         nc.scalar.activation(
@@ -81,8 +81,8 @@ def tile_mix_tierx_mix_gelu_kernel(tc, x, w8_words, w8_scales, w4_words, w4_scal
         quantise_eye(0, 1, diag[:, 0:K_PASS])
         shift_diag(1)
         shift_diag(2)
-        quantise_eye(1, 1, shifted[:, 0:K_PASS])
         shift_diag(3)
+        quantise_eye(1, 1, shifted[:, 0:K_PASS])
         quantise_eye(2, 2, shifted[:, K_PASS:])
 
         raw = {}
@@ -102,8 +102,8 @@ def tile_mix_tierx_mix_gelu_kernel(tc, x, w8_words, w8_scales, w4_words, w4_scal
             for pos in range(count):
                 raw[first + pos] = slab[:, :, pos * CHUNK : (pos + 1) * CHUNK]
 
-        def load_plane(g, scales):
-            for r in range(4):
+        def load_plane(g, scales, rows):
+            for r in rows:
                 nc.sync.dma_start(
                     out=w_planes[r:P:32, g * N : (g + 1) * N].bitcast(I32), in_=scales[0, r:16:4, :].bitcast(I32)
                 )
@@ -112,20 +112,21 @@ def tile_mix_tierx_mix_gelu_kernel(tc, x, w8_words, w8_scales, w4_words, w4_scal
         w4 = sb("w4", [P, 2 * N], U8)
         load_x(0, 1)
         load_x(1, 1)
-        nc.sync.dma_start(
-            out=bias_rows[0:P:32, :].rearrange("q (n i) -> q n i", n=N_TILES),
-            in_=b.rearrange("(n q i) -> q n i", n=N_TILES, q=4),
-        )
         load_x(2, 1)
+        load_plane(1, w4_scales, [0, 1])
         load_x(3, 1)
-        load_x(4, 2)
+        load_plane(1, w4_scales, [2, 3])
+        load_x(4, 1)
+        load_x(5, 1)
         nc.sync.dma_start(out=w4[:].bitcast(I32), in_=w4_words[0].bitcast(I32))
-        load_plane(1, w4_scales)
-        load_x(6, 2)
+        load_x(6, 1)
+        load_x(7, 1)
         load_x(8, 2)
         nc.sync.dma_start(out=w8[:].bitcast(I32), in_=w8_words[0].rearrange("p n i -> p (n i)").bitcast(I32))
-        load_plane(0, w8_scales)
+        load_plane(0, w8_scales, range(4))
         load_x(10, 2)
+        with nc.allow_non_contiguous_dma(reason="one bias value a partition"):
+            nc.sync.dma_start(out=bias[:], in_=b.rearrange("(n p) -> p n", p=P))
         load_x(12, 2)
         load_x(14, 2)
 
@@ -225,13 +226,13 @@ def tile_mix_tierx_mix_gelu_kernel(tc, x, w8_words, w8_scales, w4_words, w4_scal
                     out=result[:],
                     in_=acc[sum_id][:, t0 - window : t0 - window + width],
                     func=GELU,
-                    bias=bias[:, 32 * n : 32 * n + 1],
+                    bias=bias[:, n : n + 1],
                     scale=1.0,
                 )
                 nc.sync.dma_start(out=out[n * P : (n + 1) * P, t0 : t0 + width], in_=result[:])
 
         warm = psum.tile([P, BANK], F32, tag="acc", bufs=SUM_BANKS, name="acc")
-        for count in [1] * 4 + [2] * 4:
+        for count in [1] * 4 + [2] * 2 + [4]:
             nc.tensor.matmul_mx(
                 out=warm[:, eye_cols(0, count)],
                 lhsT=eye_codes[:, eye_cols(0)].bitcast(E4M3),
@@ -262,26 +263,27 @@ def tile_mix_tierx_mix_gelu_kernel(tc, x, w8_words, w8_scales, w4_words, w4_scal
             reused = sums.index(sum_id) - SUM_BANKS
             return max(codes_at, read_at[sums[reused]] + 1 if reused >= 0 else 0)
 
-        def take_passes(i, count):
-            for turn in range(count):
-                seen = set()
-                for entry in waiting:
-                    opened = entry[0] in acc
-                    if ready_at(*entry) <= i and (entry[0] not in seen or (opened and entry[1:] != (0, 1))):
-                        waiting.remove(entry)
-                        multiply(*entry)
-                        if entry[0] in early and entry[1:] == (0, 1):
-                            finish(entry[0])
-                        break
-                    seen.add(entry[0])
+        def take_passes(i, columns):
+            blocked = set()
+            for entry in list(waiting):
+                sum_id, g, tier = entry
+                width = BANK if tier else sum_id[3] - sum_id[2]
+                closing = (g, tier) == (0, 1)
+                in_turn = sum_id not in blocked or (sum_id in acc and not closing)
+                if ready_at(*entry) <= i and in_turn and width <= columns:
+                    waiting.remove(entry)
+                    multiply(*entry)
+                    columns -= width
+                    if closing and sum_id in early:
+                        finish(sum_id)
+                else:
+                    blocked.add(sum_id)
 
-        cast(0, nc.vector.tensor_copy)
-        nc.vector.transpose(out=bias[:], in_=bias_rows[:])
-        quantise_x(0)
-        dequantise(0)
-        cast(1, nc.scalar.copy)
-        quantise_x(1)
-        dequantise(1)
+        for i in range(AHEAD):
+            cast(i, nc.vector.tensor_copy, 0, VECTOR_SHARE)
+            cast(i, nc.scalar.copy, VECTOR_SHARE, CHUNK)
+            quantise_x(i)
+            dequantise(i)
         cast(2, nc.scalar.copy)
         for i in range(N_CHUNKS):
             subtract(i)
@@ -295,10 +297,10 @@ def tile_mix_tierx_mix_gelu_kernel(tc, x, w8_words, w8_scales, w4_words, w4_scal
             for sum_id in first_half:
                 if read_at[sum_id] == i:
                     finish(sum_id)
-            take_passes(i, 2)
+            take_passes(i, 2 * BANK if i < N_CHUNKS - 1 else BANK)
         quantise_rest(N_CHUNKS - 2, 1)
         quantise_rest(N_CHUNKS - 1, 1)
         for sum_id, g, tier in waiting:
             multiply(sum_id, g, tier)
             if (g, tier) == (0, 1):
-                finish(sum_id, 2 if sum_id == late[0] else 1)
+                finish(sum_id, (sum_id[3] - sum_id[2]) // PIECE)

@@ -41,7 +41,7 @@ def tile_mix_tierx_mix_gelu_kernel(tc, x, w8_words, w8_scales, w4_words, w4_scal
         ctx.enter_context(tc.manual_schedule())
 
         def sb(name, shape, dtype):
-            return keep.tile(shape, dtype, name=name, align_bytes=64)
+            return keep.tile(shape, dtype, name=name, align_bytes=256)
 
         w_planes = sb("w_planes", [P, 2 * N], U8)
         diag = sb("diag", [P, K_PASS + PACK], BF16)

@@ -23,13 +23,16 @@ CHUNK = 128
 PER_UNIT = BANK // CHUNK
 N_CHUNKS = (K // K_PASS) * (T // CHUNK)
 N_TILES = N // P
-LINE = 2
+W8, W4 = 0, 1
+FIRST, REST = 0, 1
+ALIGN = 256
+PAIR = 2
 AHEAD = 2
+VALUE_BANKS = 2
 SUM_BANKS = 6
-SPLIT = 1
-PIECE = 256
+SHARED = 3
 VECTOR_SHARE = 80
-READ_AT = [10, 12, 12, 13]
+PIECE = 256
 EYE_ORDER = [3, 1, 0, 2]
 
 
@@ -41,7 +44,7 @@ def tile_mix_tierx_mix_gelu_kernel(tc, x, w8_words, w8_scales, w4_words, w4_scal
         ctx.enter_context(tc.manual_schedule())
 
         def sb(name, shape, dtype):
-            return keep.tile(shape, dtype, name=name, align_bytes=256)
+            return keep.tile(shape, dtype, name=name, align_bytes=ALIGN)
 
         w_planes = sb("w_planes", [P, 2 * N], U8)
         diag = sb("diag", [P, K_PASS + PACK], BF16)
@@ -49,15 +52,14 @@ def tile_mix_tierx_mix_gelu_kernel(tc, x, w8_words, w8_scales, w4_words, w4_scal
         eye_codes = sb("eye_codes", [P, K_PASS], U32)
         eye_plane = sb("eye_plane", [P, K_PASS], U8)
         bias = sb("bias", [P, N_TILES], F32)
+        diag_words = diag[:].bitcast(F32)
         nc.vector.memset(diag[:].bitcast(I32), 0)
         nc.vector.memset(w_planes[:].bitcast(I32), 0)
         table_warm = sb("table_warm", [P, 1], F32)
-        nc.scalar.activation(
-            out=table_warm[:], in_=diag[:].bitcast(F32)[:, 0:1], func=GELU, bias=diag[:].bitcast(F32)[:, 0:1], scale=1.0
-        )
+        nc.scalar.activation(out=table_warm[:], in_=diag_words[:, 0:1], func=GELU, bias=diag_words[:, 0:1], scale=1.0)
         nc.gpsimd.affine_select(
-            out=diag[:].bitcast(F32)[:, 1:],
-            in_=diag[:].bitcast(F32)[:, 1:],
+            out=diag_words[:, 1:],
+            in_=diag_words[:, 1:],
             compare_op=mybir.AluOpType.not_equal,
             fill=1.0,
             base=0,
@@ -65,31 +67,27 @@ def tile_mix_tierx_mix_gelu_kernel(tc, x, w8_words, w8_scales, w4_words, w4_scal
             channel_multiplier=2,
         )
 
-        def eye_cols(slot, count=1):
-            return slice(slot * P, (slot + count) * P)
+        def eye_cols(quarter, count=1):
+            return slice(quarter * P, (quarter + count) * P)
 
-        def quantise_eye(slot, count, rows):
-            cols = eye_cols(slot, count)
+        def quantise_eye(quarter, count, rows):
+            cols = eye_cols(quarter, count)
             nc.vector.quantize_mx(out=eye_codes[:, cols].bitcast(E4M3), scales=eye_plane[:, cols], in_=rows)
 
-        def shift_diag(slot):
-            shift = PACK - 1 - EYE_ORDER[slot]
-            nc.vector.tensor_copy(
-                out=shifted[:, (slot - 1) * K_PASS : slot * K_PASS], in_=diag[:, shift : shift + K_PASS]
-            )
-
         quantise_eye(0, 1, diag[:, 0:K_PASS])
-        shift_diag(1)
-        shift_diag(2)
-        shift_diag(3)
+        for quarter in range(1, PACK):
+            shift = PACK - 1 - EYE_ORDER[quarter]
+            nc.vector.tensor_copy(
+                out=shifted[:, (quarter - 1) * K_PASS : quarter * K_PASS], in_=diag[:, shift : shift + K_PASS]
+            )
         quantise_eye(1, 1, shifted[:, 0:K_PASS])
         quantise_eye(2, 2, shifted[:, K_PASS:])
 
         raw = {}
 
         def place(i):
-            unit, c = divmod(i, PER_UNIT)
-            return 1 - unit % 2, (unit // 2) * BANK + c * CHUNK
+            unit, block = divmod(i, PER_UNIT)
+            return W4 if unit % 2 == 0 else W8, (unit // 2) * BANK + block * CHUNK
 
         def load_x(first, count):
             g, t0 = place(first)
@@ -110,101 +108,109 @@ def tile_mix_tierx_mix_gelu_kernel(tc, x, w8_words, w8_scales, w4_words, w4_scal
 
         w8 = sb("w8", [P, 4 * N], U8)
         w4 = sb("w4", [P, 2 * N], U8)
+
+        def load_w8(half):
+            cols = slice(2 * N * half, 2 * N * (half + 1))
+            nc.sync.dma_start(
+                out=w8[:, cols].bitcast(I32), in_=w8_words[0].rearrange("p n i -> p (n i)")[:, cols].bitcast(I32)
+            )
+
         load_x(0, 1)
         load_x(1, 1)
         load_x(2, 1)
-        load_plane(1, w4_scales, [0, 1])
+        load_plane(W4, w4_scales, [0, 1])
         load_x(3, 1)
-        load_plane(1, w4_scales, [2, 3])
+        load_plane(W4, w4_scales, [2, 3])
         load_x(4, 1)
         load_x(5, 1)
         nc.sync.dma_start(out=w4[:].bitcast(I32), in_=w4_words[0].bitcast(I32))
         load_x(6, 1)
         load_x(7, 1)
         load_x(8, 2)
-        nc.sync.dma_start(out=w8[:].bitcast(I32), in_=w8_words[0].rearrange("p n i -> p (n i)").bitcast(I32))
-        load_plane(0, w8_scales, range(4))
+        load_w8(0)
+        load_plane(W8, w8_scales, [0, 1, 2, 3])
         load_x(10, 2)
-        with nc.allow_non_contiguous_dma(reason="one bias value a partition"):
-            nc.sync.dma_start(out=bias[:], in_=b.rearrange("(n p) -> p n", p=P))
+        load_w8(1)
         load_x(12, 2)
+        with nc.allow_non_contiguous_dma(reason="one bias value a partition and output tile"):
+            nc.sync.dma_start(out=bias[:], in_=b.rearrange("(n p) -> p n", p=P))
         load_x(14, 2)
 
-        q_codes = [sb("q_codes%d" % g, [P, T], U32) for g in range(2)]
-        q_plane = [sb("q_plane%d" % g, [P, T], U8) for g in range(2)]
-        r_codes = [sb("r_codes%d" % g, [P, T], U32) for g in range(2)]
-        r_plane = [sb("r_plane%d" % g, [P, T], U8) for g in range(2)]
+        q_codes = [sb("q_codes%d" % g, [P, T], U32) for g in (W8, W4)]
+        q_plane = [sb("q_plane%d" % g, [P, T], U8) for g in (W8, W4)]
+        r_codes = [sb("r_codes%d" % g, [P, T], U32) for g in (W8, W4)]
+        r_plane = [sb("r_plane%d" % g, [P, T], U8) for g in (W8, W4)]
+        tiers = {FIRST: (q_codes, q_plane, E4M3), REST: (r_codes, r_plane, E5M2)}
         x_bf = sb("x_bf", [P, N_CHUNKS * K_PASS], BF16)
         r_bf = sb("r_bf", [P, N_CHUNKS * K_PASS], BF16)
 
         def rows_walk(ap):
-            return ap.rearrange("p j (c i) -> p c j i", i=LINE)
+            return ap.rearrange("p j (c i) -> p c j i", i=PAIR)
 
         def words_walk(ap):
-            return ap.rearrange("p (c i j) -> p c j i", i=LINE, j=PACK)
+            return ap.rearrange("p (c i j) -> p c j i", i=PAIR, j=PACK)
+
+        def staged(tile, i, lo, hi):
+            return tile[:, i * K_PASS + lo * PACK : i * K_PASS + hi * PACK]
 
         values = {}
         acc = {}
 
         def cast(i, copy, lo=0, hi=CHUNK):
-            copy(
-                out=words_walk(x_bf[:, i * K_PASS + lo * PACK : i * K_PASS + hi * PACK]),
-                in_=rows_walk(raw[i][:, :, lo:hi]),
-            )
+            copy(out=words_walk(staged(x_bf, i, lo, hi)), in_=rows_walk(raw[i][:, :, lo:hi]))
 
-        def quantise(codes, plane, fmt, staged, first, count):
-            g, t0 = place(first)
-            cols = slice(t0, t0 + count * CHUNK)
+        def cast_shared(i):
+            cast(i, nc.vector.tensor_copy, 0, VECTOR_SHARE)
+            cast(i, nc.scalar.copy, VECTOR_SHARE, CHUNK)
+
+        def quantise(tier, i, lo, hi):
+            codes, plane, fmt = tiers[tier]
+            g, t0 = place(i)
+            cols = slice(t0 + lo, t0 + hi)
             nc.vector.quantize_mx(
                 out=codes[g][:, cols].bitcast(fmt),
                 scales=plane[g][:, cols],
-                in_=staged[:, first * K_PASS : (first + count) * K_PASS],
+                in_=staged(r_bf if tier == REST else x_bf, i, lo, hi),
             )
 
-        def quantise_x(first, count=1):
-            quantise(q_codes, q_plane, E4M3, x_bf, first, count)
-
-        def quantise_rest(first, count):
-            quantise(r_codes, r_plane, E5M2, r_bf, first, count)
-
-        def dequantise(i):
+        def first_tier(i):
+            quantise(FIRST, i, 0, CHUNK)
             g, t0 = place(i)
             cols = slice(t0, t0 + CHUNK)
-            bank = psum.tile([P, PACK, CHUNK], F32, tag="values", bufs=2, name="values")
-            for slot, j in enumerate(EYE_ORDER):
+            values[i] = psum.tile([P, PACK, CHUNK], F32, tag="values", bufs=VALUE_BANKS, name="values")
+            for quarter, j in enumerate(EYE_ORDER):
                 nc.tensor.matmul_mx(
-                    out=bank[:, j, :],
-                    lhsT=eye_codes[:, eye_cols(slot)].bitcast(E4M3),
-                    lhsT_scale=eye_plane[:, eye_cols(slot)],
+                    out=values[i][:, j, :],
+                    lhsT=eye_codes[:, eye_cols(quarter)].bitcast(E4M3),
+                    lhsT_scale=eye_plane[:, eye_cols(quarter)],
                     rhs=q_codes[g][:, cols].bitcast(E4M3),
                     rhs_scale=q_plane[g][:, cols],
                     start=True,
                     stop=True,
                 )
-            values[i] = bank
 
-        def subtract(i):
+        def subtract(i, lo=0, hi=CHUNK):
             nc.vector.tensor_tensor(
-                out=words_walk(r_bf[:, i * K_PASS : (i + 1) * K_PASS]),
-                in0=rows_walk(raw[i]),
-                in1=rows_walk(values[i][:]),
+                out=words_walk(staged(r_bf, i, lo, hi)),
+                in0=rows_walk(raw[i][:, :, lo:hi]),
+                in1=rows_walk(values[i][:, :, lo:hi]),
                 op=mybir.AluOpType.subtract,
             )
 
         def multiply(sum_id, g, tier):
             n, window, lo, hi = sum_id
-            codes, plane, fmt = (r_codes, r_plane, E5M2) if tier else (q_codes, q_plane, E4M3)
-            first = sum_id not in acc
-            if first:
+            codes, plane, fmt = tiers[tier]
+            opening = sum_id not in acc
+            if opening:
                 acc[sum_id] = psum.tile([P, BANK], F32, tag="acc", bufs=SUM_BANKS, name="acc")
-            if g == 0:
+            if g == W8:
                 weights = w8[:, 4 * P * n : 4 * P * (n + 1)].bitcast(E4M3)
             else:
                 weights = w4[:, 2 * P * n : 2 * P * (n + 1)].bitcast(E2M1)
-            if tier or hi - lo == BANK:
+            if tier == REST or hi - lo == BANK:
                 spans = [(window, window + BANK)]
             else:
-                width = CHUNK if g else hi - lo
+                width = CHUNK if g == W4 else hi - lo
                 spans = [(t0, t0 + width) for t0 in range(lo, hi, width)]
             for t0, t1 in spans:
                 nc.tensor.matmul_mx(
@@ -213,13 +219,12 @@ def tile_mix_tierx_mix_gelu_kernel(tc, x, w8_words, w8_scales, w4_words, w4_scal
                     lhsT_scale=w_planes[:, g * N + P * n : g * N + P * (n + 1)],
                     rhs=codes[g][:, t0:t1].bitcast(fmt),
                     rhs_scale=plane[g][:, t0:t1],
-                    start=first,
-                    stop=(g == 0 and tier == 1),
+                    start=opening,
+                    stop=(g, tier) == (W8, REST),
                 )
 
-        def finish(sum_id, pieces=1):
+        def finish(sum_id, width):
             n, window, lo, hi = sum_id
-            width = (hi - lo) // pieces
             for t0 in range(lo, hi, width):
                 result = sb("result%d_%d" % (n, t0), [P, width], F32)
                 nc.scalar.activation(
@@ -231,76 +236,91 @@ def tile_mix_tierx_mix_gelu_kernel(tc, x, w8_words, w8_scales, w4_words, w4_scal
                 )
                 nc.sync.dma_start(out=out[n * P : (n + 1) * P, t0 : t0 + width], in_=result[:])
 
+        cut = BANK + BANK // 2
+        last_tile = N_TILES - 1
+        first_half = [(n, 0, 0, BANK) for n in range(N_TILES)]
+        early = (last_tile, cut - BANK, BANK, cut)
+        late = [(n, BANK, BANK if n < last_tile else cut, T) for n in range(N_TILES)]
+        sums = first_half + late[:1] + [early] + late[1:]
+        waiting = []
+        for sum_id in sums:
+            whole = sum_id[3] - sum_id[2] == BANK
+            w4_tiers = [FIRST, REST] if whole else [REST, FIRST]
+            waiting.extend([(sum_id, W4, tier) for tier in w4_tiers] + [(sum_id, W8, FIRST), (sum_id, W8, REST)])
+
+        last_codes = N_CHUNKS - 1 - AHEAD
+        last_cast = last_codes - 1
+        read_at = {sum_id: last_cast - 2 if sum_id[0] == 0 else last_cast for sum_id in first_half}
+        late_w8_at = 2 * PER_UNIT - 1
+
+        def ready_at(sum_id, g, tier):
+            half, block = divmod(sum_id[3] // CHUNK - 1, PER_UNIT)
+            last_chunk = PER_UNIT * (2 * half + (1 if g == W8 else 0)) + block
+            codes_at = last_chunk + 1 if tier == REST else last_chunk - AHEAD
+            weights_at = late_w8_at if g == W8 and sum_id[0] >= N_TILES // 2 else 0
+            before = sums.index(sum_id) - SUM_BANKS
+            bank_at = read_at[sums[before]] + 1 if before >= 0 else 0
+            return max(codes_at, weights_at, bank_at)
+
+        def take_products(i, columns):
+            passed_over = set()
+            for product in list(waiting):
+                sum_id, g, tier = product
+                width = BANK if tier == REST else sum_id[3] - sum_id[2]
+                closing = (g, tier) == (W8, REST)
+                in_turn = sum_id not in passed_over or (sum_id in acc and not closing)
+                if ready_at(*product) <= i and in_turn and width <= columns:
+                    waiting.remove(product)
+                    multiply(*product)
+                    columns -= width
+                    if closing and sum_id == early:
+                        finish(early, PIECE)
+                else:
+                    passed_over.add(sum_id)
+
         warm = psum.tile([P, BANK], F32, tag="acc", bufs=SUM_BANKS, name="acc")
-        for count in [1] * 4 + [2] * 2 + [4]:
+
+        def warm_up(quarters):
             nc.tensor.matmul_mx(
-                out=warm[:, eye_cols(0, count)],
+                out=warm[:, eye_cols(0, quarters)],
                 lhsT=eye_codes[:, eye_cols(0)].bitcast(E4M3),
                 lhsT_scale=eye_plane[:, eye_cols(0)],
-                rhs=eye_codes[:, eye_cols(0, count)].bitcast(E4M3),
-                rhs_scale=eye_plane[:, eye_cols(0, count)],
+                rhs=eye_codes[:, eye_cols(0, quarters)].bitcast(E4M3),
+                rhs_scale=eye_plane[:, eye_cols(0, quarters)],
                 start=True,
                 stop=True,
             )
 
-        last_cast = N_CHUNKS - 1 - AHEAD
-        cut = BANK + BANK // 2
-        whole = N_TILES - SPLIT
-        first_half = [(n, 0, 0, BANK) for n in range(N_TILES)]
-        early = [(n, cut - BANK, BANK, cut) for n in range(whole, N_TILES)]
-        late = [(n, BANK, BANK if n < whole else cut, T) for n in range(N_TILES)]
-        sums = first_half + late[: SUM_BANKS - N_TILES - SPLIT] + early + late[SUM_BANKS - N_TILES - SPLIT :]
-        read_at = dict(zip(first_half, READ_AT))
-        waiting = []
-        for sum_id in sums:
-            order = [(1, 0), (1, 1), (0, 0), (0, 1)] if sum_id[3] - sum_id[2] == BANK else [(1, 1), (1, 0), (0, 0), (0, 1)]
-            waiting.extend((sum_id, g, tier) for g, tier in order)
-
-        def ready_at(sum_id, g, tier):
-            last_block = sum_id[3] // CHUNK - 1
-            last_chunk = 2 * PER_UNIT * (last_block // PER_UNIT) + PER_UNIT * (1 - g) + last_block % PER_UNIT
-            codes_at = last_chunk + 1 if tier else last_chunk - AHEAD
-            reused = sums.index(sum_id) - SUM_BANKS
-            return max(codes_at, read_at[sums[reused]] + 1 if reused >= 0 else 0)
-
-        def take_passes(i, columns):
-            blocked = set()
-            for entry in list(waiting):
-                sum_id, g, tier = entry
-                width = BANK if tier else sum_id[3] - sum_id[2]
-                closing = (g, tier) == (0, 1)
-                in_turn = sum_id not in blocked or (sum_id in acc and not closing)
-                if ready_at(*entry) <= i and in_turn and width <= columns:
-                    waiting.remove(entry)
-                    multiply(*entry)
-                    columns -= width
-                    if closing and sum_id in early:
-                        finish(sum_id)
-                else:
-                    blocked.add(sum_id)
+        for quarters in [1, 1, 1, 1, 2, 2, PACK]:
+            warm_up(quarters)
 
         for i in range(AHEAD):
-            cast(i, nc.vector.tensor_copy, 0, VECTOR_SHARE)
-            cast(i, nc.scalar.copy, VECTOR_SHARE, CHUNK)
-            quantise_x(i)
-            dequantise(i)
-        cast(2, nc.scalar.copy)
+            cast_shared(i)
+            first_tier(i)
+        for i in range(AHEAD, SHARED):
+            cast_shared(i)
+        warm_up(PACK)
+        last = N_CHUNKS - 1
+        halves = [(0, CHUNK // 2), (CHUNK // 2, CHUNK)]
         for i in range(N_CHUNKS):
-            subtract(i)
-            if i + AHEAD + 1 < N_CHUNKS:
-                cast(i + AHEAD + 1, nc.scalar.copy)
+            for lo, hi in halves if i == last else [(0, CHUNK)]:
+                subtract(i, lo, hi)
             if i <= last_cast:
-                quantise_x(i + AHEAD)
-                dequantise(i + AHEAD)
-            if 2 <= i and i % 2 == 0:
-                quantise_rest(i - 2, 2)
+                cast(i + AHEAD + 1, nc.scalar.copy)
+            if i <= last_codes:
+                first_tier(i + AHEAD)
+            if i == 0:
+                warm_up(PACK)
+            if i >= 2 and i % 2 == 0:
+                quantise(REST, i - 2, 0, 2 * CHUNK)
             for sum_id in first_half:
                 if read_at[sum_id] == i:
-                    finish(sum_id)
-            take_passes(i, 2 * BANK if i < N_CHUNKS - 1 else BANK)
-        quantise_rest(N_CHUNKS - 2, 1)
-        quantise_rest(N_CHUNKS - 1, 1)
+                    finish(sum_id, BANK)
+            take_products(i, BANK if i == last else 2 * BANK)
+        quantise(REST, last - 1, 0, CHUNK)
+        for lo, hi in halves:
+            quantise(REST, last, lo, hi)
         for sum_id, g, tier in waiting:
             multiply(sum_id, g, tier)
-            if (g, tier) == (0, 1):
-                finish(sum_id, (sum_id[3] - sum_id[2]) // PIECE)
+            if (g, tier) == (W8, REST):
+                finish(sum_id, PIECE)

@@ -299,7 +299,6 @@ def tile_mix_tierx_mix_gelu_kernel(tc, x, w8_words, w8_scales, w4_words, w4_scal
             first_tier(i)
         for i in range(AHEAD, SHARED):
             cast_shared(i)
-        warm_up(PACK)
         last = N_CHUNKS - 1
         halves = [(0, CHUNK // 2), (CHUNK // 2, CHUNK)]
         for i in range(N_CHUNKS):
@@ -309,8 +308,6 @@ def tile_mix_tierx_mix_gelu_kernel(tc, x, w8_words, w8_scales, w4_words, w4_scal
                 cast(i + AHEAD + 1, nc.scalar.copy)
             if i <= last_codes:
                 first_tier(i + AHEAD)
-            if i == 0:
-                warm_up(PACK)
             if i >= 2 and i % 2 == 0:
                 quantise(REST, i - 2, 0, 2 * CHUNK)
             for sum_id in first_half:

@@ -16,6 +16,7 @@ E2M1 = mybir.dt.float4_e2m1fn_x4
 GELU = mybir.ActivationFunctionType.Gelu_apprx_tanh
 
 P = 128
+QUAD = 32
 PACK = 4
 K_PASS = P * PACK
 BANK = 512
@@ -26,14 +27,16 @@ N_TILES = N // P
 W8, W4 = 0, 1
 FIRST, REST = 0, 1
 ALIGN = 256
-PAIR = 2
+WALK = 2
 AHEAD = 2
 VALUE_BANKS = 2
 SUM_BANKS = 6
-SHARED = 3
 VECTOR_SHARE = 80
 PIECE = 256
 EYE_ORDER = [3, 1, 0, 2]
+W4_STEP = 1
+W8_STEPS = [5, 6]
+GELU_STEPS = [9, 12, 12, 12]
 
 
 def tile_mix_tierx_mix_gelu_kernel(tc, x, w8_words, w8_scales, w4_words, w4_scales, b, out):
@@ -46,14 +49,16 @@ def tile_mix_tierx_mix_gelu_kernel(tc, x, w8_words, w8_scales, w4_words, w4_scal
         def sb(name, shape, dtype):
             return keep.tile(shape, dtype, name=name, align_bytes=ALIGN)
 
-        w_planes = sb("w_planes", [P, 2 * N], U8)
         diag = sb("diag", [P, K_PASS + PACK], BF16)
         shifted = sb("shifted", [P, (PACK - 1) * K_PASS], BF16)
         eye_codes = sb("eye_codes", [P, K_PASS], U32)
         eye_plane = sb("eye_plane", [P, K_PASS], U8)
-        bias = sb("bias", [P, N_TILES], F32)
+        w_planes = sb("w_planes", [P, 2 * N], U8)
+        bias_rows = sb("bias_rows", [P, N_TILES * QUAD], F32)
+        bias = sb("bias", [P, N_TILES * QUAD], F32)
         diag_words = diag[:].bitcast(F32)
         nc.vector.memset(diag[:].bitcast(I32), 0)
+        nc.vector.memset(bias_rows[:].bitcast(I32), 0)
         nc.vector.memset(w_planes[:].bitcast(I32), 0)
         table_warm = sb("table_warm", [P, 1], F32)
         nc.scalar.activation(out=table_warm[:], in_=diag_words[:, 0:1], func=GELU, bias=diag_words[:, 0:1], scale=1.0)
@@ -84,6 +89,8 @@ def tile_mix_tierx_mix_gelu_kernel(tc, x, w8_words, w8_scales, w4_words, w4_scal
         quantise_eye(2, 2, shifted[:, K_PASS:])
 
         raw = {}
+        w8 = sb("w8", [P, 4 * N], U8)
+        w4 = sb("w4", [P, 2 * N], U8)
 
         def place(i):
             unit, block = divmod(i, PER_UNIT)
@@ -100,14 +107,20 @@ def tile_mix_tierx_mix_gelu_kernel(tc, x, w8_words, w8_scales, w4_words, w4_scal
             for pos in range(count):
                 raw[first + pos] = slab[:, :, pos * CHUNK : (pos + 1) * CHUNK]
 
-        def load_plane(g, scales, rows):
-            for r in rows:
+        def load_bias():
+            nc.sync.dma_start(
+                out=bias_rows[0:P:QUAD, :].rearrange("q (n c) -> q n c", c=QUAD),
+                in_=b.rearrange("(n q c) -> q n c", q=P // QUAD, c=QUAD),
+            )
+
+        def load_plane(g, scales):
+            for r in range(4):
                 nc.sync.dma_start(
-                    out=w_planes[r:P:32, g * N : (g + 1) * N].bitcast(I32), in_=scales[0, r:16:4, :].bitcast(I32)
+                    out=w_planes[r:P:QUAD, g * N : (g + 1) * N].bitcast(I32), in_=scales[0, r:16:4, :].bitcast(I32)
                 )
 
-        w8 = sb("w8", [P, 4 * N], U8)
-        w4 = sb("w4", [P, 2 * N], U8)
+        def load_w4():
+            nc.sync.dma_start(out=w4[:].bitcast(I32), in_=w4_words[0].bitcast(I32))
 
         def load_w8(half):
             cols = slice(2 * N * half, 2 * N * (half + 1))
@@ -115,25 +128,19 @@ def tile_mix_tierx_mix_gelu_kernel(tc, x, w8_words, w8_scales, w4_words, w4_scal
                 out=w8[:, cols].bitcast(I32), in_=w8_words[0].rearrange("p n i -> p (n i)")[:, cols].bitcast(I32)
             )
 
-        load_x(0, 1)
-        load_x(1, 1)
-        load_x(2, 1)
-        load_plane(W4, w4_scales, [0, 1])
-        load_x(3, 1)
-        load_plane(W4, w4_scales, [2, 3])
-        load_x(4, 1)
-        load_x(5, 1)
-        nc.sync.dma_start(out=w4[:].bitcast(I32), in_=w4_words[0].bitcast(I32))
-        load_x(6, 1)
-        load_x(7, 1)
-        load_x(8, 2)
+        load_x(0, 2)
+        load_bias()
+        load_x(2, 2)
+        load_w4()
+        load_x(4, 2)
+        load_plane(W4, w4_scales)
+        load_x(6, 2)
         load_w8(0)
-        load_plane(W8, w8_scales, [0, 1, 2, 3])
-        load_x(10, 2)
+        load_x(8, 2)
+        load_plane(W8, w8_scales)
         load_w8(1)
+        load_x(10, 2)
         load_x(12, 2)
-        with nc.allow_non_contiguous_dma(reason="one bias value a partition and output tile"):
-            nc.sync.dma_start(out=bias[:], in_=b.rearrange("(n p) -> p n", p=P))
         load_x(14, 2)
 
         q_codes = [sb("q_codes%d" % g, [P, T], U32) for g in (W8, W4)]
@@ -145,23 +152,20 @@ def tile_mix_tierx_mix_gelu_kernel(tc, x, w8_words, w8_scales, w4_words, w4_scal
         r_bf = sb("r_bf", [P, N_CHUNKS * K_PASS], BF16)
 
         def rows_walk(ap):
-            return ap.rearrange("p j (c i) -> p c j i", i=PAIR)
+            return ap.rearrange("p j (c i) -> p c j i", i=WALK)
 
         def words_walk(ap):
-            return ap.rearrange("p (c i j) -> p c j i", i=PAIR, j=PACK)
+            return ap.rearrange("p (c i j) -> p c j i", i=WALK, j=PACK)
 
         def staged(tile, i, lo, hi):
             return tile[:, i * K_PASS + lo * PACK : i * K_PASS + hi * PACK]
 
         values = {}
         acc = {}
+        coded = {(g, tier): 0 for g in (W8, W4) for tier in (FIRST, REST)}
 
         def cast(i, copy, lo=0, hi=CHUNK):
             copy(out=words_walk(staged(x_bf, i, lo, hi)), in_=rows_walk(raw[i][:, :, lo:hi]))
-
-        def cast_shared(i):
-            cast(i, nc.vector.tensor_copy, 0, VECTOR_SHARE)
-            cast(i, nc.scalar.copy, VECTOR_SHARE, CHUNK)
 
         def quantise(tier, i, lo, hi):
             codes, plane, fmt = tiers[tier]
@@ -172,6 +176,7 @@ def tile_mix_tierx_mix_gelu_kernel(tc, x, w8_words, w8_scales, w4_words, w4_scal
                 scales=plane[g][:, cols],
                 in_=staged(r_bf if tier == REST else x_bf, i, lo, hi),
             )
+            coded[(g, tier)] = t0 + hi
 
         def first_tier(i):
             quantise(FIRST, i, 0, CHUNK)
@@ -223,6 +228,8 @@ def tile_mix_tierx_mix_gelu_kernel(tc, x, w8_words, w8_scales, w4_words, w4_scal
                     stop=(g, tier) == (W8, REST),
                 )
 
+        stored = set()
+
         def finish(sum_id, width):
             n, window, lo, hi = sum_id
             for t0 in range(lo, hi, width):
@@ -231,10 +238,11 @@ def tile_mix_tierx_mix_gelu_kernel(tc, x, w8_words, w8_scales, w4_words, w4_scal
                     out=result[:],
                     in_=acc[sum_id][:, t0 - window : t0 - window + width],
                     func=GELU,
-                    bias=bias[:, n : n + 1],
+                    bias=bias[:, QUAD * n : QUAD * n + 1],
                     scale=1.0,
                 )
                 nc.sync.dma_start(out=out[n * P : (n + 1) * P, t0 : t0 + width], in_=result[:])
+            stored.add(sum_id)
 
         cut = BANK + BANK // 2
         last_tile = N_TILES - 1
@@ -248,28 +256,19 @@ def tile_mix_tierx_mix_gelu_kernel(tc, x, w8_words, w8_scales, w4_words, w4_scal
             w4_tiers = [FIRST, REST] if whole else [REST, FIRST]
             waiting.extend([(sum_id, W4, tier) for tier in w4_tiers] + [(sum_id, W8, FIRST), (sum_id, W8, REST)])
 
-        last_codes = N_CHUNKS - 1 - AHEAD
-        last_cast = last_codes - 1
-        read_at = {sum_id: last_cast - 2 if sum_id[0] == 0 else last_cast for sum_id in first_half}
-        late_w8_at = 2 * PER_UNIT - 1
-
-        def ready_at(sum_id, g, tier):
-            half, block = divmod(sum_id[3] // CHUNK - 1, PER_UNIT)
-            last_chunk = PER_UNIT * (2 * half + (1 if g == W8 else 0)) + block
-            codes_at = last_chunk + 1 if tier == REST else last_chunk - AHEAD
-            weights_at = late_w8_at if g == W8 and sum_id[0] >= N_TILES // 2 else 0
+        def ready(i, freed, sum_id, g, tier):
             before = sums.index(sum_id) - SUM_BANKS
-            bank_at = read_at[sums[before]] + 1 if before >= 0 else 0
-            return max(codes_at, weights_at, bank_at)
+            weights_at = W4_STEP if g == W4 else W8_STEPS[sum_id[0] // 2]
+            return coded[(g, tier)] >= sum_id[3] and i >= weights_at and (before < 0 or sums[before] in freed)
 
-        def take_products(i, columns):
+        def take_products(i, freed, columns):
             passed_over = set()
             for product in list(waiting):
                 sum_id, g, tier = product
                 width = BANK if tier == REST else sum_id[3] - sum_id[2]
                 closing = (g, tier) == (W8, REST)
                 in_turn = sum_id not in passed_over or (sum_id in acc and not closing)
-                if ready_at(*product) <= i and in_turn and width <= columns:
+                if ready(i, freed, *product) and in_turn and width <= columns:
                     waiting.remove(product)
                     multiply(*product)
                     columns -= width
@@ -279,8 +278,7 @@ def tile_mix_tierx_mix_gelu_kernel(tc, x, w8_words, w8_scales, w4_words, w4_scal
                     passed_over.add(sum_id)
 
         warm = psum.tile([P, BANK], F32, tag="acc", bufs=SUM_BANKS, name="acc")
-
-        def warm_up(quarters):
+        for quarters in [1, 1, 1, 1, 2, 2, PACK]:
             nc.tensor.matmul_mx(
                 out=warm[:, eye_cols(0, quarters)],
                 lhsT=eye_codes[:, eye_cols(0)].bitcast(E4M3),
@@ -291,29 +289,29 @@ def tile_mix_tierx_mix_gelu_kernel(tc, x, w8_words, w8_scales, w4_words, w4_scal
                 stop=True,
             )
 
-        for quarters in [1, 1, 1, 1, 2, 2, PACK]:
-            warm_up(quarters)
-
         for i in range(AHEAD):
-            cast_shared(i)
+            cast(i, nc.vector.tensor_copy, 0, VECTOR_SHARE)
+            cast(i, nc.scalar.copy, VECTOR_SHARE, CHUNK)
+        for i in range(AHEAD):
             first_tier(i)
-        for i in range(AHEAD, SHARED):
-            cast_shared(i)
+        nc.vector.transpose(out=bias[:], in_=bias_rows[:])
+        cast(AHEAD, nc.scalar.copy)
         last = N_CHUNKS - 1
         halves = [(0, CHUNK // 2), (CHUNK // 2, CHUNK)]
         for i in range(N_CHUNKS):
+            freed = set(stored)
             for lo, hi in halves if i == last else [(0, CHUNK)]:
                 subtract(i, lo, hi)
-            if i <= last_cast:
+            if i + AHEAD + 1 <= last:
                 cast(i + AHEAD + 1, nc.scalar.copy)
-            if i <= last_codes:
+            if i + AHEAD <= last:
                 first_tier(i + AHEAD)
-            if i >= 2 and i % 2 == 0:
+            if i % 2 == 0 and i >= 2:
                 quantise(REST, i - 2, 0, 2 * CHUNK)
             for sum_id in first_half:
-                if read_at[sum_id] == i:
+                if GELU_STEPS[sum_id[0]] == i:
                     finish(sum_id, BANK)
-            take_products(i, BANK if i == last else 2 * BANK)
+            take_products(i, freed, BANK if i == last else 2 * BANK)
         quantise(REST, last - 1, 0, CHUNK)
         for lo, hi in halves:
             quantise(REST, last, lo, hi)

@@ -36,7 +36,8 @@ PIECE = 256
 EYE_ORDER = [3, 1, 0, 2]
 W4_STEP = 1
 W8_STEPS = [5, 6]
-GELU_STEPS = [9, 12, 12, 12]
+SPLIT = 1
+GELU_STEPS = [10, 12, 12, 12]
 
 
 def tile_mix_tierx_mix_gelu_kernel(tc, x, w8_words, w8_scales, w4_words, w4_scales, b, out):
@@ -54,11 +55,9 @@ def tile_mix_tierx_mix_gelu_kernel(tc, x, w8_words, w8_scales, w4_words, w4_scal
         eye_codes = sb("eye_codes", [P, K_PASS], U32)
         eye_plane = sb("eye_plane", [P, K_PASS], U8)
         w_planes = sb("w_planes", [P, 2 * N], U8)
-        bias_rows = sb("bias_rows", [P, N_TILES * QUAD], F32)
-        bias = sb("bias", [P, N_TILES * QUAD], F32)
+        bias = sb("bias", [P, N_TILES], F32)
         diag_words = diag[:].bitcast(F32)
         nc.vector.memset(diag[:].bitcast(I32), 0)
-        nc.vector.memset(bias_rows[:].bitcast(I32), 0)
         nc.vector.memset(w_planes[:].bitcast(I32), 0)
         table_warm = sb("table_warm", [P, 1], F32)
         nc.scalar.activation(out=table_warm[:], in_=diag_words[:, 0:1], func=GELU, bias=diag_words[:, 0:1], scale=1.0)
@@ -108,13 +107,11 @@ def tile_mix_tierx_mix_gelu_kernel(tc, x, w8_words, w8_scales, w4_words, w4_scal
                 raw[first + pos] = slab[:, :, pos * CHUNK : (pos + 1) * CHUNK]
 
         def load_bias():
-            nc.sync.dma_start(
-                out=bias_rows[0:P:QUAD, :].rearrange("q (n c) -> q n c", c=QUAD),
-                in_=b.rearrange("(n q c) -> q n c", q=P // QUAD, c=QUAD),
-            )
+            with nc.allow_non_contiguous_dma(reason="one bias value a partition and output tile"):
+                nc.sync.dma_start(out=bias[:], in_=b.rearrange("(n p) -> p n", p=P))
 
-        def load_plane(g, scales):
-            for r in range(4):
+        def load_plane(g, scales, rows):
+            for r in rows:
                 nc.sync.dma_start(
                     out=w_planes[r:P:QUAD, g * N : (g + 1) * N].bitcast(I32), in_=scales[0, r:16:4, :].bitcast(I32)
                 )
@@ -128,19 +125,24 @@ def tile_mix_tierx_mix_gelu_kernel(tc, x, w8_words, w8_scales, w4_words, w4_scal
                 out=w8[:, cols].bitcast(I32), in_=w8_words[0].rearrange("p n i -> p (n i)")[:, cols].bitcast(I32)
             )
 
-        load_x(0, 2)
-        load_bias()
-        load_x(2, 2)
+        load_x(0, 1)
+        load_x(1, 1)
+        load_x(2, 1)
+        load_plane(W4, w4_scales, [0, 1])
+        load_x(3, 1)
+        load_plane(W4, w4_scales, [2, 3])
+        load_x(4, 1)
+        load_x(5, 1)
         load_w4()
-        load_x(4, 2)
-        load_plane(W4, w4_scales)
-        load_x(6, 2)
-        load_w8(0)
+        load_x(6, 1)
+        load_x(7, 1)
         load_x(8, 2)
-        load_plane(W8, w8_scales)
+        load_w8(0)
+        load_plane(W8, w8_scales, [0, 1, 2, 3])
         load_w8(1)
         load_x(10, 2)
         load_x(12, 2)
+        load_bias()
         load_x(14, 2)
 
         q_codes = [sb("q_codes%d" % g, [P, T], U32) for g in (W8, W4)]
@@ -202,8 +204,8 @@ def tile_mix_tierx_mix_gelu_kernel(tc, x, w8_words, w8_scales, w4_words, w4_scal
                 op=mybir.AluOpType.subtract,
             )
 
-        def multiply(sum_id, g, tier):
-            n, window, lo, hi = sum_id
+        def multiply(sum_id, g, tier, t0, t1):
+            n, window = sum_id[:2]
             codes, plane, fmt = tiers[tier]
             opening = sum_id not in acc
             if opening:
@@ -212,21 +214,15 @@ def tile_mix_tierx_mix_gelu_kernel(tc, x, w8_words, w8_scales, w4_words, w4_scal
                 weights = w8[:, 4 * P * n : 4 * P * (n + 1)].bitcast(E4M3)
             else:
                 weights = w4[:, 2 * P * n : 2 * P * (n + 1)].bitcast(E2M1)
-            if tier == REST or hi - lo == BANK:
-                spans = [(window, window + BANK)]
-            else:
-                width = CHUNK if g == W4 else hi - lo
-                spans = [(t0, t0 + width) for t0 in range(lo, hi, width)]
-            for t0, t1 in spans:
-                nc.tensor.matmul_mx(
-                    out=acc[sum_id][:, t0 - window : t1 - window],
-                    lhsT=weights,
-                    lhsT_scale=w_planes[:, g * N + P * n : g * N + P * (n + 1)],
-                    rhs=codes[g][:, t0:t1].bitcast(fmt),
-                    rhs_scale=plane[g][:, t0:t1],
-                    start=opening,
-                    stop=(g, tier) == (W8, REST),
-                )
+            nc.tensor.matmul_mx(
+                out=acc[sum_id][:, t0 - window : t1 - window],
+                lhsT=weights,
+                lhsT_scale=w_planes[:, g * N + P * n : g * N + P * (n + 1)],
+                rhs=codes[g][:, t0:t1].bitcast(fmt),
+                rhs_scale=plane[g][:, t0:t1],
+                start=opening,
+                stop=(g, tier) == (W8, REST),
+            )
 
         stored = set()
 
@@ -238,44 +234,52 @@ def tile_mix_tierx_mix_gelu_kernel(tc, x, w8_words, w8_scales, w4_words, w4_scal
                     out=result[:],
                     in_=acc[sum_id][:, t0 - window : t0 - window + width],
                     func=GELU,
-                    bias=bias[:, QUAD * n : QUAD * n + 1],
+                    bias=bias[:, n : n + 1],
                     scale=1.0,
                 )
                 nc.sync.dma_start(out=out[n * P : (n + 1) * P, t0 : t0 + width], in_=result[:])
             stored.add(sum_id)
 
         cut = BANK + BANK // 2
-        last_tile = N_TILES - 1
+        whole_tiles = N_TILES - SPLIT
         first_half = [(n, 0, 0, BANK) for n in range(N_TILES)]
-        early = (last_tile, cut - BANK, BANK, cut)
-        late = [(n, BANK, BANK if n < last_tile else cut, T) for n in range(N_TILES)]
-        sums = first_half + late[:1] + [early] + late[1:]
-        waiting = []
-        for sum_id in sums:
-            whole = sum_id[3] - sum_id[2] == BANK
-            w4_tiers = [FIRST, REST] if whole else [REST, FIRST]
-            waiting.extend([(sum_id, W4, tier) for tier in w4_tiers] + [(sum_id, W8, FIRST), (sum_id, W8, REST)])
+        early = [(n, cut - BANK, BANK, cut) for n in range(whole_tiles, N_TILES)]
+        late = [(n, BANK, BANK if n < whole_tiles else cut, T) for n in range(N_TILES)]
+        sums = first_half + late[:1] + early + late[1:]
+        reached = {(sum_id, g, tier): sum_id[2] for sum_id in sums for g in (W8, W4) for tier in (FIRST, REST)}
 
-        def ready(i, freed, sum_id, g, tier):
-            before = sums.index(sum_id) - SUM_BANKS
-            weights_at = W4_STEP if g == W4 else W8_STEPS[sum_id[0] // 2]
-            return coded[(g, tier)] >= sum_id[3] and i >= weights_at and (before < 0 or sums[before] in freed)
+        def next_pass(sum_id, g, tier, narrow):
+            n, window, lo, hi = sum_id
+            t0 = reached[(sum_id, g, tier)]
+            ready = min(coded[(g, tier)], hi) - t0
+            whole = hi - lo == BANK
+            if tier == REST:
+                before = [(W4, FIRST), (W4, REST), (W8, FIRST)] if g == W8 else [(W4, FIRST)] if whole else []
+                waits = ready < hi - lo or any(reached[(sum_id, *other)] < hi for other in before)
+                return None if waits else (window, window + BANK)
+            if ready <= 0 or (not whole and sum_id not in acc) or (ready < hi - t0 and not narrow):
+                return None
+            widths = [BANK, CHUNK] if g == W4 else [BANK, 2 * CHUNK, CHUNK]
+            return t0, t0 + [width for width in widths if width <= ready][0]
 
-        def take_products(i, freed, columns):
-            passed_over = set()
-            for product in list(waiting):
-                sum_id, g, tier = product
-                width = BANK if tier == REST else sum_id[3] - sum_id[2]
-                closing = (g, tier) == (W8, REST)
-                in_turn = sum_id not in passed_over or (sum_id in acc and not closing)
-                if ready(i, freed, *product) and in_turn and width <= columns:
-                    waiting.remove(product)
-                    multiply(*product)
-                    columns -= width
-                    if closing and sum_id == early:
-                        finish(early, PIECE)
-                else:
-                    passed_over.add(sum_id)
+        def take_passes(i, freed, columns, only=None):
+            for narrow in (False, True):
+                for number, sum_id in enumerate(sums):
+                    if number >= SUM_BANKS and sums[number - SUM_BANKS] not in freed:
+                        break
+                    if only not in (None, sum_id):
+                        continue
+                    for g, tier in [(W4, FIRST), (W4, REST), (W4, FIRST), (W8, FIRST), (W8, REST)]:
+                        if i < (W4_STEP if g == W4 else W8_STEPS[sum_id[0] // 2]):
+                            continue
+                        span = next_pass(sum_id, g, tier, narrow)
+                        while span and span[1] - span[0] <= columns:
+                            multiply(sum_id, g, tier, *span)
+                            columns -= span[1] - span[0]
+                            reached[(sum_id, g, tier)] = sum_id[3] if tier == REST else span[1]
+                            if (g, tier) == (W8, REST) and sum_id not in first_half:
+                                finish(sum_id, PIECE)
+                            span = next_pass(sum_id, g, tier, narrow)
 
         warm = psum.tile([P, BANK], F32, tag="acc", bufs=SUM_BANKS, name="acc")
         for quarters in [1, 1, 1, 1, 2, 2, PACK]:
@@ -289,13 +293,15 @@ def tile_mix_tierx_mix_gelu_kernel(tc, x, w8_words, w8_scales, w4_words, w4_scal
                 stop=True,
             )
 
-        for i in range(AHEAD):
+        def cast_shared(i):
             cast(i, nc.vector.tensor_copy, 0, VECTOR_SHARE)
             cast(i, nc.scalar.copy, VECTOR_SHARE, CHUNK)
-        for i in range(AHEAD):
-            first_tier(i)
-        nc.vector.transpose(out=bias[:], in_=bias_rows[:])
-        cast(AHEAD, nc.scalar.copy)
+
+        cast_shared(0)
+        first_tier(0)
+        cast_shared(1)
+        first_tier(1)
+        cast_shared(2)
         last = N_CHUNKS - 1
         halves = [(0, CHUNK // 2), (CHUNK // 2, CHUNK)]
         for i in range(N_CHUNKS):
@@ -306,16 +312,15 @@ def tile_mix_tierx_mix_gelu_kernel(tc, x, w8_words, w8_scales, w4_words, w4_scal
                 cast(i + AHEAD + 1, nc.scalar.copy)
             if i + AHEAD <= last:
                 first_tier(i + AHEAD)
-            if i % 2 == 0 and i >= 2:
-                quantise(REST, i - 2, 0, 2 * CHUNK)
+            if i % 2 == 1 and i < last:
+                quantise(REST, i - 1, 0, CHUNK)
+                quantise(REST, i, 0, CHUNK)
             for sum_id in first_half:
                 if GELU_STEPS[sum_id[0]] == i:
                     finish(sum_id, BANK)
-            take_products(i, freed, BANK if i == last else 2 * BANK)
+            take_passes(i, freed, BANK if i % PER_UNIT == 0 or i == last else 2 * BANK)
         quantise(REST, last - 1, 0, CHUNK)
         for lo, hi in halves:
             quantise(REST, last, lo, hi)
-        for sum_id, g, tier in waiting:
-            multiply(sum_id, g, tier)
-            if (g, tier) == (W8, REST):
-                finish(sum_id, PIECE)
+        for sum_id in late:
+            take_passes(last, stored, 4 * BANK, sum_id)

@@ -31,13 +31,13 @@ WALK = 2
 AHEAD = 2
 VALUE_BANKS = 2
 SUM_BANKS = 6
-VECTOR_SHARE = 80
 PIECE = 256
 EYE_ORDER = [3, 1, 0, 2]
 W4_STEP = 1
 W8_STEPS = [5, 6]
 SPLIT = 1
-GELU_STEPS = [10, 12, 12, 12]
+STEP_COLUMNS = [1024, 1024, 1024, 1024, 1024, 1024, 1024, 1024, 512, 1024, 1024, 1024, 512, 1024, 1024, 512]
+GELU_STEPS = [9, 11, 12, 12]
 
 
 def tile_mix_tierx_mix_gelu_kernel(tc, x, w8_words, w8_scales, w4_words, w4_scales, b, out):
@@ -85,7 +85,6 @@ def tile_mix_tierx_mix_gelu_kernel(tc, x, w8_words, w8_scales, w4_words, w4_scal
                 out=shifted[:, (quarter - 1) * K_PASS : quarter * K_PASS], in_=diag[:, shift : shift + K_PASS]
             )
         quantise_eye(1, 1, shifted[:, 0:K_PASS])
-        quantise_eye(2, 2, shifted[:, K_PASS:])
 
         raw = {}
         w8 = sb("w8", [P, 4 * N], U8)
@@ -257,13 +256,15 @@ def tile_mix_tierx_mix_gelu_kernel(tc, x, w8_words, w8_scales, w4_words, w4_scal
                 before = [(W4, FIRST), (W4, REST), (W8, FIRST)] if g == W8 else [(W4, FIRST)] if whole else []
                 waits = ready < hi - lo or any(reached[(sum_id, *other)] < hi for other in before)
                 return None if waits else (window, window + BANK)
+            if g == W8:
+                ready = min(ready, reached[(sum_id, W4, FIRST)] - t0)
             if ready <= 0 or (not whole and sum_id not in acc) or (ready < hi - t0 and not narrow):
                 return None
             widths = [BANK, CHUNK] if g == W4 else [BANK, 2 * CHUNK, CHUNK]
             return t0, t0 + [width for width in widths if width <= ready][0]
 
         def take_passes(i, freed, columns, only=None):
-            for narrow in (False, True):
+            for narrow in (False,):
                 for number, sum_id in enumerate(sums):
                     if number >= SUM_BANKS and sums[number - SUM_BANKS] not in freed:
                         break
@@ -280,9 +281,10 @@ def tile_mix_tierx_mix_gelu_kernel(tc, x, w8_words, w8_scales, w4_words, w4_scal
                             if (g, tier) == (W8, REST) and sum_id not in first_half:
                                 finish(sum_id, PIECE)
                             span = next_pass(sum_id, g, tier, narrow)
+            return columns
 
         warm = psum.tile([P, BANK], F32, tag="acc", bufs=SUM_BANKS, name="acc")
-        for quarters in [1, 1, 1, 1, 2, 2, PACK]:
+        for quarters in [1, 1, 1, 1, 2, 2, 2, 2]:
             nc.tensor.matmul_mx(
                 out=warm[:, eye_cols(0, quarters)],
                 lhsT=eye_codes[:, eye_cols(0)].bitcast(E4M3),
@@ -293,32 +295,36 @@ def tile_mix_tierx_mix_gelu_kernel(tc, x, w8_words, w8_scales, w4_words, w4_scal
                 stop=True,
             )
 
-        def cast_shared(i):
-            cast(i, nc.vector.tensor_copy, 0, VECTOR_SHARE)
-            cast(i, nc.scalar.copy, VECTOR_SHARE, CHUNK)
+        def cast_shared(i, share):
+            cast(i, nc.vector.tensor_copy, 0, share)
+            cast(i, nc.scalar.copy, share, CHUNK)
 
-        cast_shared(0)
+        cast_shared(0, 80)
+        quantise_eye(2, 2, shifted[:, K_PASS:])
         first_tier(0)
-        cast_shared(1)
+        cast_shared(1, 64)
         first_tier(1)
-        cast_shared(2)
+        cast_shared(2, 48)
         last = N_CHUNKS - 1
         halves = [(0, CHUNK // 2), (CHUNK // 2, CHUNK)]
+        spare = 0
         for i in range(N_CHUNKS):
             freed = set(stored)
             for lo, hi in halves if i == last else [(0, CHUNK)]:
                 subtract(i, lo, hi)
             if i + AHEAD + 1 <= last:
                 cast(i + AHEAD + 1, nc.scalar.copy)
+            if i == 1:
+                quantise(REST, 0, 0, CHUNK)
             if i + AHEAD <= last:
                 first_tier(i + AHEAD)
             if i % 2 == 1 and i < last:
-                quantise(REST, i - 1, 0, CHUNK)
-                quantise(REST, i, 0, CHUNK)
+                for chunk in range(max(i - 1, 1), i + 1):
+                    quantise(REST, chunk, 0, CHUNK)
             for sum_id in first_half:
                 if GELU_STEPS[sum_id[0]] == i:
                     finish(sum_id, BANK)
-            take_passes(i, freed, BANK if i % PER_UNIT == 0 or i == last else 2 * BANK)
+            spare = take_passes(i, freed, STEP_COLUMNS[i] + spare) % BANK
         quantise(REST, last - 1, 0, CHUNK)
         for lo, hi in halves:
             quantise(REST, last, lo, hi)

@@ -26,17 +26,17 @@ N_CHUNKS = (K // K_PASS) * (T // CHUNK)
 N_TILES = N // P
 W8, W4 = 0, 1
 FIRST, REST = 0, 1
-ALIGN = 256
+ALIGN = 2048
 WALK = 2
 AHEAD = 2
 VALUE_BANKS = 2
 SUM_BANKS = 6
+VECTOR_SHARES = [80, 64, 48]
 PIECE = 256
 EYE_ORDER = [3, 1, 0, 2]
 W4_STEP = 1
 W8_STEPS = [5, 6]
 SPLIT = 1
-STEP_COLUMNS = [1024, 1024, 1024, 1024, 1024, 1024, 1024, 1024, 512, 1024, 1024, 1024, 512, 1024, 1024, 512]
 GELU_STEPS = [9, 11, 12, 12]
 
 
@@ -247,40 +247,37 @@ def tile_mix_tierx_mix_gelu_kernel(tc, x, w8_words, w8_scales, w4_words, w4_scal
         sums = first_half + late[:1] + early + late[1:]
         reached = {(sum_id, g, tier): sum_id[2] for sum_id in sums for g in (W8, W4) for tier in (FIRST, REST)}
 
-        def next_pass(sum_id, g, tier, narrow):
+        def next_pass(sum_id, g, tier):
             n, window, lo, hi = sum_id
             t0 = reached[(sum_id, g, tier)]
-            ready = min(coded[(g, tier)], hi) - t0
             whole = hi - lo == BANK
+            if t0 == hi or coded[(g, tier)] < hi:
+                return None
             if tier == REST:
                 before = [(W4, FIRST), (W4, REST), (W8, FIRST)] if g == W8 else [(W4, FIRST)] if whole else []
-                waits = ready < hi - lo or any(reached[(sum_id, *other)] < hi for other in before)
+                waits = any(reached[(sum_id, *other)] < hi for other in before)
                 return None if waits else (window, window + BANK)
-            if g == W8:
-                ready = min(ready, reached[(sum_id, W4, FIRST)] - t0)
-            if ready <= 0 or (not whole and sum_id not in acc) or (ready < hi - t0 and not narrow):
+            if (g == W8 and reached[(sum_id, W4, FIRST)] < hi) or (not whole and sum_id not in acc):
                 return None
-            widths = [BANK, CHUNK] if g == W4 else [BANK, 2 * CHUNK, CHUNK]
-            return t0, t0 + [width for width in widths if width <= ready][0]
+            return t0, (hi if whole or g == W8 else t0 + CHUNK)
 
         def take_passes(i, freed, columns, only=None):
-            for narrow in (False,):
-                for number, sum_id in enumerate(sums):
-                    if number >= SUM_BANKS and sums[number - SUM_BANKS] not in freed:
-                        break
-                    if only not in (None, sum_id):
+            for number, sum_id in enumerate(sums):
+                if number >= SUM_BANKS and sums[number - SUM_BANKS] not in freed:
+                    break
+                if only not in (None, sum_id):
+                    continue
+                for g, tier in [(W4, FIRST), (W4, REST), (W4, FIRST), (W8, FIRST), (W8, REST)]:
+                    if i < (W4_STEP if g == W4 else W8_STEPS[sum_id[0] // 2]):
                         continue
-                    for g, tier in [(W4, FIRST), (W4, REST), (W4, FIRST), (W8, FIRST), (W8, REST)]:
-                        if i < (W4_STEP if g == W4 else W8_STEPS[sum_id[0] // 2]):
-                            continue
-                        span = next_pass(sum_id, g, tier, narrow)
-                        while span and span[1] - span[0] <= columns:
-                            multiply(sum_id, g, tier, *span)
-                            columns -= span[1] - span[0]
-                            reached[(sum_id, g, tier)] = sum_id[3] if tier == REST else span[1]
-                            if (g, tier) == (W8, REST) and sum_id not in first_half:
-                                finish(sum_id, PIECE)
-                            span = next_pass(sum_id, g, tier, narrow)
+                    span = next_pass(sum_id, g, tier)
+                    while span and span[1] - span[0] <= columns:
+                        multiply(sum_id, g, tier, *span)
+                        columns -= span[1] - span[0]
+                        reached[(sum_id, g, tier)] = sum_id[3] if tier == REST else span[1]
+                        if (g, tier) == (W8, REST) and sum_id not in first_half:
+                            finish(sum_id, PIECE)
+                        span = next_pass(sum_id, g, tier)
             return columns
 
         warm = psum.tile([P, BANK], F32, tag="acc", bufs=SUM_BANKS, name="acc")
@@ -295,16 +292,16 @@ def tile_mix_tierx_mix_gelu_kernel(tc, x, w8_words, w8_scales, w4_words, w4_scal
                 stop=True,
             )
 
-        def cast_shared(i, share):
-            cast(i, nc.vector.tensor_copy, 0, share)
-            cast(i, nc.scalar.copy, share, CHUNK)
+        def cast_shared(i):
+            cast(i, nc.vector.tensor_copy, 0, VECTOR_SHARES[i])
+            cast(i, nc.scalar.copy, VECTOR_SHARES[i], CHUNK)
 
-        cast_shared(0, 80)
+        cast_shared(0)
         quantise_eye(2, 2, shifted[:, K_PASS:])
         first_tier(0)
-        cast_shared(1, 64)
+        cast_shared(1)
         first_tier(1)
-        cast_shared(2, 48)
+        cast_shared(2)
         last = N_CHUNKS - 1
         halves = [(0, CHUNK // 2), (CHUNK // 2, CHUNK)]
         spare = 0
@@ -324,7 +321,8 @@ def tile_mix_tierx_mix_gelu_kernel(tc, x, w8_words, w8_scales, w4_words, w4_scal
             for sum_id in first_half:
                 if GELU_STEPS[sum_id[0]] == i:
                     finish(sum_id, BANK)
-            spare = take_passes(i, freed, STEP_COLUMNS[i] + spare) % BANK
+            light = i == last or (i >= N_CHUNKS // 2 and i % PER_UNIT == 0)
+            spare = take_passes(i, freed, (BANK if light else 2 * BANK) + spare) % BANK
         quantise(REST, last - 1, 0, CHUNK)
         for lo, hi in halves:
             quantise(REST, last, lo, hi)

@@ -36,6 +36,8 @@ PIECE = 256
 EYE_ORDER = [3, 1, 0, 2]
 W4_STEP = 1
 W8_STEPS = [5, 6]
+WARM = 256
+WARM_UPS = 9
 SPLIT = 1
 GELU_STEPS = [9, 11, 12, 12]
 
@@ -56,7 +58,14 @@ def tile_mix_tierx_mix_gelu_kernel(tc, x, w8_words, w8_scales, w4_words, w4_scal
         eye_plane = sb("eye_plane", [P, K_PASS], U8)
         w_planes = sb("w_planes", [P, 2 * N], U8)
         bias = sb("bias", [P, N_TILES], F32)
+        q_codes = [sb("q_codes%d" % g, [P, T], U32) for g in (W8, W4)]
+        q_plane = [sb("q_plane%d" % g, [P, T], U8) for g in (W8, W4)]
+        r_codes = [sb("r_codes%d" % g, [P, T], U32) for g in (W8, W4)]
+        r_plane = [sb("r_plane%d" % g, [P, T], U8) for g in (W8, W4)]
         diag_words = diag[:].bitcast(F32)
+        warm_codes = q_codes[W8][:, 0:WARM]
+        warm_plane = q_codes[W8][:, WARM : WARM + WARM // PACK].bitcast(U8)
+        nc.vector.memset(q_codes[W8][:, 0 : WARM + WARM // PACK].bitcast(I32), 0)
         nc.vector.memset(diag[:].bitcast(I32), 0)
         nc.vector.memset(w_planes[:].bitcast(I32), 0)
         table_warm = sb("table_warm", [P, 1], F32)
@@ -144,10 +153,6 @@ def tile_mix_tierx_mix_gelu_kernel(tc, x, w8_words, w8_scales, w4_words, w4_scal
         load_bias()
         load_x(14, 2)
 
-        q_codes = [sb("q_codes%d" % g, [P, T], U32) for g in (W8, W4)]
-        q_plane = [sb("q_plane%d" % g, [P, T], U8) for g in (W8, W4)]
-        r_codes = [sb("r_codes%d" % g, [P, T], U32) for g in (W8, W4)]
-        r_plane = [sb("r_plane%d" % g, [P, T], U8) for g in (W8, W4)]
         tiers = {FIRST: (q_codes, q_plane, E4M3), REST: (r_codes, r_plane, E5M2)}
         x_bf = sb("x_bf", [P, N_CHUNKS * K_PASS], BF16)
         r_bf = sb("r_bf", [P, N_CHUNKS * K_PASS], BF16)
@@ -281,13 +286,13 @@ def tile_mix_tierx_mix_gelu_kernel(tc, x, w8_words, w8_scales, w4_words, w4_scal
             return columns
 
         warm = psum.tile([P, BANK], F32, tag="acc", bufs=SUM_BANKS, name="acc")
-        for quarters in [1, 1, 1, 1, 2, 2, 2, 2]:
+        for count in range(WARM_UPS):
             nc.tensor.matmul_mx(
-                out=warm[:, eye_cols(0, quarters)],
-                lhsT=eye_codes[:, eye_cols(0)].bitcast(E4M3),
-                lhsT_scale=eye_plane[:, eye_cols(0)],
-                rhs=eye_codes[:, eye_cols(0, quarters)].bitcast(E4M3),
-                rhs_scale=eye_plane[:, eye_cols(0, quarters)],
+                out=warm[:, 0:WARM],
+                lhsT=warm_codes[:, 0:P].bitcast(E4M3),
+                lhsT_scale=warm_plane[:, 0:P],
+                rhs=warm_codes.bitcast(E4M3),
+                rhs_scale=warm_plane,
                 start=True,
                 stop=True,
             )

@@ -31,7 +31,8 @@ WALK = 2
 AHEAD = 2
 VALUE_BANKS = 2
 SUM_BANKS = 6
-VECTOR_SHARES = [80, 64, 48]
+VECTOR_SHARE = 80
+SHARE_STEP = 16
 PIECE = 256
 EYE_ORDER = [3, 1, 0, 2]
 W4_STEP = 1
@@ -39,7 +40,8 @@ W8_STEPS = [5, 6]
 WARM = 256
 WARM_UPS = 9
 SPLIT = 1
-GELU_STEPS = [9, 11, 12, 12]
+FIRST_GELU = 9
+GELU_EVERY = 2
 
 
 def tile_mix_tierx_mix_gelu_kernel(tc, x, w8_words, w8_scales, w4_words, w4_scales, b, out):
@@ -63,20 +65,22 @@ def tile_mix_tierx_mix_gelu_kernel(tc, x, w8_words, w8_scales, w4_words, w4_scal
         r_codes = [sb("r_codes%d" % g, [P, T], U32) for g in (W8, W4)]
         r_plane = [sb("r_plane%d" % g, [P, T], U8) for g in (W8, W4)]
         diag_words = diag[:].bitcast(F32)
-        warm_codes = q_codes[W8][:, 0:WARM]
-        warm_plane = q_codes[W8][:, WARM : WARM + WARM // PACK].bitcast(U8)
-        nc.vector.memset(q_codes[W8][:, 0 : WARM + WARM // PACK].bitcast(I32), 0)
-        nc.vector.memset(diag[:].bitcast(I32), 0)
+        zeros = q_codes[W8][:, 0 : WARM + WARM // PACK]
+        warm_codes = zeros[:, 0:WARM]
+        warm_plane = zeros[:, WARM:].bitcast(U8)
+        nc.vector.memset(zeros.bitcast(I32), 0)
         nc.vector.memset(w_planes[:].bitcast(I32), 0)
         table_warm = sb("table_warm", [P, 1], F32)
-        nc.scalar.activation(out=table_warm[:], in_=diag_words[:, 0:1], func=GELU, bias=diag_words[:, 0:1], scale=1.0)
+        zero = zeros[:, 0:1].bitcast(F32)
+        nc.scalar.activation(out=table_warm[:], in_=zero, func=GELU, bias=zero, scale=1.0)
+        diag_width = (K_PASS + PACK) // 2
         nc.gpsimd.affine_select(
-            out=diag_words[:, 1:],
-            in_=diag_words[:, 1:],
+            out=diag_words,
+            in_=zeros[:, 0:diag_width].bitcast(F32),
             compare_op=mybir.AluOpType.not_equal,
             fill=1.0,
-            base=0,
-            pattern=[[-1, (K_PASS + PACK) // 2 - 1]],
+            base=1,
+            pattern=[[-1, diag_width]],
             channel_multiplier=2,
         )
 
@@ -298,8 +302,9 @@ def tile_mix_tierx_mix_gelu_kernel(tc, x, w8_words, w8_scales, w4_words, w4_scal
             )
 
         def cast_shared(i):
-            cast(i, nc.vector.tensor_copy, 0, VECTOR_SHARES[i])
-            cast(i, nc.scalar.copy, VECTOR_SHARES[i], CHUNK)
+            share = VECTOR_SHARE - SHARE_STEP * i
+            cast(i, nc.vector.tensor_copy, 0, share)
+            cast(i, nc.scalar.copy, share, CHUNK)
 
         cast_shared(0)
         quantise_eye(2, 2, shifted[:, K_PASS:])
@@ -324,7 +329,7 @@ def tile_mix_tierx_mix_gelu_kernel(tc, x, w8_words, w8_scales, w4_words, w4_scal
                 for chunk in range(max(i - 1, 1), i + 1):
                     quantise(REST, chunk, 0, CHUNK)
             for sum_id in first_half:
-                if GELU_STEPS[sum_id[0]] == i:
+                if min(FIRST_GELU + GELU_EVERY * sum_id[0], last - AHEAD - 1) == i:
                     finish(sum_id, BANK)
             light = i == last or (i >= N_CHUNKS // 2 and i % PER_UNIT == 0)
             spare = take_passes(i, freed, (BANK if light else 2 * BANK) + spare) % BANK

@@ -37,11 +37,11 @@ PIECE = 256
 EYE_ORDER = [3, 1, 0, 2]
 W4_STEP = 1
 W8_STEPS = [5, 6]
+BIAS_PITCH = 8
 WARM = 256
 WARM_UPS = 9
 SPLIT = 1
 FIRST_GELU = 9
-GELU_EVERY = 2
 
 
 def tile_mix_tierx_mix_gelu_kernel(tc, x, w8_words, w8_scales, w4_words, w4_scales, b, out):
@@ -59,7 +59,7 @@ def tile_mix_tierx_mix_gelu_kernel(tc, x, w8_words, w8_scales, w4_words, w4_scal
         eye_codes = sb("eye_codes", [P, K_PASS], U32)
         eye_plane = sb("eye_plane", [P, K_PASS], U8)
         w_planes = sb("w_planes", [P, 2 * N], U8)
-        bias = sb("bias", [P, N_TILES], F32)
+        bias = sb("bias", [P, N_TILES, BIAS_PITCH], F32)
         q_codes = [sb("q_codes%d" % g, [P, T], U32) for g in (W8, W4)]
         q_plane = [sb("q_plane%d" % g, [P, T], U8) for g in (W8, W4)]
         r_codes = [sb("r_codes%d" % g, [P, T], U32) for g in (W8, W4)]
@@ -118,9 +118,9 @@ def tile_mix_tierx_mix_gelu_kernel(tc, x, w8_words, w8_scales, w4_words, w4_scal
             for pos in range(count):
                 raw[first + pos] = slab[:, :, pos * CHUNK : (pos + 1) * CHUNK]
 
-        def load_bias():
+        def load_bias(lo, hi):
             with nc.allow_non_contiguous_dma(reason="one bias value a partition and output tile"):
-                nc.sync.dma_start(out=bias[:], in_=b.rearrange("(n p) -> p n", p=P))
+                nc.sync.dma_start(out=bias[:, lo:hi, 0], in_=b.rearrange("(n p) -> p n", p=P)[:, lo:hi])
 
         def load_plane(g, scales, rows):
             for r in rows:
@@ -154,8 +154,9 @@ def tile_mix_tierx_mix_gelu_kernel(tc, x, w8_words, w8_scales, w4_words, w4_scal
         load_w8(1)
         load_x(10, 2)
         load_x(12, 2)
-        load_bias()
+        load_bias(0, 1)
         load_x(14, 2)
+        load_bias(1, N_TILES)
 
         tiers = {FIRST: (q_codes, q_plane, E4M3), REST: (r_codes, r_plane, E5M2)}
         x_bf = sb("x_bf", [P, N_CHUNKS * K_PASS], BF16)
@@ -242,7 +243,7 @@ def tile_mix_tierx_mix_gelu_kernel(tc, x, w8_words, w8_scales, w4_words, w4_scal
                     out=result[:],
                     in_=acc[sum_id][:, t0 - window : t0 - window + width],
                     func=GELU,
-                    bias=bias[:, n : n + 1],
+                    bias=bias[:, n, 0:1],
                     scale=1.0,
                 )
                 nc.sync.dma_start(out=out[n * P : (n + 1) * P, t0 : t0 + width], in_=result[:])
@@ -329,7 +330,7 @@ def tile_mix_tierx_mix_gelu_kernel(tc, x, w8_words, w8_scales, w4_words, w4_scal
                 for chunk in range(max(i - 1, 1), i + 1):
                     quantise(REST, chunk, 0, CHUNK)
             for sum_id in first_half:
-                if min(FIRST_GELU + GELU_EVERY * sum_id[0], last - AHEAD - 1) == i:
+                if i == (FIRST_GELU if sum_id[0] == 0 else last - AHEAD - 1):
                     finish(sum_id, BANK)
             light = i == last or (i >= N_CHUNKS // 2 and i % PER_UNIT == 0)
             spare = take_passes(i, freed, (BANK if light else 2 * BANK) + spare) % BANK

@@ -38,6 +38,8 @@ EYE_ORDER = [3, 1, 0, 2]
 W4_STEP = 1
 W8_STEPS = [5, 6]
 BIAS_PITCH = 8
+CODES_AT = 16
+PLANE_AT = 192
 WARM = 256
 WARM_UPS = 9
 SPLIT = 1
@@ -60,10 +62,10 @@ def tile_mix_tierx_mix_gelu_kernel(tc, x, w8_words, w8_scales, w4_words, w4_scal
         eye_plane = sb("eye_plane", [P, K_PASS], U8)
         w_planes = sb("w_planes", [P, 2 * N], U8)
         bias = sb("bias", [P, N_TILES, BIAS_PITCH], F32)
-        q_codes = [sb("q_codes%d" % g, [P, T], U32) for g in (W8, W4)]
-        q_plane = [sb("q_plane%d" % g, [P, T], U8) for g in (W8, W4)]
-        r_codes = [sb("r_codes%d" % g, [P, T], U32) for g in (W8, W4)]
-        r_plane = [sb("r_plane%d" % g, [P, T], U8) for g in (W8, W4)]
+        q_codes = [sb("q_codes%d" % g, [P, CODES_AT + T], U32)[:, CODES_AT:] for g in (W8, W4)]
+        q_plane = [sb("q_plane%d" % g, [P, PLANE_AT + T], U8)[:, PLANE_AT:] for g in (W8, W4)]
+        r_codes = [sb("r_codes%d" % g, [P, CODES_AT + T], U32)[:, CODES_AT:] for g in (W8, W4)]
+        r_plane = [sb("r_plane%d" % g, [P, PLANE_AT + T], U8)[:, PLANE_AT:] for g in (W8, W4)]
         diag_words = diag[:].bitcast(F32)
         zeros = q_codes[W8][:, 0 : WARM + WARM // PACK]
         warm_codes = zeros[:, 0:WARM]

@@ -21,29 +21,31 @@ PACK = 4
 K_PASS = P * PACK
 BANK = 512
 CHUNK = 128
-PER_UNIT = BANK // CHUNK
+PAIR = 2 * CHUNK
 N_CHUNKS = (K // K_PASS) * (T // CHUNK)
 N_TILES = N // P
 W8, W4 = 0, 1
 FIRST, REST = 0, 1
-ALIGN = 2048
+ALIGN = 1024
 WALK = 2
 AHEAD = 2
 VALUE_BANKS = 2
 SUM_BANKS = 6
 VECTOR_SHARE = 80
 SHARE_STEP = 16
-PIECE = 256
 EYE_ORDER = [3, 1, 0, 2]
-W4_STEP = 1
-W8_STEPS = [5, 6]
+W4_STEP = 0
+W8_STEP = 3
 BIAS_PITCH = 8
 CODES_AT = 16
 PLANE_AT = 192
 WARM = 256
 WARM_UPS = 9
-SPLIT = 1
-FIRST_GELU = 9
+WINDOWS = [(0, 256, 2), (256, 256, 2), (512, 256, 2), (768, 128, 4), (896, 128, 2)]
+ORDER = [(W4, 0), (W4, 1), (W8, 0), (W8, 1), (W4, 2), (W8, 2), (W4, 3), (W8, 3), (W4, 4), (W8, 4)]
+PASS_COLUMNS = 1024
+STORE_TILES = 2
+GELU_COLUMNS = 256
 
 
 def tile_mix_tierx_mix_gelu_kernel(tc, x, w8_words, w8_scales, w4_words, w4_scales, b, out):
@@ -101,24 +103,20 @@ def tile_mix_tierx_mix_gelu_kernel(tc, x, w8_words, w8_scales, w4_words, w4_scal
             )
         quantise_eye(1, 1, shifted[:, 0:K_PASS])
 
+        chunks = [(g, t0) for g, w in ORDER for t0 in range(WINDOWS[w][0], WINDOWS[w][0] + WINDOWS[w][1], CHUNK)]
         raw = {}
         w8 = sb("w8", [P, 4 * N], U8)
         w4 = sb("w4", [P, 2 * N], U8)
 
-        def place(i):
-            unit, block = divmod(i, PER_UNIT)
-            return W4 if unit % 2 == 0 else W8, (unit // 2) * BANK + block * CHUNK
-
-        def load_x(first, count):
-            g, t0 = place(first)
-            width = CHUNK * count
+        def load_x(first, width):
+            g, t0 = chunks[first]
             slab = sb("x%d" % first, [P, PACK, width], F32)
             nc.sync.dma_start(
                 out=slab[:],
                 in_=x[g * K_PASS : (g + 1) * K_PASS, t0 : t0 + width].rearrange("(p j) w -> p j w", j=PACK),
             )
-            for pos in range(count):
-                raw[first + pos] = slab[:, :, pos * CHUNK : (pos + 1) * CHUNK]
+            for pos in range(0, width, CHUNK):
+                raw[(g, t0 + pos)] = slab[:, :, pos : pos + CHUNK]
 
         def load_bias(lo, hi):
             with nc.allow_non_contiguous_dma(reason="one bias value a partition and output tile"):
@@ -139,26 +137,25 @@ def tile_mix_tierx_mix_gelu_kernel(tc, x, w8_words, w8_scales, w4_words, w4_scal
                 out=w8[:, cols].bitcast(I32), in_=w8_words[0].rearrange("p n i -> p (n i)")[:, cols].bitcast(I32)
             )
 
-        load_x(0, 1)
-        load_x(1, 1)
-        load_x(2, 1)
+        load_x(0, CHUNK)
+        load_x(1, CHUNK)
+        load_x(2, CHUNK)
         load_plane(W4, w4_scales, [0, 1])
-        load_x(3, 1)
+        load_x(3, CHUNK)
         load_plane(W4, w4_scales, [2, 3])
-        load_x(4, 1)
-        load_x(5, 1)
         load_w4()
-        load_x(6, 1)
-        load_x(7, 1)
-        load_x(8, 2)
-        load_w8(0)
+        load_x(4, CHUNK)
+        load_x(5, CHUNK)
         load_plane(W8, w8_scales, [0, 1, 2, 3])
+        load_w8(0)
+        load_x(6, CHUNK)
         load_w8(1)
-        load_x(10, 2)
-        load_x(12, 2)
-        load_bias(0, 1)
-        load_x(14, 2)
-        load_bias(1, N_TILES)
+        load_x(7, CHUNK)
+        load_x(8, PAIR)
+        load_bias(0, N_TILES)
+        load_x(10, PAIR)
+        load_x(12, PAIR)
+        load_x(13, PAIR)
 
         tiers = {FIRST: (q_codes, q_plane, E4M3), REST: (r_codes, r_plane, E5M2)}
         x_bf = sb("x_bf", [P, N_CHUNKS * K_PASS], BF16)
@@ -174,15 +171,14 @@ def tile_mix_tierx_mix_gelu_kernel(tc, x, w8_words, w8_scales, w4_words, w4_scal
             return tile[:, i * K_PASS + lo * PACK : i * K_PASS + hi * PACK]
 
         values = {}
-        acc = {}
         coded = {(g, tier): 0 for g in (W8, W4) for tier in (FIRST, REST)}
 
         def cast(i, copy, lo=0, hi=CHUNK):
-            copy(out=words_walk(staged(x_bf, i, lo, hi)), in_=rows_walk(raw[i][:, :, lo:hi]))
+            copy(out=words_walk(staged(x_bf, i, lo, hi)), in_=rows_walk(raw[chunks[i]][:, :, lo:hi]))
 
-        def quantise(tier, i, lo, hi):
+        def quantise(tier, i, lo=0, hi=CHUNK):
             codes, plane, fmt = tiers[tier]
-            g, t0 = place(i)
+            g, t0 = chunks[i]
             cols = slice(t0 + lo, t0 + hi)
             nc.vector.quantize_mx(
                 out=codes[g][:, cols].bitcast(fmt),
@@ -192,8 +188,8 @@ def tile_mix_tierx_mix_gelu_kernel(tc, x, w8_words, w8_scales, w4_words, w4_scal
             coded[(g, tier)] = t0 + hi
 
         def first_tier(i):
-            quantise(FIRST, i, 0, CHUNK)
-            g, t0 = place(i)
+            quantise(FIRST, i)
+            g, t0 = chunks[i]
             cols = slice(t0, t0 + CHUNK)
             values[i] = psum.tile([P, PACK, CHUNK], F32, tag="values", bufs=VALUE_BANKS, name="values")
             for quarter, j in enumerate(EYE_ORDER):
@@ -210,87 +206,76 @@ def tile_mix_tierx_mix_gelu_kernel(tc, x, w8_words, w8_scales, w4_words, w4_scal
         def subtract(i, lo=0, hi=CHUNK):
             nc.vector.tensor_tensor(
                 out=words_walk(staged(r_bf, i, lo, hi)),
-                in0=rows_walk(raw[i][:, :, lo:hi]),
+                in0=rows_walk(raw[chunks[i]][:, :, lo:hi]),
                 in1=rows_walk(values[i][:, :, lo:hi]),
                 op=mybir.AluOpType.subtract,
             )
 
-        def multiply(sum_id, g, tier, t0, t1):
-            n, window = sum_id[:2]
+        banks = [(w, n0) for w, (t0, width, tiles) in enumerate(WINDOWS) for n0 in range(0, N_TILES, tiles)]
+        products = [(W4, FIRST), (W4, REST), (W8, FIRST), (W8, REST)]
+        waiting = {
+            (w, n0): [(g, tier, n) for g, tier in products for n in range(n0, n0 + WINDOWS[w][2])] for w, n0 in banks
+        }
+        acc = {}
+        closed = []
+        emptied = set()
+        results = {}
+
+        def multiply(bank, g, tier, n):
+            w, n0 = bank
+            t0, width, tiles = WINDOWS[w]
             codes, plane, fmt = tiers[tier]
-            opening = sum_id not in acc
+            opening = bank not in acc
             if opening:
-                acc[sum_id] = psum.tile([P, BANK], F32, tag="acc", bufs=SUM_BANKS, name="acc")
+                acc[bank] = psum.tile([P, BANK], F32, tag="acc", bufs=SUM_BANKS, name="acc")
             if g == W8:
                 weights = w8[:, 4 * P * n : 4 * P * (n + 1)].bitcast(E4M3)
             else:
                 weights = w4[:, 2 * P * n : 2 * P * (n + 1)].bitcast(E2M1)
+            waiting[bank].remove((g, tier, n))
             nc.tensor.matmul_mx(
-                out=acc[sum_id][:, t0 - window : t1 - window],
+                out=acc[bank][:, (n - n0) * width : (n - n0 + 1) * width],
                 lhsT=weights,
                 lhsT_scale=w_planes[:, g * N + P * n : g * N + P * (n + 1)],
-                rhs=codes[g][:, t0:t1].bitcast(fmt),
-                rhs_scale=plane[g][:, t0:t1],
+                rhs=codes[g][:, t0 : t0 + width].bitcast(fmt),
+                rhs_scale=plane[g][:, t0 : t0 + width],
                 start=opening,
-                stop=(g, tier) == (W8, REST),
+                stop=not waiting[bank],
             )
+            if not waiting[bank]:
+                closed.extend((bank, tile) for tile in range(n0, n0 + tiles))
 
-        stored = set()
+        def take_passes(i, columns):
+            for number, bank in enumerate(banks):
+                if number + 1 >= SUM_BANKS + 1 and banks[number - SUM_BANKS] not in emptied:
+                    break
+                t0, width, tiles = WINDOWS[bank[0]]
+                for g, tier, n in list(waiting[bank]):
+                    landed = i >= (W4_STEP if g == W4 else W8_STEP)
+                    if landed and coded[(g, tier)] >= t0 + width and columns >= width:
+                        multiply(bank, g, tier, n)
+                        columns -= width
 
-        def finish(sum_id, width):
-            n, window, lo, hi = sum_id
-            for t0 in range(lo, hi, width):
-                result = sb("result%d_%d" % (n, t0), [P, width], F32)
+        def finish(columns):
+            while closed and columns >= WINDOWS[closed[0][0][0]][1]:
+                bank, n = closed.pop(0)
+                w, n0 = bank
+                t0, width, tiles = WINDOWS[w]
+                if n % STORE_TILES == 0:
+                    results[w] = sb("result%d_%d" % (w, n), [P, STORE_TILES, width], F32)
                 nc.scalar.activation(
-                    out=result[:],
-                    in_=acc[sum_id][:, t0 - window : t0 - window + width],
+                    out=results[w][:, n % STORE_TILES, :],
+                    in_=acc[bank][:, (n - n0) * width : (n - n0 + 1) * width],
                     func=GELU,
                     bias=bias[:, n, 0:1],
                     scale=1.0,
                 )
-                nc.sync.dma_start(out=out[n * P : (n + 1) * P, t0 : t0 + width], in_=result[:])
-            stored.add(sum_id)
-
-        cut = BANK + BANK // 2
-        whole_tiles = N_TILES - SPLIT
-        first_half = [(n, 0, 0, BANK) for n in range(N_TILES)]
-        early = [(n, cut - BANK, BANK, cut) for n in range(whole_tiles, N_TILES)]
-        late = [(n, BANK, BANK if n < whole_tiles else cut, T) for n in range(N_TILES)]
-        sums = first_half + late[:1] + early + late[1:]
-        reached = {(sum_id, g, tier): sum_id[2] for sum_id in sums for g in (W8, W4) for tier in (FIRST, REST)}
-
-        def next_pass(sum_id, g, tier):
-            n, window, lo, hi = sum_id
-            t0 = reached[(sum_id, g, tier)]
-            whole = hi - lo == BANK
-            if t0 == hi or coded[(g, tier)] < hi:
-                return None
-            if tier == REST:
-                before = [(W4, FIRST), (W4, REST), (W8, FIRST)] if g == W8 else [(W4, FIRST)] if whole else []
-                waits = any(reached[(sum_id, *other)] < hi for other in before)
-                return None if waits else (window, window + BANK)
-            if (g == W8 and reached[(sum_id, W4, FIRST)] < hi) or (not whole and sum_id not in acc):
-                return None
-            return t0, (hi if whole or g == W8 else t0 + CHUNK)
-
-        def take_passes(i, freed, columns, only=None):
-            for number, sum_id in enumerate(sums):
-                if number >= SUM_BANKS and sums[number - SUM_BANKS] not in freed:
-                    break
-                if only not in (None, sum_id):
-                    continue
-                for g, tier in [(W4, FIRST), (W4, REST), (W4, FIRST), (W8, FIRST), (W8, REST)]:
-                    if i < (W4_STEP if g == W4 else W8_STEPS[sum_id[0] // 2]):
-                        continue
-                    span = next_pass(sum_id, g, tier)
-                    while span and span[1] - span[0] <= columns:
-                        multiply(sum_id, g, tier, *span)
-                        columns -= span[1] - span[0]
-                        reached[(sum_id, g, tier)] = sum_id[3] if tier == REST else span[1]
-                        if (g, tier) == (W8, REST) and sum_id not in first_half:
-                            finish(sum_id, PIECE)
-                        span = next_pass(sum_id, g, tier)
-            return columns
+                if (n + 1) % STORE_TILES == 0:
+                    rows = out[(n + 1 - STORE_TILES) * P : (n + 1) * P, t0 : t0 + width]
+                    nc.sync.dma_start(out=rows.rearrange("(n p) t -> p n t", p=P), in_=results[w][:])
+                columns -= width
+                if n == n0 + tiles - 1:
+                    emptied.add(bank)
 
         warm = psum.tile([P, BANK], F32, tag="acc", bufs=SUM_BANKS, name="acc")
         for count in range(WARM_UPS):
@@ -317,27 +302,27 @@ def tile_mix_tierx_mix_gelu_kernel(tc, x, w8_words, w8_scales, w4_words, w4_scal
         cast_shared(2)
         last = N_CHUNKS - 1
         halves = [(0, CHUNK // 2), (CHUNK // 2, CHUNK)]
-        spare = 0
         for i in range(N_CHUNKS):
-            freed = set(stored)
             for lo, hi in halves if i == last else [(0, CHUNK)]:
                 subtract(i, lo, hi)
-            if i + AHEAD + 1 <= last:
+            rounds = i + AHEAD + 1 <= last
+            if rounds:
                 cast(i + AHEAD + 1, nc.scalar.copy)
+            finish(GELU_COLUMNS if rounds else T * N_TILES)
             if i == 1:
-                quantise(REST, 0, 0, CHUNK)
+                quantise(REST, 0)
             if i + AHEAD <= last:
                 first_tier(i + AHEAD)
+            if i != last - AHEAD:
+                take_passes(i, PASS_COLUMNS)
             if i % 2 == 1 and i < last:
                 for chunk in range(max(i - 1, 1), i + 1):
-                    quantise(REST, chunk, 0, CHUNK)
-            for sum_id in first_half:
-                if i == (FIRST_GELU if sum_id[0] == 0 else last - AHEAD - 1):
-                    finish(sum_id, BANK)
-            light = i == last or (i >= N_CHUNKS // 2 and i % PER_UNIT == 0)
-            spare = take_passes(i, freed, (BANK if light else 2 * BANK) + spare) % BANK
-        quantise(REST, last - 1, 0, CHUNK)
+                    quantise(REST, chunk)
+            if i == last - AHEAD:
+                take_passes(i, PASS_COLUMNS)
+        finish(T * N_TILES)
+        quantise(REST, last - 1)
         for lo, hi in halves:
             quantise(REST, last, lo, hi)
-        for sum_id in late:
-            take_passes(last, stored, 4 * BANK, sum_id)
+        take_passes(last, T * N_TILES)
+        finish(T * N_TILES)

@@ -21,7 +21,6 @@ PACK = 4
 K_PASS = P * PACK
 BANK = 512
 CHUNK = 128
-PAIR = 2 * CHUNK
 N_CHUNKS = (K // K_PASS) * (T // CHUNK)
 N_TILES = N // P
 W8, W4 = 0, 1
@@ -35,17 +34,17 @@ VECTOR_SHARE = 80
 SHARE_STEP = 16
 EYE_ORDER = [3, 1, 0, 2]
 W4_STEP = 0
-W8_STEP = 3
+W8_STEP = 5
 BIAS_PITCH = 8
 CODES_AT = 16
 PLANE_AT = 192
 WARM = 256
 WARM_UPS = 9
 WINDOWS = [(0, 256, 2), (256, 256, 2), (512, 256, 2), (768, 128, 4), (896, 128, 2)]
-ORDER = [(W4, 0), (W4, 1), (W8, 0), (W8, 1), (W4, 2), (W8, 2), (W4, 3), (W8, 3), (W4, 4), (W8, 4)]
+ORDER = [(W4, 0), (W4, 1), (W4, 2), (W8, 0), (W8, 1), (W8, 2), (W4, 3), (W8, 3), (W4, 4), (W8, 4)]
 PASS_COLUMNS = 1024
 STORE_TILES = 2
-GELU_COLUMNS = 256
+FIRST_GELU = 9
 
 
 def tile_mix_tierx_mix_gelu_kernel(tc, x, w8_words, w8_scales, w4_words, w4_scales, b, out):
@@ -108,19 +107,17 @@ def tile_mix_tierx_mix_gelu_kernel(tc, x, w8_words, w8_scales, w4_words, w4_scal
         w8 = sb("w8", [P, 4 * N], U8)
         w4 = sb("w4", [P, 2 * N], U8)
 
-        def load_x(first, width):
-            g, t0 = chunks[first]
-            slab = sb("x%d" % first, [P, PACK, width], F32)
+        def load_x(i):
+            g, t0 = chunks[i]
+            raw[i] = sb("x%d" % i, [P, PACK, CHUNK], F32)
             nc.sync.dma_start(
-                out=slab[:],
-                in_=x[g * K_PASS : (g + 1) * K_PASS, t0 : t0 + width].rearrange("(p j) w -> p j w", j=PACK),
+                out=raw[i][:],
+                in_=x[g * K_PASS : (g + 1) * K_PASS, t0 : t0 + CHUNK].rearrange("(p j) w -> p j w", j=PACK),
             )
-            for pos in range(0, width, CHUNK):
-                raw[(g, t0 + pos)] = slab[:, :, pos : pos + CHUNK]
 
-        def load_bias(lo, hi):
+        def load_bias():
             with nc.allow_non_contiguous_dma(reason="one bias value a partition and output tile"):
-                nc.sync.dma_start(out=bias[:, lo:hi, 0], in_=b.rearrange("(n p) -> p n", p=P)[:, lo:hi])
+                nc.sync.dma_start(out=bias[:, :, 0], in_=b.rearrange("(n p) -> p n", p=P))
 
         def load_plane(g, scales, rows):
             for r in rows:
@@ -137,25 +134,27 @@ def tile_mix_tierx_mix_gelu_kernel(tc, x, w8_words, w8_scales, w4_words, w4_scal
                 out=w8[:, cols].bitcast(I32), in_=w8_words[0].rearrange("p n i -> p (n i)")[:, cols].bitcast(I32)
             )
 
-        load_x(0, CHUNK)
-        load_x(1, CHUNK)
-        load_x(2, CHUNK)
+        load_x(0)
+        load_x(1)
+        load_x(2)
         load_plane(W4, w4_scales, [0, 1])
-        load_x(3, CHUNK)
+        load_x(3)
         load_plane(W4, w4_scales, [2, 3])
+        load_x(4)
         load_w4()
-        load_x(4, CHUNK)
-        load_x(5, CHUNK)
-        load_plane(W8, w8_scales, [0, 1, 2, 3])
+        load_x(5)
+        load_x(6)
+        load_plane(W8, w8_scales, [0, 1])
+        load_x(7)
+        load_plane(W8, w8_scales, [2, 3])
         load_w8(0)
-        load_x(6, CHUNK)
+        load_x(8)
         load_w8(1)
-        load_x(7, CHUNK)
-        load_x(8, PAIR)
-        load_bias(0, N_TILES)
-        load_x(10, PAIR)
-        load_x(12, PAIR)
-        load_x(13, PAIR)
+        load_x(9)
+        load_x(10)
+        load_bias()
+        for i in range(11, N_CHUNKS):
+            load_x(i)
 
         tiers = {FIRST: (q_codes, q_plane, E4M3), REST: (r_codes, r_plane, E5M2)}
         x_bf = sb("x_bf", [P, N_CHUNKS * K_PASS], BF16)
@@ -174,7 +173,7 @@ def tile_mix_tierx_mix_gelu_kernel(tc, x, w8_words, w8_scales, w4_words, w4_scal
         coded = {(g, tier): 0 for g in (W8, W4) for tier in (FIRST, REST)}
 
         def cast(i, copy, lo=0, hi=CHUNK):
-            copy(out=words_walk(staged(x_bf, i, lo, hi)), in_=rows_walk(raw[chunks[i]][:, :, lo:hi]))
+            copy(out=words_walk(staged(x_bf, i, lo, hi)), in_=rows_walk(raw[i][:, :, lo:hi]))
 
         def quantise(tier, i, lo=0, hi=CHUNK):
             codes, plane, fmt = tiers[tier]
@@ -206,7 +205,7 @@ def tile_mix_tierx_mix_gelu_kernel(tc, x, w8_words, w8_scales, w4_words, w4_scal
         def subtract(i, lo=0, hi=CHUNK):
             nc.vector.tensor_tensor(
                 out=words_walk(staged(r_bf, i, lo, hi)),
-                in0=rows_walk(raw[chunks[i]][:, :, lo:hi]),
+                in0=rows_walk(raw[i][:, :, lo:hi]),
                 in1=rows_walk(values[i][:, :, lo:hi]),
                 op=mybir.AluOpType.subtract,
             )
@@ -305,10 +304,15 @@ def tile_mix_tierx_mix_gelu_kernel(tc, x, w8_words, w8_scales, w4_words, w4_scal
         for i in range(N_CHUNKS):
             for lo, hi in halves if i == last else [(0, CHUNK)]:
                 subtract(i, lo, hi)
-            rounds = i + AHEAD + 1 <= last
-            if rounds:
+            if i < FIRST_GELU:
                 cast(i + AHEAD + 1, nc.scalar.copy)
-            finish(GELU_COLUMNS if rounds else T * N_TILES)
+            elif i == FIRST_GELU:
+                for chunk in range(i + AHEAD + 1, last):
+                    cast(chunk, nc.scalar.copy)
+                finish(BANK)
+                cast(last, nc.scalar.copy)
+            else:
+                finish(T * N_TILES)
             if i == 1:
                 quantise(REST, 0)
             if i + AHEAD <= last:

@@ -34,16 +34,15 @@ VECTOR_SHARE = 80
 SHARE_STEP = 16
 EYE_ORDER = [3, 1, 0, 2]
 W4_STEP = 0
-W8_STEP = 5
+W8_STEP = 6
 BIAS_PITCH = 8
 CODES_AT = 16
 PLANE_AT = 192
 WARM = 256
 WARM_UPS = 9
-WINDOWS = [(0, 256, 2), (256, 256, 2), (512, 256, 2), (768, 128, 4), (896, 128, 2)]
+WINDOWS = [(0, 256, 2, 2), (256, 256, 2, 2), (512, 256, 2, 2), (768, 128, 4, 2), (896, 128, 1, 2)]
 ORDER = [(W4, 0), (W4, 1), (W4, 2), (W8, 0), (W8, 1), (W8, 2), (W4, 3), (W8, 3), (W4, 4), (W8, 4)]
 PASS_COLUMNS = 1024
-STORE_TILES = 2
 FIRST_GELU = 9
 
 
@@ -107,13 +106,16 @@ def tile_mix_tierx_mix_gelu_kernel(tc, x, w8_words, w8_scales, w4_words, w4_scal
         w8 = sb("w8", [P, 4 * N], U8)
         w4 = sb("w4", [P, 2 * N], U8)
 
-        def load_x(i):
-            g, t0 = chunks[i]
-            raw[i] = sb("x%d" % i, [P, PACK, CHUNK], F32)
+        def load_x(first, count=1):
+            g, t0 = chunks[first]
+            width = count * CHUNK
+            slab = sb("x%d" % first, [P, PACK, width], F32)
             nc.sync.dma_start(
-                out=raw[i][:],
-                in_=x[g * K_PASS : (g + 1) * K_PASS, t0 : t0 + CHUNK].rearrange("(p j) w -> p j w", j=PACK),
+                out=slab[:],
+                in_=x[g * K_PASS : (g + 1) * K_PASS, t0 : t0 + width].rearrange("(p j) w -> p j w", j=PACK),
             )
+            for pos in range(count):
+                raw[first + pos] = slab[:, :, pos * CHUNK : (pos + 1) * CHUNK]
 
         def load_bias():
             with nc.allow_non_contiguous_dma(reason="one bias value a partition and output tile"):
@@ -128,11 +130,8 @@ def tile_mix_tierx_mix_gelu_kernel(tc, x, w8_words, w8_scales, w4_words, w4_scal
         def load_w4():
             nc.sync.dma_start(out=w4[:].bitcast(I32), in_=w4_words[0].bitcast(I32))
 
-        def load_w8(half):
-            cols = slice(2 * N * half, 2 * N * (half + 1))
-            nc.sync.dma_start(
-                out=w8[:, cols].bitcast(I32), in_=w8_words[0].rearrange("p n i -> p (n i)")[:, cols].bitcast(I32)
-            )
+        def load_w8():
+            nc.sync.dma_start(out=w8[:].bitcast(I32), in_=w8_words[0].rearrange("p n i -> p (n i)").bitcast(I32))
 
         load_x(0)
         load_x(1)
@@ -144,17 +143,14 @@ def tile_mix_tierx_mix_gelu_kernel(tc, x, w8_words, w8_scales, w4_words, w4_scal
         load_w4()
         load_x(5)
         load_x(6)
-        load_plane(W8, w8_scales, [0, 1])
         load_x(7)
+        load_plane(W8, w8_scales, [0, 1])
+        load_x(8, 2)
         load_plane(W8, w8_scales, [2, 3])
-        load_w8(0)
-        load_x(8)
-        load_w8(1)
-        load_x(9)
-        load_x(10)
-        load_bias()
-        for i in range(11, N_CHUNKS):
+        load_w8()
+        for i in range(10, N_CHUNKS):
             load_x(i)
+        load_bias()
 
         tiers = {FIRST: (q_codes, q_plane, E4M3), REST: (r_codes, r_plane, E5M2)}
         x_bf = sb("x_bf", [P, N_CHUNKS * K_PASS], BF16)
@@ -210,7 +206,7 @@ def tile_mix_tierx_mix_gelu_kernel(tc, x, w8_words, w8_scales, w4_words, w4_scal
                 op=mybir.AluOpType.subtract,
             )
 
-        banks = [(w, n0) for w, (t0, width, tiles) in enumerate(WINDOWS) for n0 in range(0, N_TILES, tiles)]
+        banks = [(w, n0) for w, (t0, width, tiles, count) in enumerate(WINDOWS) for n0 in range(0, N_TILES, tiles)]
         products = [(W4, FIRST), (W4, REST), (W8, FIRST), (W8, REST)]
         waiting = {
             (w, n0): [(g, tier, n) for g, tier in products for n in range(n0, n0 + WINDOWS[w][2])] for w, n0 in banks
@@ -222,7 +218,7 @@ def tile_mix_tierx_mix_gelu_kernel(tc, x, w8_words, w8_scales, w4_words, w4_scal
 
         def multiply(bank, g, tier, n):
             w, n0 = bank
-            t0, width, tiles = WINDOWS[w]
+            t0, width, tiles, count = WINDOWS[w]
             codes, plane, fmt = tiers[tier]
             opening = bank not in acc
             if opening:
@@ -248,7 +244,7 @@ def tile_mix_tierx_mix_gelu_kernel(tc, x, w8_words, w8_scales, w4_words, w4_scal
             for number, bank in enumerate(banks):
                 if number + 1 >= SUM_BANKS + 1 and banks[number - SUM_BANKS] not in emptied:
                     break
-                t0, width, tiles = WINDOWS[bank[0]]
+                t0, width, tiles, count = WINDOWS[bank[0]]
                 for g, tier, n in list(waiting[bank]):
                     landed = i >= (W4_STEP if g == W4 else W8_STEP)
                     if landed and coded[(g, tier)] >= t0 + width and columns >= width:
@@ -259,18 +255,18 @@ def tile_mix_tierx_mix_gelu_kernel(tc, x, w8_words, w8_scales, w4_words, w4_scal
             while closed and columns >= WINDOWS[closed[0][0][0]][1]:
                 bank, n = closed.pop(0)
                 w, n0 = bank
-                t0, width, tiles = WINDOWS[w]
-                if n % STORE_TILES == 0:
-                    results[w] = sb("result%d_%d" % (w, n), [P, STORE_TILES, width], F32)
+                t0, width, tiles, count = WINDOWS[w]
+                if n % count == 0:
+                    results[w] = sb("result%d_%d" % (w, n), [P, count, width], F32)
                 nc.scalar.activation(
-                    out=results[w][:, n % STORE_TILES, :],
+                    out=results[w][:, n % count, :],
                     in_=acc[bank][:, (n - n0) * width : (n - n0 + 1) * width],
                     func=GELU,
                     bias=bias[:, n, 0:1],
                     scale=1.0,
                 )
-                if (n + 1) % STORE_TILES == 0:
-                    rows = out[(n + 1 - STORE_TILES) * P : (n + 1) * P, t0 : t0 + width]
+                if (n + 1) % count == 0:
+                    rows = out[(n + 1 - count) * P : (n + 1) * P, t0 : t0 + width]
                     nc.sync.dma_start(out=rows.rearrange("(n p) t -> p n t", p=P), in_=results[w][:])
                 columns -= width
                 if n == n0 + tiles - 1:
@@ -306,24 +302,21 @@ def tile_mix_tierx_mix_gelu_kernel(tc, x, w8_words, w8_scales, w4_words, w4_scal
                 subtract(i, lo, hi)
             if i < FIRST_GELU:
                 cast(i + AHEAD + 1, nc.scalar.copy)
-            elif i == FIRST_GELU:
-                for chunk in range(i + AHEAD + 1, last):
-                    cast(chunk, nc.scalar.copy)
-                finish(BANK)
-                cast(last, nc.scalar.copy)
             else:
+                if i == FIRST_GELU:
+                    for chunk in range(i + AHEAD + 1, N_CHUNKS):
+                        cast(chunk, nc.scalar.copy)
                 finish(T * N_TILES)
             if i == 1:
                 quantise(REST, 0)
             if i + AHEAD <= last:
                 first_tier(i + AHEAD)
-            if i != last - AHEAD:
-                take_passes(i, PASS_COLUMNS)
             if i % 2 == 1 and i < last:
                 for chunk in range(max(i - 1, 1), i + 1):
                     quantise(REST, chunk)
-            if i == last - AHEAD:
-                take_passes(i, PASS_COLUMNS)
+            if i < last:
+                moved = {last - AHEAD - 1: -BANK, last - AHEAD: BANK}.get(i, 0)
+                take_passes(i, PASS_COLUMNS + moved)
         finish(T * N_TILES)
         quantise(REST, last - 1)
         for lo, hi in halves:

@@ -40,8 +40,14 @@ CODES_AT = 16
 PLANE_AT = 192
 WARM = 256
 WARM_UPS = 9
-WINDOWS = [(0, 256, 2, 2), (256, 256, 2, 2), (512, 256, 2, 2), (768, 128, 4, 2), (896, 128, 1, 2)]
-ORDER = [(W4, 0), (W4, 1), (W4, 2), (W8, 0), (W8, 1), (W8, 2), (W4, 3), (W8, 3), (W4, 4), (W8, 4)]
+WINDOWS = [(0, 512, 1, 1), (512, 256, 2, 2), (768, 128, 4, 2), (896, 128, 1, 2)]
+ORDER = [(W4, 0), (W4, 1), (W8, 0), (W8, 1), (W4, 2), (W8, 2), (W4, 3), (W8, 3)]
+WIDEST = 256
+POOL_CHUNKS = [13, 15]
+POOL_SHARE = 64
+POOL_BEHIND = 5
+BEHIND_W4 = 4
+LATE_SHARE = 48
 PASS_COLUMNS = 1024
 FIRST_GELU = 9
 
@@ -139,8 +145,8 @@ def tile_mix_tierx_mix_gelu_kernel(tc, x, w8_words, w8_scales, w4_words, w4_scal
         load_plane(W4, w4_scales, [0, 1])
         load_x(3)
         load_plane(W4, w4_scales, [2, 3])
-        load_x(4)
         load_w4()
+        load_x(4)
         load_x(5)
         load_x(6)
         load_x(7)
@@ -153,8 +159,20 @@ def tile_mix_tierx_mix_gelu_kernel(tc, x, w8_words, w8_scales, w4_words, w4_scal
         load_bias()
 
         tiers = {FIRST: (q_codes, q_plane, E4M3), REST: (r_codes, r_plane, E5M2)}
-        x_bf = sb("x_bf", [P, N_CHUNKS * K_PASS], BF16)
-        r_bf = sb("r_bf", [P, N_CHUNKS * K_PASS], BF16)
+        stage = sb("stage", [P, 2 * N_CHUNKS * K_PASS], BF16)
+        stage_at = {}
+        free_at = 0
+        for i in range(N_CHUNKS):
+            stage_at[(FIRST, i)] = free_at
+            free_at += K_PASS
+            if i in POOL_CHUNKS:
+                free_at -= PACK * POOL_SHARE
+                stage_at[(REST, i - POOL_BEHIND)] = free_at
+                free_at += K_PASS
+        for i in range(N_CHUNKS):
+            if (REST, i) not in stage_at:
+                stage_at[(REST, i)] = free_at
+                free_at += K_PASS
 
         def rows_walk(ap):
             return ap.rearrange("p j (c i) -> p c j i", i=WALK)
@@ -162,14 +180,28 @@ def tile_mix_tierx_mix_gelu_kernel(tc, x, w8_words, w8_scales, w4_words, w4_scal
         def words_walk(ap):
             return ap.rearrange("p (c i j) -> p c j i", i=WALK, j=PACK)
 
-        def staged(tile, i, lo, hi):
-            return tile[:, i * K_PASS + lo * PACK : i * K_PASS + hi * PACK]
+        def staged(tier, i, lo, hi):
+            return stage[:, stage_at[(tier, i)] + lo * PACK : stage_at[(tier, i)] + hi * PACK]
 
         values = {}
         coded = {(g, tier): 0 for g in (W8, W4) for tier in (FIRST, REST)}
 
         def cast(i, copy, lo=0, hi=CHUNK):
-            copy(out=words_walk(staged(x_bf, i, lo, hi)), in_=rows_walk(raw[i][:, :, lo:hi]))
+            copy(out=words_walk(staged(FIRST, i, lo, hi)), in_=rows_walk(raw[i][:, :, lo:hi]))
+
+        def cast_scalar(i):
+            cast(i, nc.scalar.copy, 0, CHUNK - POOL_SHARE if i in POOL_CHUNKS else CHUNK)
+
+        def cast_pool(i):
+            lo = CHUNK - POOL_SHARE
+            nc.gpsimd.tensor_scalar(
+                out=words_walk(staged(FIRST, i, lo, CHUNK)),
+                in0=rows_walk(raw[i][:, :, lo:]),
+                scalar1=1.0,
+                scalar2=0.0,
+                op0=mybir.AluOpType.mult,
+                op1=mybir.AluOpType.add,
+            )
 
         def quantise(tier, i, lo=0, hi=CHUNK):
             codes, plane, fmt = tiers[tier]
@@ -178,7 +210,7 @@ def tile_mix_tierx_mix_gelu_kernel(tc, x, w8_words, w8_scales, w4_words, w4_scal
             nc.vector.quantize_mx(
                 out=codes[g][:, cols].bitcast(fmt),
                 scales=plane[g][:, cols],
-                in_=staged(r_bf if tier == REST else x_bf, i, lo, hi),
+                in_=staged(tier, i, lo, hi),
             )
             coded[(g, tier)] = t0 + hi
 
@@ -200,7 +232,7 @@ def tile_mix_tierx_mix_gelu_kernel(tc, x, w8_words, w8_scales, w4_words, w4_scal
 
         def subtract(i, lo=0, hi=CHUNK):
             nc.vector.tensor_tensor(
-                out=words_walk(staged(r_bf, i, lo, hi)),
+                out=words_walk(staged(REST, i, lo, hi)),
                 in0=rows_walk(raw[i][:, :, lo:hi]),
                 in1=rows_walk(values[i][:, :, lo:hi]),
                 op=mybir.AluOpType.subtract,
@@ -208,17 +240,23 @@ def tile_mix_tierx_mix_gelu_kernel(tc, x, w8_words, w8_scales, w4_words, w4_scal
 
         banks = [(w, n0) for w, (t0, width, tiles, count) in enumerate(WINDOWS) for n0 in range(0, N_TILES, tiles)]
         products = [(W4, FIRST), (W4, REST), (W8, FIRST), (W8, REST)]
-        waiting = {
-            (w, n0): [(g, tier, n) for g, tier in products for n in range(n0, n0 + WINDOWS[w][2])] for w, n0 in banks
-        }
+        waiting = {}
+        for w, n0 in banks:
+            t0, width, tiles, count = WINDOWS[w]
+            parts = range(t0, t0 + width, WIDEST)
+            waiting[(w, n0)] = [
+                (g, tier, n, t) for t in parts for g, tier in products for n in range(n0, n0 + tiles)
+            ]
         acc = {}
         closed = []
         emptied = set()
         results = {}
 
-        def multiply(bank, g, tier, n):
+        def multiply(bank, g, tier, n, t):
             w, n0 = bank
             t0, width, tiles, count = WINDOWS[w]
+            cols = slice(t, t + min(width, WIDEST))
+            first = (n - n0) * width - t0
             codes, plane, fmt = tiers[tier]
             opening = bank not in acc
             if opening:
@@ -227,13 +265,13 @@ def tile_mix_tierx_mix_gelu_kernel(tc, x, w8_words, w8_scales, w4_words, w4_scal
                 weights = w8[:, 4 * P * n : 4 * P * (n + 1)].bitcast(E4M3)
             else:
                 weights = w4[:, 2 * P * n : 2 * P * (n + 1)].bitcast(E2M1)
-            waiting[bank].remove((g, tier, n))
+            waiting[bank].remove((g, tier, n, t))
             nc.tensor.matmul_mx(
-                out=acc[bank][:, (n - n0) * width : (n - n0 + 1) * width],
+                out=acc[bank][:, first + cols.start : first + cols.stop],
                 lhsT=weights,
                 lhsT_scale=w_planes[:, g * N + P * n : g * N + P * (n + 1)],
-                rhs=codes[g][:, t0 : t0 + width].bitcast(fmt),
-                rhs_scale=plane[g][:, t0 : t0 + width],
+                rhs=codes[g][:, cols].bitcast(fmt),
+                rhs_scale=plane[g][:, cols],
                 start=opening,
                 stop=not waiting[bank],
             )
@@ -244,11 +282,11 @@ def tile_mix_tierx_mix_gelu_kernel(tc, x, w8_words, w8_scales, w4_words, w4_scal
             for number, bank in enumerate(banks):
                 if number + 1 >= SUM_BANKS + 1 and banks[number - SUM_BANKS] not in emptied:
                     break
-                t0, width, tiles, count = WINDOWS[bank[0]]
-                for g, tier, n in list(waiting[bank]):
+                width = min(WINDOWS[bank[0]][1], WIDEST)
+                for g, tier, n, t in list(waiting[bank]):
                     landed = i >= (W4_STEP if g == W4 else W8_STEP)
-                    if landed and coded[(g, tier)] >= t0 + width and columns >= width:
-                        multiply(bank, g, tier, n)
+                    if landed and coded[(g, tier)] >= t + width and columns >= width:
+                        multiply(bank, g, tier, n, t)
                         columns -= width
 
         def finish(columns):
@@ -300,12 +338,14 @@ def tile_mix_tierx_mix_gelu_kernel(tc, x, w8_words, w8_scales, w4_words, w4_scal
         for i in range(N_CHUNKS):
             for lo, hi in halves if i == last else [(0, CHUNK)]:
                 subtract(i, lo, hi)
-            if i < FIRST_GELU:
-                cast(i + AHEAD + 1, nc.scalar.copy)
+            if i + AHEAD + 1 == BEHIND_W4:
+                cast(BEHIND_W4, nc.scalar.copy, LATE_SHARE, CHUNK)
+            elif i < FIRST_GELU:
+                cast_scalar(i + AHEAD + 1)
             else:
                 if i == FIRST_GELU:
                     for chunk in range(i + AHEAD + 1, N_CHUNKS):
-                        cast(chunk, nc.scalar.copy)
+                        cast_scalar(chunk)
                 finish(T * N_TILES)
             if i == 1:
                 quantise(REST, 0)
@@ -314,8 +354,12 @@ def tile_mix_tierx_mix_gelu_kernel(tc, x, w8_words, w8_scales, w4_words, w4_scal
             if i % 2 == 1 and i < last:
                 for chunk in range(max(i - 1, 1), i + 1):
                     quantise(REST, chunk)
+                    if chunk + POOL_BEHIND in POOL_CHUNKS:
+                        cast_pool(chunk + POOL_BEHIND)
+            if i + AHEAD + 1 == BEHIND_W4:
+                cast(BEHIND_W4, nc.vector.tensor_copy, 0, LATE_SHARE)
             if i < last:
-                moved = {last - AHEAD - 1: -BANK, last - AHEAD: BANK}.get(i, 0)
+                moved = {last - AHEAD - 1: -WIDEST, last - AHEAD: WIDEST}.get(i, 0)
                 take_passes(i, PASS_COLUMNS + moved)
         finish(T * N_TILES)
         quantise(REST, last - 1)

@@ -30,8 +30,7 @@ WALK = 2
 AHEAD = 2
 VALUE_BANKS = 2
 SUM_BANKS = 6
-VECTOR_SHARE = 80
-SHARE_STEP = 16
+VECTOR_SHARES = [88, 88, 48]
 EYE_ORDER = [3, 1, 0, 2]
 W4_STEP = 0
 W8_STEP = 6
@@ -48,6 +47,7 @@ POOL_SHARE = 64
 POOL_BEHIND = 5
 BEHIND_W4 = 4
 LATE_SHARE = 48
+REST_FIRST = [1, 3]
 PASS_COLUMNS = 1024
 FIRST_GELU = 9
 
@@ -323,7 +323,7 @@ def tile_mix_tierx_mix_gelu_kernel(tc, x, w8_words, w8_scales, w4_words, w4_scal
             )
 
         def cast_shared(i):
-            share = VECTOR_SHARE - SHARE_STEP * i
+            share = VECTOR_SHARES[i]
             cast(i, nc.vector.tensor_copy, 0, share)
             cast(i, nc.scalar.copy, share, CHUNK)
 
@@ -347,12 +347,12 @@ def tile_mix_tierx_mix_gelu_kernel(tc, x, w8_words, w8_scales, w4_words, w4_scal
                     for chunk in range(i + AHEAD + 1, N_CHUNKS):
                         cast_scalar(chunk)
                 finish(T * N_TILES)
-            if i == 1:
-                quantise(REST, 0)
+            if i in REST_FIRST:
+                quantise(REST, i - 1)
             if i + AHEAD <= last:
                 first_tier(i + AHEAD)
             if i % 2 == 1 and i < last:
-                for chunk in range(max(i - 1, 1), i + 1):
+                for chunk in range(i if i in REST_FIRST else i - 1, i + 1):
                     quantise(REST, chunk)
                     if chunk + POOL_BEHIND in POOL_CHUNKS:
                         cast_pool(chunk + POOL_BEHIND)

@@ -30,8 +30,8 @@ WALK = 2
 AHEAD = 2
 VALUE_BANKS = 2
 SUM_BANKS = 6
-VECTOR_SHARES = [88, 88, 48]
-EYE_ORDER = [3, 1, 0, 2]
+VECTOR_SHARES = [128, 64, 48]
+BF16_ONE = 0x3F80
 W4_STEP = 0
 W8_STEP = 6
 BIAS_PITCH = 8
@@ -62,8 +62,9 @@ def tile_mix_tierx_mix_gelu_kernel(tc, x, w8_words, w8_scales, w4_words, w4_scal
         def sb(name, shape, dtype):
             return keep.tile(shape, dtype, name=name, align_bytes=ALIGN)
 
-        diag = sb("diag", [P, K_PASS + PACK], BF16)
-        shifted = sb("shifted", [P, (PACK - 1) * K_PASS], BF16)
+        eye_words = K_PASS // 2
+        ramp = sb("ramp", [P, eye_words], I32)
+        eye_in = sb("eye_in", [P, PACK * eye_words], I32)
         eye_codes = sb("eye_codes", [P, K_PASS], U32)
         eye_plane = sb("eye_plane", [P, K_PASS], U8)
         w_planes = sb("w_planes", [P, 2 * N], U8)
@@ -72,7 +73,7 @@ def tile_mix_tierx_mix_gelu_kernel(tc, x, w8_words, w8_scales, w4_words, w4_scal
         q_plane = [sb("q_plane%d" % g, [P, PLANE_AT + T], U8)[:, PLANE_AT:] for g in (W8, W4)]
         r_codes = [sb("r_codes%d" % g, [P, CODES_AT + T], U32)[:, CODES_AT:] for g in (W8, W4)]
         r_plane = [sb("r_plane%d" % g, [P, PLANE_AT + T], U8)[:, PLANE_AT:] for g in (W8, W4)]
-        diag_words = diag[:].bitcast(F32)
+        nc.gpsimd.iota(ramp[:], pattern=[[1, eye_words]], base=0, channel_multiplier=-2)
         zeros = q_codes[W8][:, 0 : WARM + WARM // PACK]
         warm_codes = zeros[:, 0:WARM]
         warm_plane = zeros[:, WARM:].bitcast(U8)
@@ -81,31 +82,28 @@ def tile_mix_tierx_mix_gelu_kernel(tc, x, w8_words, w8_scales, w4_words, w4_scal
         table_warm = sb("table_warm", [P, 1], F32)
         zero = zeros[:, 0:1].bitcast(F32)
         nc.scalar.activation(out=table_warm[:], in_=zero, func=GELU, bias=zero, scale=1.0)
-        diag_width = (K_PASS + PACK) // 2
-        nc.gpsimd.affine_select(
-            out=diag_words,
-            in_=zeros[:, 0:diag_width].bitcast(F32),
-            compare_op=mybir.AluOpType.not_equal,
-            fill=1.0,
-            base=1,
-            pattern=[[-1, diag_width]],
-            channel_multiplier=2,
-        )
-
-        def eye_cols(quarter, count=1):
-            return slice(quarter * P, (quarter + count) * P)
-
-        def quantise_eye(quarter, count, rows):
-            cols = eye_cols(quarter, count)
-            nc.vector.quantize_mx(out=eye_codes[:, cols].bitcast(E4M3), scales=eye_plane[:, cols], in_=rows)
-
-        quantise_eye(0, 1, diag[:, 0:K_PASS])
-        for quarter in range(1, PACK):
-            shift = PACK - 1 - EYE_ORDER[quarter]
-            nc.vector.tensor_copy(
-                out=shifted[:, (quarter - 1) * K_PASS : quarter * K_PASS], in_=diag[:, shift : shift + K_PASS]
+        for j in range(PACK):
+            nc.vector.tensor_scalar(
+                out=eye_in[:, j * eye_words : (j + 1) * eye_words],
+                in0=ramp[:],
+                scalar1=float(j // 2),
+                scalar2=float(BF16_ONE << (16 * (j % 2))),
+                op0=mybir.AluOpType.is_equal,
+                op1=mybir.AluOpType.mult,
             )
-        quantise_eye(1, 1, shifted[:, 0:K_PASS])
+
+        def eye_cols(j, count=1):
+            return slice(j * P, (j + count) * P)
+
+        def quantise_eye(j, count):
+            cols = eye_cols(j, count)
+            nc.vector.quantize_mx(
+                out=eye_codes[:, cols].bitcast(E4M3),
+                scales=eye_plane[:, cols],
+                in_=eye_in[:, j * eye_words : (j + count) * eye_words].bitcast(BF16),
+            )
+
+        quantise_eye(0, 2)
 
         chunks = [(g, t0) for g, w in ORDER for t0 in range(WINDOWS[w][0], WINDOWS[w][0] + WINDOWS[w][1], CHUNK)]
         raw = {}
@@ -219,11 +217,11 @@ def tile_mix_tierx_mix_gelu_kernel(tc, x, w8_words, w8_scales, w4_words, w4_scal
             g, t0 = chunks[i]
             cols = slice(t0, t0 + CHUNK)
             values[i] = psum.tile([P, PACK, CHUNK], F32, tag="values", bufs=VALUE_BANKS, name="values")
-            for quarter, j in enumerate(EYE_ORDER):
+            for j in range(PACK):
                 nc.tensor.matmul_mx(
                     out=values[i][:, j, :],
-                    lhsT=eye_codes[:, eye_cols(quarter)].bitcast(E4M3),
-                    lhsT_scale=eye_plane[:, eye_cols(quarter)],
+                    lhsT=eye_codes[:, eye_cols(j)].bitcast(E4M3),
+                    lhsT_scale=eye_plane[:, eye_cols(j)],
                     rhs=q_codes[g][:, cols].bitcast(E4M3),
                     rhs_scale=q_plane[g][:, cols],
                     start=True,
@@ -325,10 +323,11 @@ def tile_mix_tierx_mix_gelu_kernel(tc, x, w8_words, w8_scales, w4_words, w4_scal
         def cast_shared(i):
             share = VECTOR_SHARES[i]
             cast(i, nc.vector.tensor_copy, 0, share)
-            cast(i, nc.scalar.copy, share, CHUNK)
+            if share < CHUNK:
+                cast(i, nc.scalar.copy, share, CHUNK)
 
         cast_shared(0)
-        quantise_eye(2, 2, shifted[:, K_PASS:])
+        quantise_eye(2, 2)
         first_tier(0)
         cast_shared(1)
         first_tier(1)

@@ -38,7 +38,7 @@ BIAS_PITCH = 8
 CODES_AT = 16
 PLANE_AT = 192
 WARM = 256
-WARM_UPS = 9
+WARM_UPS = 7
 WINDOWS = [(0, 512, 1, 1), (512, 256, 2, 2), (768, 128, 4, 2), (896, 128, 1, 2)]
 ORDER = [(W4, 0), (W4, 1), (W8, 0), (W8, 1), (W4, 2), (W8, 2), (W4, 3), (W8, 3)]
 WIDEST = 256

from contextlib import ExitStack

import concourse.mybir as mybir

K, N, T = 1024, 512, 1024
FLOPS = 2 * 2 * K * N * T

F32 = mybir.dt.float32
BF16 = mybir.dt.bfloat16
I32 = mybir.dt.int32
U32 = mybir.dt.uint32
U8 = mybir.dt.uint8
E4M3 = mybir.dt.float8_e4m3fn_x4
E5M2 = mybir.dt.float8_e5m2_x4
E2M1 = mybir.dt.float4_e2m1fn_x4
GELU = mybir.ActivationFunctionType.Gelu_apprx_tanh

P = 128
QUAD = 32
PACK = 4
K_PASS = P * PACK
BANK = 512
CHUNK = 128
N_CHUNKS = (K // K_PASS) * (T // CHUNK)
N_TILES = N // P
W8, W4 = 0, 1
FIRST, REST = 0, 1
ALIGN = 1024
WALK = 2
AHEAD = 2
VALUE_BANKS = 2
SUM_BANKS = 6
VECTOR_SHARES = [128, 64, 48]
BF16_ONE = 0x3F80
W4_STEP = 0
W8_STEP = 6
BIAS_PITCH = 8
CODES_AT = 16
PLANE_AT = 192
WARM = 256
WARM_UPS = 7
WINDOWS = [(0, 512, 1, 1), (512, 256, 2, 2), (768, 128, 4, 2), (896, 128, 1, 2)]
ORDER = [(W4, 0), (W4, 1), (W8, 0), (W8, 1), (W4, 2), (W8, 2), (W4, 3), (W8, 3)]
WIDEST = 256
POOL_CHUNKS = [13, 15]
POOL_SHARE = 64
POOL_BEHIND = 5
BEHIND_W4 = 4
LATE_SHARE = 48
REST_FIRST = [1, 3]
PASS_COLUMNS = 1024
FIRST_GELU = 9


def tile_mix_tierx_mix_gelu_kernel(tc, x, w8_words, w8_scales, w4_words, w4_scales, b, out):
    nc = tc.nc
    with ExitStack() as ctx:
        keep = ctx.enter_context(tc.tile_pool(name="keep", bufs=1))
        psum = ctx.enter_context(tc.psum_pool(name="psum", bufs=1))
        ctx.enter_context(tc.manual_schedule())

        def sb(name, shape, dtype):
            return keep.tile(shape, dtype, name=name, align_bytes=ALIGN)

        eye_words = K_PASS // 2
        ramp = sb("ramp", [P, eye_words], I32)
        eye_in = sb("eye_in", [P, PACK * eye_words], I32)
        eye_codes = sb("eye_codes", [P, K_PASS], U32)
        eye_plane = sb("eye_plane", [P, K_PASS], U8)
        w_planes = sb("w_planes", [P, 2 * N], U8)
        bias = sb("bias", [P, N_TILES, BIAS_PITCH], F32)
        q_codes = [sb("q_codes%d" % g, [P, CODES_AT + T], U32)[:, CODES_AT:] for g in (W8, W4)]
        q_plane = [sb("q_plane%d" % g, [P, PLANE_AT + T], U8)[:, PLANE_AT:] for g in (W8, W4)]
        r_codes = [sb("r_codes%d" % g, [P, CODES_AT + T], U32)[:, CODES_AT:] for g in (W8, W4)]
        r_plane = [sb("r_plane%d" % g, [P, PLANE_AT + T], U8)[:, PLANE_AT:] for g in (W8, W4)]
        nc.gpsimd.iota(ramp[:], pattern=[[1, eye_words]], base=0, channel_multiplier=-2)
        zeros = q_codes[W8][:, 0 : WARM + WARM // PACK]
        warm_codes = zeros[:, 0:WARM]
        warm_plane = zeros[:, WARM:].bitcast(U8)
        nc.vector.memset(zeros.bitcast(I32), 0)
        nc.vector.memset(w_planes[:].bitcast(I32), 0)
        table_warm = sb("table_warm", [P, 1], F32)
        zero = zeros[:, 0:1].bitcast(F32)
        nc.scalar.activation(out=table_warm[:], in_=zero, func=GELU, bias=zero, scale=1.0)
        for j in range(PACK):
            nc.vector.tensor_scalar(
                out=eye_in[:, j * eye_words : (j + 1) * eye_words],
                in0=ramp[:],
                scalar1=float(j // 2),
                scalar2=float(BF16_ONE << (16 * (j % 2))),
                op0=mybir.AluOpType.is_equal,
                op1=mybir.AluOpType.mult,
            )

        def eye_cols(j, count=1):
            return slice(j * P, (j + count) * P)

        def quantise_eye(j, count):
            cols = eye_cols(j, count)
            nc.vector.quantize_mx(
                out=eye_codes[:, cols].bitcast(E4M3),
                scales=eye_plane[:, cols],
                in_=eye_in[:, j * eye_words : (j + count) * eye_words].bitcast(BF16),
            )

        quantise_eye(0, 2)

        chunks = [(g, t0) for g, w in ORDER for t0 in range(WINDOWS[w][0], WINDOWS[w][0] + WINDOWS[w][1], CHUNK)]
        raw = {}
        w8 = sb("w8", [P, 4 * N], U8)
        w4 = sb("w4", [P, 2 * N], U8)

        def load_x(first, count=1):
            g, t0 = chunks[first]
            width = count * CHUNK
            slab = sb("x%d" % first, [P, PACK, width], F32)
            nc.sync.dma_start(
                out=slab[:],
                in_=x[g * K_PASS : (g + 1) * K_PASS, t0 : t0 + width].rearrange("(p j) w -> p j w", j=PACK),
            )
            for pos in range(count):
                raw[first + pos] = slab[:, :, pos * CHUNK : (pos + 1) * CHUNK]

        def load_bias():
            with nc.allow_non_contiguous_dma(reason="one bias value a partition and output tile"):
                nc.sync.dma_start(out=bias[:, :, 0], in_=b.rearrange("(n p) -> p n", p=P))

        def load_plane(g, scales, rows):
            for r in rows:
                nc.sync.dma_start(
                    out=w_planes[r:P:QUAD, g * N : (g + 1) * N].bitcast(I32), in_=scales[0, r:16:4, :].bitcast(I32)
                )

        def load_w4():
            nc.sync.dma_start(out=w4[:].bitcast(I32), in_=w4_words[0].bitcast(I32))

        def load_w8():
            nc.sync.dma_start(out=w8[:].bitcast(I32), in_=w8_words[0].rearrange("p n i -> p (n i)").bitcast(I32))

        load_x(0)
        load_x(1)
        load_x(2)
        load_plane(W4, w4_scales, [0, 1])
        load_x(3)
        load_plane(W4, w4_scales, [2, 3])
        load_w4()
        load_x(4)
        load_x(5)
        load_x(6)
        load_x(7)
        load_plane(W8, w8_scales, [0, 1])
        load_x(8, 2)
        load_plane(W8, w8_scales, [2, 3])
        load_w8()
        for i in range(10, N_CHUNKS):
            load_x(i)
        load_bias()

        tiers = {FIRST: (q_codes, q_plane, E4M3), REST: (r_codes, r_plane, E5M2)}
        stage = sb("stage", [P, 2 * N_CHUNKS * K_PASS], BF16)
        stage_at = {}
        free_at = 0
        for i in range(N_CHUNKS):
            stage_at[(FIRST, i)] = free_at
            free_at += K_PASS
            if i in POOL_CHUNKS:
                free_at -= PACK * POOL_SHARE
                stage_at[(REST, i - POOL_BEHIND)] = free_at
                free_at += K_PASS
        for i in range(N_CHUNKS):
            if (REST, i) not in stage_at:
                stage_at[(REST, i)] = free_at
                free_at += K_PASS

        def rows_walk(ap):
            return ap.rearrange("p j (c i) -> p c j i", i=WALK)

        def words_walk(ap):
            return ap.rearrange("p (c i j) -> p c j i", i=WALK, j=PACK)

        def staged(tier, i, lo, hi):
            return stage[:, stage_at[(tier, i)] + lo * PACK : stage_at[(tier, i)] + hi * PACK]

        values = {}
        coded = {(g, tier): 0 for g in (W8, W4) for tier in (FIRST, REST)}

        def cast(i, copy, lo=0, hi=CHUNK):
            copy(out=words_walk(staged(FIRST, i, lo, hi)), in_=rows_walk(raw[i][:, :, lo:hi]))

        def cast_scalar(i):
            cast(i, nc.scalar.copy, 0, CHUNK - POOL_SHARE if i in POOL_CHUNKS else CHUNK)

        def cast_pool(i):
            lo = CHUNK - POOL_SHARE
            nc.gpsimd.tensor_scalar(
                out=words_walk(staged(FIRST, i, lo, CHUNK)),
                in0=rows_walk(raw[i][:, :, lo:]),
                scalar1=1.0,
                scalar2=0.0,
                op0=mybir.AluOpType.mult,
                op1=mybir.AluOpType.add,
            )

        def quantise(tier, i, lo=0, hi=CHUNK):
            codes, plane, fmt = tiers[tier]
            g, t0 = chunks[i]
            cols = slice(t0 + lo, t0 + hi)
            nc.vector.quantize_mx(
                out=codes[g][:, cols].bitcast(fmt),
                scales=plane[g][:, cols],
                in_=staged(tier, i, lo, hi),
            )
            coded[(g, tier)] = t0 + hi

        def first_tier(i):
            quantise(FIRST, i)
            g, t0 = chunks[i]
            cols = slice(t0, t0 + CHUNK)
            values[i] = psum.tile([P, PACK, CHUNK], F32, tag="values", bufs=VALUE_BANKS, name="values")
            for j in range(PACK):
                nc.tensor.matmul_mx(
                    out=values[i][:, j, :],
                    lhsT=eye_codes[:, eye_cols(j)].bitcast(E4M3),
                    lhsT_scale=eye_plane[:, eye_cols(j)],
                    rhs=q_codes[g][:, cols].bitcast(E4M3),
                    rhs_scale=q_plane[g][:, cols],
                    start=True,
                    stop=True,
                )

        def subtract(i, lo=0, hi=CHUNK):
            nc.vector.tensor_tensor(
                out=words_walk(staged(REST, i, lo, hi)),
                in0=rows_walk(raw[i][:, :, lo:hi]),
                in1=rows_walk(values[i][:, :, lo:hi]),
                op=mybir.AluOpType.subtract,
            )

        banks = [(w, n0) for w, (t0, width, tiles, count) in enumerate(WINDOWS) for n0 in range(0, N_TILES, tiles)]
        products = [(W4, FIRST), (W4, REST), (W8, FIRST), (W8, REST)]
        waiting = {}
        for w, n0 in banks:
            t0, width, tiles, count = WINDOWS[w]
            parts = range(t0, t0 + width, WIDEST)
            waiting[(w, n0)] = [
                (g, tier, n, t) for t in parts for g, tier in products for n in range(n0, n0 + tiles)
            ]
        acc = {}
        closed = []
        emptied = set()
        results = {}

        def multiply(bank, g, tier, n, t):
            w, n0 = bank
            t0, width, tiles, count = WINDOWS[w]
            cols = slice(t, t + min(width, WIDEST))
            first = (n - n0) * width - t0
            codes, plane, fmt = tiers[tier]
            opening = bank not in acc
            if opening:
                acc[bank] = psum.tile([P, BANK], F32, tag="acc", bufs=SUM_BANKS, name="acc")
            if g == W8:
                weights = w8[:, 4 * P * n : 4 * P * (n + 1)].bitcast(E4M3)
            else:
                weights = w4[:, 2 * P * n : 2 * P * (n + 1)].bitcast(E2M1)
            waiting[bank].remove((g, tier, n, t))
            nc.tensor.matmul_mx(
                out=acc[bank][:, first + cols.start : first + cols.stop],
                lhsT=weights,
                lhsT_scale=w_planes[:, g * N + P * n : g * N + P * (n + 1)],
                rhs=codes[g][:, cols].bitcast(fmt),
                rhs_scale=plane[g][:, cols],
                start=opening,
                stop=not waiting[bank],
            )
            if not waiting[bank]:
                closed.extend((bank, tile) for tile in range(n0, n0 + tiles))

        def take_passes(i, columns):
            for number, bank in enumerate(banks):
                if number + 1 >= SUM_BANKS + 1 and banks[number - SUM_BANKS] not in emptied:
                    break
                width = min(WINDOWS[bank[0]][1], WIDEST)
                for g, tier, n, t in list(waiting[bank]):
                    landed = i >= (W4_STEP if g == W4 else W8_STEP)
                    if landed and coded[(g, tier)] >= t + width and columns >= width:
                        multiply(bank, g, tier, n, t)
                        columns -= width

        def finish(columns):
            while closed and columns >= WINDOWS[closed[0][0][0]][1]:
                bank, n = closed.pop(0)
                w, n0 = bank
                t0, width, tiles, count = WINDOWS[w]
                if n % count == 0:
                    results[w] = sb("result%d_%d" % (w, n), [P, count, width], F32)
                nc.scalar.activation(
                    out=results[w][:, n % count, :],
                    in_=acc[bank][:, (n - n0) * width : (n - n0 + 1) * width],
                    func=GELU,
                    bias=bias[:, n, 0:1],
                    scale=1.0,
                )
                if (n + 1) % count == 0:
                    rows = out[(n + 1 - count) * P : (n + 1) * P, t0 : t0 + width]
                    nc.sync.dma_start(out=rows.rearrange("(n p) t -> p n t", p=P), in_=results[w][:])
                columns -= width
                if n == n0 + tiles - 1:
                    emptied.add(bank)

        warm = psum.tile([P, BANK], F32, tag="acc", bufs=SUM_BANKS, name="acc")
        for count in range(WARM_UPS):
            nc.tensor.matmul_mx(
                out=warm[:, 0:WARM],
                lhsT=warm_codes[:, 0:P].bitcast(E4M3),
                lhsT_scale=warm_plane[:, 0:P],
                rhs=warm_codes.bitcast(E4M3),
                rhs_scale=warm_plane,
                start=True,
                stop=True,
            )

        def cast_shared(i):
            share = VECTOR_SHARES[i]
            cast(i, nc.vector.tensor_copy, 0, share)
            if share < CHUNK:
                cast(i, nc.scalar.copy, share, CHUNK)

        cast_shared(0)
        quantise_eye(2, 2)
        first_tier(0)
        cast_shared(1)
        first_tier(1)
        cast_shared(2)
        last = N_CHUNKS - 1
        halves = [(0, CHUNK // 2), (CHUNK // 2, CHUNK)]
        for i in range(N_CHUNKS):
            for lo, hi in halves if i == last else [(0, CHUNK)]:
                subtract(i, lo, hi)
            if i + AHEAD + 1 == BEHIND_W4:
                cast(BEHIND_W4, nc.scalar.copy, LATE_SHARE, CHUNK)
            elif i < FIRST_GELU:
                cast_scalar(i + AHEAD + 1)
            else:
                if i == FIRST_GELU:
                    for chunk in range(i + AHEAD + 1, N_CHUNKS):
                        cast_scalar(chunk)
                finish(T * N_TILES)
            if i in REST_FIRST:
                quantise(REST, i - 1)
            if i + AHEAD <= last:
                first_tier(i + AHEAD)
            if i % 2 == 1 and i < last:
                for chunk in range(i if i in REST_FIRST else i - 1, i + 1):
                    quantise(REST, chunk)
                    if chunk + POOL_BEHIND in POOL_CHUNKS:
                        cast_pool(chunk + POOL_BEHIND)
            if i + AHEAD + 1 == BEHIND_W4:
                cast(BEHIND_W4, nc.vector.tensor_copy, 0, LATE_SHARE)
            if i < last:
                moved = {last - AHEAD - 1: -WIDEST, last - AHEAD: WIDEST}.get(i, 0)
                take_passes(i, PASS_COLUMNS + moved)
        finish(T * N_TILES)
        quantise(REST, last - 1)
        for lo, hi in halves:
            quantise(REST, last, lo, hi)
        take_passes(last, T * N_TILES)
        finish(T * N_TILES)
